import numpy as np, ml_dtypes
CORES = [13,21,141,149]
N = 4
BF = ml_dtypes.bfloat16
W, H0, L, RO, Q = 2048, 768, 256, 2, 4
def base(rng):
    price = rng.integers(0, 101, (N, 8, 1, W)) + rng.integers(0, 28, (N, 8, 16, W))
    packs = rng.integers(0, W, (N, 8, 16, H0)); prev = rng.integers(0, H0, (N, 8, H0)); lots = rng.integers(0, W, (N, 8, 16, L))
    lots[:, :, 0, ::4] = lots[:1, :, 0, ::4]
    o = np.stack([rng.permutation(np.array([5, 20, 35, 50, 60, 70, 80, 90])) for q in range(N)])
    slack = o[:, :, None, None] + rng.integers(0, 9, (N, 8, 16, RO))
    return price, packs, prev, lots, rng.integers(1, 8, (N, 8, 16)), rng.integers(0, 16, (N, 8, 16)), slack
def pack(price, packs, prev, lots, inc, wt, slack):
    c = lambda a, n: np.ascontiguousarray(np.reshape(a, (N, 128, n))).astype(np.int32)
    return {"price": np.ascontiguousarray(price.reshape(N, 128, W)).astype(np.float32).astype(BF), "packs": c(packs, H0), "prev": np.ascontiguousarray(prev).astype(np.int32),
            "lots": c(lots, L), "inc": c(inc, 1), "wt": c(wt, 1), "slack": c(slack, RO)}
def edge(rng, hi, *s):
    return np.where(rng.random(s) < 0.2, rng.integers(0, hi + 1, s), hi * rng.integers(0, 2, s))
def setup_inputs(rng):
    return pack(*base(rng))
def setup_inputs_spread(rng):
    price, packs, prev, lots, inc, wt, slack = base(rng)
    price = np.minimum((np.exp2(7.65 * rng.random((N, 8, 1, W))) * rng.random((N, 8, 16, W))).astype(np.int64), 200)
    packs = np.minimum((W * rng.random((N, 8, 16, H0)) ** 3).astype(np.int64), W - 1)
    lots = W - 1 - np.minimum((W * rng.random((N, 8, 16, L)) ** 2).astype(np.int64), W - 1)
    prev = np.minimum((H0 * rng.random((N, 8, H0)) ** 2).astype(np.int64), H0 - 1)
    slack = np.minimum(np.exp2(8 * rng.random((N, 8, 1, 1)) * rng.random((N, 8, 16, RO))).astype(np.int64) - 1, 255)
    return pack(price, packs, prev, lots, inc, wt, slack)
def setup_inputs_ends(rng):
    hi = np.where(np.arange(8) == 6, 127, 200)[None, :, None, None]
    k = rng.integers(0, 3, (N, 8, 1, W)); price = hi * np.where(k == 2, rng.integers(0, 2, (N, 8, 16, W)), k)
    price[..., 0] = 0; price[..., W - 1] = hi[..., 0]
    price[:, 2:4, :, 0] = 200; price[:, 2:4, :, W - 1] = 0; price[:, 5, 9:, W - 1] = 0
    packs = edge(rng, W - 1, N, 8, 16, H0); prev = edge(rng, H0 - 1, N, 8, H0); lots = edge(rng, W - 1, N, 8, 16, L)
    inc = 1 + 6 * rng.integers(0, 2, (N, 8, 16)); inc[:, 7] = 7; inc[:, 6, 0] = 1
    o = np.argsort(rng.random((N, 8, 16)), axis=2)
    slack = np.repeat((255 * (o >= np.array([16, 9, 16, 9, 12, 16, 8, 8])[None, :, None]))[..., None], RO, axis=3)
    wt = 15 * rng.integers(0, 2, (N, 8, 16)); wt[:, 7] = 0
    full = np.array([15] * 8 + [9] + [0] * 7); wt[:, 6] = full[o[:, 6]]; wt[:, 0] = full[o[:, 0]]
    c = np.array([0, 3, L - 1]); lots[:, 6, 0, c] = W - 1; lots[:, 6, 15, c] = W - 1
    v = np.arange(W)
    back = lambda t, to: int(np.argmax(((v + (v >> 5) + 77 * (t + 1)) & (W - 1)) == to))
    lots[:, 7, 0, c] = W - 1; lots[:, 7, 1, c] = back(0, W - 1); lots[:, 7, 2, c] = back(0, back(1, W - 1))
    return pack(price, packs, prev, lots, inc, wt, slack)
def setup_inputs_corners(rng):
    price, packs, prev, lots, inc, wt, slack = base(rng); a = np.arange(H0)
    kinds = [a, np.maximum(a - 1, 0), 0 * a, 0 * a + H0 - 1, (a + 1) % H0, a ^ 1, H0 - L + a % L]
    for q in range(N):
        for g, k in enumerate(rng.permutation(8)):
            if k < 7: prev[q, g] = kinds[int(k)]
            wt[q, g] = (0, 15, 1, 7)[int(rng.integers(0, 4))] if k < 4 else wt[q, g]
            inc[q, g] = 1 if k % 3 == 0 else 7 if k % 3 == 1 else inc[q, g]
    s = [int(g) for g in rng.permutation(8)]
    for g in s[:4]: slack[:, g] = 255
    lots[:, s[0], :RO] = W - 1; wt[:, s[0]] = 0; price[:, s[0], :, W - 1] = 127; inc[:, s[0]] = 7
    lots[:, s[1], 0] = 0; price[:, s[1], :, 0] = 127 * rng.integers(0, 2, (N, 16))
    m = rng.permutation(W); lots[:, s[2], 0] = m[(np.arange(N * L) % (W - 1) + 1).reshape(N, L)]; lots[int(rng.integers(0, N)), s[2], 0, L - 1] = m[0]
    for q in range(N): lots[q, s[3], 0] = rng.permutation(W)[:L]
    packs[:, s[4], :, H0 - L:] = lots[:, s[4]]
    slack[:, s[4]] = 0; slack[:, s[5]] = 0; h = W // 2
    price[:, s[5], :, :h] = rng.integers(0, 3, (N, 16, h)); price[:, s[5], :, h:] = 127; lots[:, s[5]] = rng.integers(h, W, (N, 16, L)); packs[:, s[5]] = rng.integers(0, h, (N, 16, H0))
    nxt = lambda z, u, t: (((z * (2 * u + 1)) >> 5) + z + 77 * (t + 1)) & (W - 1)
    g = s[6]; b = int(rng.integers(0, N)); k = L // 2
    wt[:, g] = 0; inc[:, g] = 7; inc[b, g] = 1 + rng.permutation(16) % 5
    slack[:, g] = 255; slack[:, g, :, RO - 1] = 254 - rng.integers(0, 55, (N, 16)) * (np.arange(N) % 2)[:, None]
    e = rng.integers(0, W, L); own = nxt(e, 0, 0); own[k:] = nxt(own[k:], 0, 1)
    lots[:, g, 0] = own; lots[:, g, 1, :k] = e[:k]; lots[:, g, 2, k:] = e[k:]
    dear = np.zeros(W, bool); dear[own] = True; low = rng.random(W) < 0.5
    v = 200 - (rng.random((N, 16, W)) * np.where(low, 32, 8)).astype(np.int64)
    v[b] = np.where(low, rng.integers(0, 4, (16, W)), v[b])
    price[:, g] = np.where(dear, v, rng.integers(0, 3, W))
    g = s[7]; wt[:, g] = 15; inc[:, g] = 7; slack[:, g] = 255; price[:, g] = 200
    e = rng.integers(0, W, L); lots[:, g, 1] = e; lots[:, g, 0] = nxt(e, (16 * 15 * 200) & 1023, 0)
    return pack(price, packs, prev, lots, inc, wt, slack)
def setup_inputs_ties(rng):
    price, packs, prev, lots, inc, wt, slack = base(rng)
    s0 = rng.integers(0, 21, (N, 8, 16)); b = rng.integers(0, 106, (N, 8, 16)); slack = np.repeat(s0[..., None], RO, axis=3)
    n = rng.choice(np.array([0, 7, 8, 9, 10, 16]), (N, 8, 1, W)); low = rng.random((N, 8, 1, W)) < 0.5
    o = np.argsort(rng.random((N, 8, W, 16)), axis=3).transpose(0, 1, 3, 2)
    price = b[..., None] + np.where(low, 0, s0[..., None] + (o < n))
    return pack(price, packs, prev, lots, inc, wt, slack)
def check_inputs(d):
    bad = []
    for k, lo, hi in (("price", 0, 200), ("packs", 0, W - 1), ("prev", 0, H0 - 1), ("lots", 0, W - 1), ("inc", 1, 7), ("wt", 0, 15), ("slack", 0, 255)):
        v = np.asarray(d[k]).astype(np.float64)
        if not (np.min(v) >= lo and np.max(v) <= hi): bad.append("range of " + k)
        elif np.any(v != np.floor(v)): bad.append("whole numbers in " + k)
    return bad
def pick(p, t):
    return np.take_along_axis(p, t.reshape(N, 8, 1, 16 * L), 3).reshape(N, 8, 16, 16, L)
def reference(price, packs, prev, lots, inc, wt, slack):
    p = price.astype(np.float32).astype(np.int64).reshape(N, 8, 16, W)
    h = np.zeros((N, 8, 16, H0 + RO * L), np.int64); h[..., :H0] = packs.reshape(N, 8, 16, H0)
    v = np.zeros((N, 8, H0 + RO * L), np.int64); v[..., :H0] = prev
    t = lots.astype(np.int64).reshape(N, 8, 16, L)
    up = inc.astype(np.int64).reshape(N, 8, 16, 1); wr = wt.astype(np.int64).reshape(N, 8, 16, 1); sl = slack.astype(np.int64).reshape(N, 8, 16, RO)
    a = np.zeros((N, 8, L), np.int64) + (H0 - L + np.arange(L))
    for rnd in range(RO):
        x = pick(p, t); bind = np.zeros((N, 8, L), np.int64) - 1
        for e in range(Q):
            anc = np.take_along_axis(h, a[:, :, None, :], 3); y = pick(p, anc)
            rows = np.add.reduce((x - y > sl[:, :, :, rnd][:, :, :, None, None]).astype(np.int64), axis=2)
            rev = rows >= 9
            t = np.where(rev, anc, t); x = np.where(rev[:, :, None], y, x)
            bind = np.where(np.any(rev, axis=2), a, bind); last = a
            a = np.take_along_axis(v, a, 2)
        lo = H0 + L * rnd
        h[..., lo:lo + L] = t; v[..., lo:lo + L] = np.where(bind >= 0, bind, last)
        flag = np.zeros((N, 8, W), np.int64); np.put_along_axis(flag, t[:, :, rnd], 1, 2)
        offer = p * flag[:, :, None]; s = np.add.reduce(offer, axis=0)[None] - offer
        if rnd + 1 < RO:
            u = np.add.reduce(wr * np.max(x, axis=3), axis=2) & 1023
            t = (((t * (2 * u + 1)[:, :, None]) >> 5) + t + 77 * (rnd + 1)) & (W - 1)
            a = np.zeros((N, 8, L), np.int64) + (lo + np.arange(L))
        p = np.minimum(p + ((up * s) >> 6), 255)
    return {"yp": p.reshape(N, 128, W).astype(np.float32).astype(BF), "yh": np.ascontiguousarray(h[..., H0:]).reshape(N, 128, RO * L).astype(np.float32), "yv": np.ascontiguousarray(v[..., H0:]).astype(np.float32)}

@@ -1,0 +1,590 @@
+from concourse.bass import DstId, RemoteDMATransfer
+from concourse.mybir import AluOpType, ActivationFunctionType
+
+OFFS, BIG = 131072, 16384
+W, L, H0 = 2048, 256, 768
+NCH, CW = 4, 64
+NB = 2
+BW = W // NB
+BF, F32, I32, U16, F16 = "bfloat16", "float32", "int32", "uint16", "float16"
+CYC = 0.83e-3 * 1.2
+LAT, HOT, XT, XT1, FP = 0.1, 500.0, 14.0, 14.0, 0.6
+DH, DM = 0.1, 0.05
+SMH, JIT, MIX = 2.0, 0.3, 933
+CO = ((0, 0, 0, 0), (0, -1.6, 0, 0))
+SPLIT = 2
+
+SCRATCH = {
+    "P0": ("sbuf", [128, W], BF), "P1": ("sbuf", [128, W], BF), "P2": ("sbuf", [128, W], BF),
+    "ps0": ("sbuf", [128, W], BF), "ps1": ("sbuf", [128, W], BF),
+    "pk": ("sbuf", [128, H0], I32), "pv": ("sbuf", [128, H0], I32), "lt": ("sbuf", [128, L], I32),
+    "lc": ("sbuf", [128, 16], I32), "ac": ("sbuf", [128, 16], I32),
+    "ic": ("sbuf", [128, 1], I32), "wc": ("sbuf", [128, 1], I32), "sc": ("sbuf", [128, 2], I32),
+    "icf": ("sbuf", [128, 1], F32), "wcf": ("sbuf", [128, 1], F32), "scf": ("sbuf", [128, 2], F32), "mo": ("sbuf", [128, 1], F32),
+    "ip": ("sbuf", [128, 1], I32), "im": ("sbuf", [128, 128], I32), "on": ("sbuf", [128, W], BF),
+    "pg": ("sbuf", [128, 1], I32), "pgf": ("sbuf", [128, 1], F32), "pg16": ("sbuf", [128, 1], F32), "ipf": ("sbuf", [128, 1], F32),
+    "pl": ("sbuf", [128, 1], I32), "plf": ("sbuf", [128, 1], F32), "mg": ("sbuf", [128, 128], I32),
+    "Z": ("sbuf", [128, 144], BF), "Zh": ("sbuf", [128, 144], F16), "BR": ("sbuf", [128, 128], F16),
+    "BDw": ("sbuf", [128, 128], BF), "IB": ("sbuf", [128, 128], BF), "IL": ("sbuf", [128, 128], BF),
+    "ID": ("sbuf", [128, 128], BF), "DG": ("sbuf", [128, 128], BF), "E": ("sbuf", [128, W], BF),
+    "scd": ("sbuf", [128, 1024], BF), "LT": ("sbuf", [128, 16], F32),
+    "pvh": ("sbuf", [128, H0], F16), "vt": ("sbuf", [128, H0], F32), "btab": ("sbuf", [128, 6 * L], F32),
+    "Btab": ("sbuf", [128, 512 + 6 * L], F32), "bh": ("sbuf", [128, 6 * L], F16), "lst": ("sbuf", [128, 6 * 16], U16),
+    "A16": ("sbuf", [128, 8 * L], U16), "AC": ("sbuf", [128, 8 * L], F32), "Bf": ("sbuf", [128, 4 * L], F32),
+    "A16c": ("sbuf", [128, 8 * 16], U16), "ACc": ("sbuf", [128, 8 * 16], F32),
+    "T16": ("sbuf", [128, 2 * L], U16), "TT": ("sbuf", [128, 2 * L], I32), "Lr": ("sbuf", [128, 2 * L], I32),
+    "T16c": ("sbuf", [128, 32], U16), "TTc": ("sbuf", [128, 32], I32), "Lc": ("sbuf", [128, 16], I32),
+    "x": ("sbuf", [128, 4096 + 256], BF), "mk": ("sbuf", [128, 4096 + 256], BF), "sm": ("sbuf", [128, 4096], BF),
+    "yhf": ("sbuf", [128, 2 * L], F32), "Q": ("sbuf", [128, L], I32),
+    "w1": ("sbuf", [128, L], I32), "w2": ("sbuf", [128, L], I32), "w3": ("sbuf", [128, L], I32), "w4": ("sbuf", [128, L], I32),
+    "w5": ("sbuf", [128, L], I32),
+    "hi": ("sbuf", [128, 2 * L], I32), "hb": ("sbuf", [128, 2 * L], BF), "hm": ("sbuf", [128, 512], BF),
+    "Y": ("sbuf", [128, 4 * 144], BF), "e1": ("sbuf", [128, 32], F32), "e2": ("sbuf", [128, 32], F32), "e3": ("sbuf", [128, 32], F32),
+    "el": ("sbuf", [128, 32], U16), "ctab": ("sbuf", [128, 4 * L], F32), "par": ("sbuf", [128, L], F32),
+    "hl": ("sbuf", [128, 64], I32), "hlb": ("sbuf", [128, 64], F32),
+    "OH": ("sbuf", [128, 16 * 128], BF), "OL": ("sbuf", [128, 16 * 128], BF), "C": ("sbuf", [128, 256], BF),
+    "O0": ("sbuf", [128, W], BF), "O1": ("sbuf", [128, W], BF), "N16": ("sbuf", [128, W], F16),
+    "LO0": ("sbuf", [128, 3 * W], BF), "LO1": ("sbuf", [128, 3 * W], BF),
+    "HB": ("sbuf", [128, 2 * W], BF),
+}
+for _i in range(8):
+    SCRATCH["pb%d" % _i] = ("psum", [128, 512], F32)
+ND = 48
+SEMAPHORES = ["qv", "qs", "qt", "qg", "snd", "hs"] + ["d%d" % i for i in range(ND)] + \
+    ["%s%d_%d" % (n, t, b) for n in ("arr", "far", "hin") for t in range(2) for b in range(NB)]
+
+A = AluOpType
+AF = ActivationFunctionType
+
+
+def build():
+    ops = []
+    hot = [0.0]
+
+    def add(q, cost, fn, rd, wr, kind="c", tag=""):
+        ops.append({"q": q, "cost": cost, "fn": fn, "rd": rd, "wr": wr, "kind": kind, "tag": tag, "hot": hot[0]})
+
+    def vc(n, cyc=1.0):
+        return max(64, n * cyc) * CYC + 0.01
+
+    def ga(n):
+        return n * 1.55 * CYC + 0.06
+
+    def S(T, r):
+        return T[r[0]][:, r[1]:r[2]] if len(r) == 3 else T[r[0]][:, r[1]:r[2]:r[3]]
+
+    def n_of(r):
+        return len(range(*r[1:]))
+
+    def copy(out, in_, cyc=1.0, tag=""):
+        add("v", vc(n_of(out), cyc), lambda g, T, X: g.vector.tensor_copy(S(T, out), S(T, in_)), [in_], [out], tag=tag)
+
+    def ts(out, in_, s1, op0, s2=None, op1=None, cyc=1.0, tag=""):
+        rd = [in_] + [s for s in (s1, s2) if isinstance(s, tuple)]
+
+        def fn(g, T, X):
+            a = S(T, s1) if isinstance(s1, tuple) else s1
+            b = S(T, s2) if isinstance(s2, tuple) else s2
+            if op1 is None:
+                return g.vector.tensor_scalar(S(T, out), S(T, in_), a, None, op0)
+            return g.vector.tensor_scalar(S(T, out), S(T, in_), a, b, op0, op1)
+        add("v", vc(n_of(out), cyc), fn, rd, [out], tag=tag)
+
+    def tt(out, a, b, op, tag=""):
+        two = 1.0 if (a[0][:2] == "pb" or b[0][:2] == "pb") else 2.0
+        add("v", vc(n_of(out), two), lambda g, T, X: g.vector.tensor_tensor(S(T, out), S(T, a), S(T, b), op), [a, b], [out], tag=tag)
+
+    def act(out, in_, bias=0.0, tag=""):
+        def fn(g, T, X):
+            if bias:
+                return g.scalar.activation(S(T, out), S(T, in_), AF.Copy, bias=bias)
+            return g.scalar.activation(S(T, out), S(T, in_), AF.Copy)
+        add("s", n_of(out) * CYC + 0.06, fn, [in_], [out], tag=tag)
+
+    def relu(out, in_, bias, scale, tag=""):
+        add("s", n_of(out) * CYC + 0.06, lambda g, T, X: g.scalar.activation(S(T, out), S(T, in_), AF.Relu, bias=S(T, bias), scale=scale),
+            [in_, bias], [out], tag=tag)
+
+    def gath(out, win, off, tag="", comp=False):
+        def fn(g, T, X):
+            i = S(T, win).indirect(S(T, off))
+            if comp:
+                return g.scalar.activation(S(T, out), i, AF.Copy, bias=255.0, scale=-1.0)
+            return g.scalar.activation(S(T, out), i, AF.Copy)
+        add("s", ga(n_of(out)), fn, [win, off], [out], tag=tag)
+
+    def mm(out, pairs, tag="", k=128, first=True, last=True):
+        def fn(g, T, X):
+            r = None
+            for i, (l, h) in enumerate(pairs):
+                a, b = (S(T, l), S(T, h)) if k == 128 else (T[l[0]][0:k, l[1]:l[2]], T[h[0]][0:k, h[1]:h[2]])
+                r = g.tensor.matmul(S(T, out), a, b, first and i == 0, last and i == len(pairs) - 1)
+            return r
+        add("t", sum(max(64, n_of(h)) for l, h in pairs) * CYC + 0.06, fn, [p for lh in pairs for p in lh], [out], tag=tag)
+
+    def dma(out, in_, kb, rd, wr, q="y", tag=""):
+        def fn(g, T, X):
+            return (g.sync if q == "y" else g.scalar).dma_start(out(T), in_(T))
+        add(q, 2.0 + kb / 180.0, fn, rd, wr, kind="d", tag=tag)
+
+    def iota(out, pattern, base, cm, small=False):
+        n = n_of(out)
+
+        def fn(g, T, X):
+            if small:
+                return g.iota(S(T, out), pattern, base, cm, allow_small_or_imprecise_dtypes=True)
+            return g.iota(S(T, out), pattern, base, cm)
+        add("g", 0.15 + 2 * n * CYC, fn, [], [out])
+
+    def select(out, in_, pattern, cmp, cm):
+        add("g", 0.17 + 2 * n_of(out) * CYC, lambda g, T, X: g.affine_select(S(T, out), S(T, in_), pattern, cmp, 0.0, 0, cm), [in_], [out])
+
+    def mset(out, v):
+        add("v", vc(n_of(out), 0.5), lambda g, T, X: g.vector.memset(S(T, out), v), [], [out])
+
+    R = lambda b, n, a=0: (b, a, a + n)
+
+    hot[0] = 2000.0
+    dma(lambda T: T["pv"][0:8, :], lambda T: T.prev[:], 24, [], [R("pv", H0)], q="s")
+    hot[0] = 1990.0
+    dma(lambda T: T["lc"][:], lambda T: T.lots[0::16, :], 8, [], [R("lc", 16)])
+    hot[0] = 1985.0
+    dma(lambda T: T["P0"][:, 0:W], lambda T: T.price[:], 512, [], [R("P0", W)], q="s")
+    hot[0] = 1980.0
+    dma(lambda T: T["sc"][:], lambda T: T.slack[:], 1, [], [R("sc", 2)])
+    dma(lambda T: T["ac"][:], lambda T: T.packs[0::16, H0 - L:H0], 8, [], [R("ac", 16)])
+    dma(lambda T: T["lt"][:], lambda T: T.lots[:], 128, [], [R("lt", L)])
+    hot[0] = 1970.0
+    dma(lambda T: T["pk"][:], lambda T: T.packs[:], 384, [], [R("pk", H0)])
+    hot[0] = 0.0
+    dma(lambda T: T["wc"][:], lambda T: T.wt[:], 1, [], [R("wc", 1)])
+    dma(lambda T: T["ic"][:], lambda T: T.inc[:], 1, [], [R("ic", 1)])
+    iota(R("ip", 1), [[1, 1]], 0, 1)
+    iota(R("im", 128), [[1, 128]], 0, 0)
+    iota(R("btab", L), [[1, L]], H0 - L, 0, True)
+    iota(R("IL", 128), [[1, 128]], 0, 0, True)
+    iota(R("on", W), [[0, W]], 1, 0, True)
+    select(R("ID", 128), R("on", 128), [[-1, 128]], A.is_equal, 1)
+    select(R("scd", 1024), R("on", 1024), [[0, 64], [1, 16]], A.not_equal, 0)
+    select(R("E", W), R("on", W), [[-1, 16], [-16, 8], [0, 16]], A.is_equal, 1)
+    hot[0] = -HOT
+    iota(R("ctab", L), [[1, L]], H0, 0, True)
+    hot[0] = HOT
+    mset(R("Z", 144), 0.0)
+    ts(R("pg", 1), R("ip", 1), 4, A.logical_shift_right)
+    copy(R("ipf", 1), R("ip", 1))
+    copy(R("pgf", 1), R("pg", 1))
+    ts(R("mg", 128), R("im", 128), 4, A.logical_shift_right)
+    ts(("Z", 15, 128, 16), R("im", 8), R("pgf", 1), A.is_equal, float(BIG), A.mult)
+    ts(R("BR", 128), R("mg", 128), R("ipf", 1), A.is_equal)
+    ts(R("Zh", 144), R("Z", 144), 1.0 / BIG, A.mult)
+    hot[0] = 0.0
+    mset(R("mo", 1), -256.0)
+    ts(R("pg16", 1), R("pg", 1), 16.0, A.mult)
+    ts(R("IB", 128), R("im", 128), R("pg16", 1), A.subtract)
+    ts(R("icf", 1), R("ic", 1), 1.0 / 64, A.mult)
+    ts(R("DG", 128), R("im", 128), R("ipf", 1), A.is_equal, R("icf", 1), A.mult)
+    copy(R("wcf", 1), R("wc", 1))
+    ts(R("BDw", 128), R("mg", 128), R("pgf", 1), A.is_equal, R("wcf", 1), A.mult)
+    ts(R("pl", 1), R("ip", 1), 15, A.bitwise_and)
+    copy(R("plf", 1), R("pl", 1))
+    ts(R("LT", 16), R("im", 16), 16.0, A.mult, R("plf", 1), A.add)
+    ts(R("LT", 16), R("LT", 16), -256.0, A.add)
+    mset(R("Y", 576), 0.0)
+    con = [float(2048 * (e + 1) + OFFS) for e in range(4)]
+    hot[0] = 4 * HOT
+    copy(R("T16c", 16), R("lc", 16))
+    hot[0] = 3 * HOT
+    copy(R("A16c", 16), R("ac", 16))
+    ts(R("scf", 2), R("sc", 2), -1.0, A.mult, 255.0, A.add)
+    relu(R("ps0", W), R("P0", W), R("scf", 1), -1.0, tag="ps0")
+    ts(R("ACc", 16), R("ac", 16), con[0], A.add)
+    ts(R("TTc", 16), R("lc", 16), float(OFFS), A.add)
+    hot[0] = HOT
+    for o, n in ((512, 256), (0, 512)):
+        add("v", vc(n), lambda g, T, X, o=o, n=n: g.vector.tensor_copy(T["pvh"][0:8, o:o + n], T["pv"][0:8, o:o + n]), [R("pv", n, o)], [R("pvh", n, o)])
+    mm(R("pb1", 256), [(R("BR", 128), R("pvh", 256, 512))], k=8)
+    mm(R("pb0", 512), [(R("BR", 128), R("pvh", 512))], k=8)
+    copy(R("bh", L, L), R("pb1", 256))
+    act(R("vt", 256, 512), R("pb1", 256))
+    act(R("vt", 512), R("pb0", 512))
+    hot[0] = 2 * HOT
+    copy(R("T16", L), R("lt", L))
+    copy(R("A16", L), R("pk", L, H0 - L))
+    hot[0] = HOT
+    copy(R("Btab", H0), R("pk", H0))
+    hot[0] = 0.0
+    ts(R("TT", L), R("lt", L), float(OFFS), A.add)
+    act(R("AC", L), R("Btab", L, 512), con[0])
+    hot[0] = -HOT
+    act(R("btab", L, L), R("vt", L, 512))
+
+    def lot_forms(i, src, e):
+        copy(R("A16", L, L * i), src, tag="A16")
+        act(R("AC", L, L * i), src, con[e], tag="AC")
+        claim_forms(i, i // 4)
+
+    def claim_forms(i, t):
+        src, a = ("T16", 0) if i == 4 else ("A16", L * i)
+        dma(lambda T: T["A16c"][:, 16 * i:16 * i + 16], lambda T: T[src][t::16, a:a + L], 8, [R(src, L, a)], [R("A16c", 16, 16 * i)])
+        dma(lambda T: T["ACc"][:, 16 * i:16 * i + 16], lambda T: T["AC"][t::16, L * i:L * i + L], 8, [R("AC", L, L * i)], [R("ACc", 16, 16 * i)])
+
+    def chain(e):
+        hot[0] = HOT if e < 4 else 0.0
+        mm(R("pb7", 16), [(R("Zh", 128, 15 - s), ("bh", L * e + s, L * e + L, 16)) for s in range(16)], tag="list")
+        ts(R("lst", 16, 16 * e), R("pb7", 16), 1.0 / 16, A.mult)
+        if e < 5:
+            gath(R("btab", L, L * (e + 1)), R("vt", H0), R("lst", 16, 16 * e))
+            copy(R("bh", L, L * (e + 1)), R("btab", L, L * (e + 1)))
+        gath(R("Btab", L, 512 + L * e), R("Btab", H0), R("lst", 16, 16 * e))
+        if e < 4:
+            lot_forms(e, R("Btab", L, 512 + L * e), e)
+        hot[0] = 0.0
+
+    for e in range(1, 4):
+        chain(e)
+
+    def trial(t, e, c):
+        i = 4 * t + e
+        if c is None:
+            w, xo, pb, parts = 16, 4096, "pb6", 1
+            a16, acd, t16, tcd, l = R("A16c", 16, 16 * i), R("ACc", 16, 16 * i), R("T16c", 16, 16 * t), R("TTc", 16, 16 * t), R("Lc", 16)
+        else:
+            w, xo, pb, parts = CW, 16 * CW * c, "pb%d" % (2 + c % 4), SPLIT
+            a16, acd = R("A16", w, L * i + w * c) if i != 4 else R("T16", w, w * c), R("AC", w, L * i + w * c)
+            t16, tcd, l = R("T16", w, L * t + w * c), R("TT", w, L * t + w * c), R("Lr", w, L * t + w * c)
+        n, ps = 16 * w, "ps%d" % t
+        tag = "t%d%d%s" % (t, e, c)
+        for s in range(parts):
+            nn, ww = n // parts, w // parts
+            xs, ts_, as_ = R("x", nn, xo + nn * s), R(t16[0], ww, t16[1] + ww * s), R(a16[0], ww, a16[1] + ww * s)
+            gath(xs, R("P%d" % t, W), ts_, tag="x" + tag, comp=True)
+            add("v", ga(nn), lambda g, T, X, xs=xs, as_=as_: g.vector.tensor_tensor(T["mk"][:, xs[1]:xs[2]], T[ps][:, 0:W].indirect(S(T, as_)), S(T, xs), A.is_gt),
+                [R(ps, W), as_, xs], [("mk", xs[1], xs[2])], tag="m" + tag)
+        mm(R(pb, w), [(R("Z", 128, 15 - k), ("mk", xo + k, xo + n, 16)) for k in range(16)], tag="c" + tag)
+        h0 = hot[0]
+        hot[0] += SMH if c is not None else 0.0
+        tt(R(pb, w, 128), R(pb, w), acd, A.min)
+        tt(tcd, R(pb, w, 128), tcd, A.max)
+        if c is not None or e < 3:
+            ts(l, tcd, 2047, A.bitwise_and)
+        if e < 3 or (t == 0 and c is not None):
+            copy(t16, l)
+        hot[0] = h0
+
+    def claims(t):
+        P, O, LO = "P%d" % t, "O%d" % t, "LO%d" % t
+        ts(R("hl", 16, 32 * t), R("TTc", 16, 16 * t), 7, A.logical_shift_right, 15, A.bitwise_and)
+        ts(R("hl", 16, 32 * t + 16), R("TTc", 16, 16 * t), 127, A.bitwise_and)
+        copy(R("hlb", 32, 32 * t), R("hl", 32, 32 * t))
+        for s in range(16):
+            ts(R("OH", 128, 128 * s), R("IB", 128), R("hlb", 1, 32 * t + s), A.is_equal, cyc=0.5)
+            ts(R("OL", 128, 128 * s), R("IL", 128), R("hlb", 1, 32 * t + 16 + s), A.is_equal, cyc=0.5)
+        mm(R("pb7", 128), [(R("OH", 128, 128 * s), R("OL", 128, 128 * s)) for s in range(16)], tag="C%d" % t)
+        if t == 0:
+            ts(R("C", 128), R("pb7", 128), 1.0, A.min, 256.0, A.mult)
+        else:
+            ts(R("C", 128, 128), R("pb7", 128), 1.0, A.min)
+        for b in range(4):
+            pb, o = "pb%d" % (b % 2), 512 * b
+
+            def fn(g, T, X, o=o, pb=pb):
+                r = None
+                for h in range(0, 512, 128):
+                    if t == 0:
+                        g.tensor.matmul(T[pb][:, h:h + 128], T["ID"][:], T[P][:, o + h:o + h + 128], True, False)
+                    r = g.tensor.matmul(T[pb][:, h:h + 128], T["E"][:, o + h:o + h + 128], T["C"][:, 128 * t:128 * t + 128], t == 1, True)
+                return r
+            add("t", 512 * CYC * (2 - t), fn, [R("ID", 128), R(P, 512, o), R("E", 512, o), R("C", 128, 128 * t)], [R(pb, 512)], tag="F")
+            if t == 0:
+                relu(R(O, 512, o), R(pb, 512), R("mo", 1), 1.0, tag="O")
+            else:
+                tt(R(O, 512, o), R(pb, 512), R(P, 512, o), A.mult, tag="O")
+            if (b + 1) * 512 % BW == 0:
+                k = ((b + 1) * 512 - 1) // BW
+                add("g", 1.0, lambda g, T, X, k=k: X["send"](g, T, t, k), [R(O, BW, BW * k)], [("wire%d" % t, k, k + 1)], kind="r", tag="send")
+                for far in (0, 1):
+                    add("x%d%d%d" % (far, t, k), ((XT, XT1)[t] + 3.0 * k) * (FP, 1.0)[far], "%s%d_%d" % (("arr", "far")[far], t, k), [("wire%d" % t, k, k + 1)],
+                        [R(LO, BW, q * W + BW * k) for q in ((0,), (1, 2))[far]], kind="x", tag="arrive")
+
+    def prices(t):
+        P, N, LO = "P%d" % t, "P%d" % (t + 1), "LO%d" % t
+        for b in range(4):
+            o, pb = 512 * b, "pb%d" % (b % 2)
+            mm(R(pb, 512), [(R("ID", 128), R(P, 512, o)), (R("DG", 128), R(LO, 512, o))], tag="W1", last=False)
+            mm(R(pb, 512), [(R("DG", 128), R(LO, 512, q * W + o)) for q in (1, 2)], tag="W2", first=False)
+            ts(R("N16", 512, o), R(pb, 512), 1025.0 - 63.0 / 128, A.add, 1280.0, A.min)
+            ts(R(N, 512, o), R("N16", 512, o), -1025.0, A.add, cyc=0.5)
+            if t == 0:
+                relu(R("ps1", 512, o), R(N, 512, o), R("scf", 1, 1), -1.0, tag="ps1")
+            else:
+                dma(lambda T, o=o: T.yp[:, o:o + 512], lambda T, o=o: T["P2"][:, o:o + 512], 128, [R("P2", 512, o)], [], q="ys"[b % 2])
+
+    def parents(t):
+        for h in range(2):
+            o, k = L * t + 128 * h, 2 * t + h
+            ts(R("hi", 128, o), R("TT", 128, o), 11, A.logical_shift_right, 7, A.bitwise_and)
+            copy(R("hb", 128, o), R("hi", 128, o))
+            mm(R("pb7", 128), [(R("hb", 128, o), R("ID", 128))], tag="hT")
+            add("v", vc(128), lambda g, T, X, k=k: g.vector.tensor_tensor_scan(T["hm"][:, 128 * k:128 * k + 128], T["scd"][:, 0:128], T["pb7"][:, 0:128], 0.0, A.mult, A.max),
+                [R("scd", 128), R("pb7", 128)], [R("hm", 128, 128 * k)])
+            ts(("Y", 144 * k + 15, 144 * k + 128, 16), ("hm", 128 * k + 15, 128 * k + 128, 16), 256.0, A.mult)
+            y, q, p = 144 * k, 16 * t + 8 * h, R("pb7", 8, 256)
+            mm(p, [(R("Y", 128, y + 15 - s), ("ID", s, 128, 16)) for s in range(16)], tag="elist")
+            ts(R("e1", 8, q), p, 0.0, A.is_equal, 1024.0, A.mult)
+            tt(R("e2", 8, q), p, R("LT", 8, 8 * h), A.add)
+            tt(R("e3", 8, q), R("e2", 8, q), R("e1", 8, q), A.add)
+            copy(R("el", 8, q), R("e3", 8, q))
+
+    hot[0] = HOT
+    for e in range(4):
+        trial(0, e, None)
+    claims(0)
+    chain(4)
+    chain(5)
+    for e in range(4):
+        for c in range(NCH):
+            hot[0] = -CO[0][c]
+            trial(0, e, c)
+    hot[0] = 0.0
+    prices(0)
+    for c in range(NCH):
+        r = lambda b, k=0: R(b, CW, k + CW * c)
+        n = 16 * CW
+        gath(R("x", n, n * c), R("P0", W), r("T16"), tag="x04%d" % c)
+        add("v", vc(n, 0.5), lambda g, T, X, c=c, n=n: g.vector.tensor_tensor_scan(T["sm"][:, n * c:n * c + n], T["scd"][:, 0:n], T["x"][:, n * c:n * c + n], 0.0, A.mult, A.max),
+            [R("scd", n), R("x", n, n * c)], [R("sm", n, n * c)], tag="scan")
+        mm(R("pb7", CW), [(R("BDw", 128), ("sm", n * c + 15, n * c + n, 16))], tag="u")
+        ts(r("w1"), R("pb7", CW), 2.0, A.mult, 1.0, A.add)
+        ts(r("w2"), r("w1"), 2047, A.bitwise_and)
+        ts(r("Q"), r("w2"), 32.0, A.add)
+        tt(r("w3"), r("Q"), r("Lr"), A.mult)
+        ts(r("w4"), r("w3"), 2464.0, A.add)
+        ts(r("w5"), r("w4"), 5, A.logical_shift_right, 2047, A.bitwise_and)
+        copy(r("T16", L), r("w5"))
+        ts(r("TT", L), r("w5"), float(OFFS), A.add)
+        copy(r("yhf"), r("Lr"))
+        act(r("AC", 4 * L), r("yhf"), con[0])
+    dma(lambda T: T.yh[:, 0:L], lambda T: T["yhf"][:, 0:L], 128, [R("yhf", L)], [])
+    hot[0] = HOT / 2
+    dma(lambda T: T["T16c"][:, 16:32], lambda T: T["T16"][1::16, L:2 * L], 8, [R("T16", L, L)], [R("T16c", 16, 16)])
+    dma(lambda T: T["TTc"][:, 16:32], lambda T: T["TT"][1::16, L:2 * L], 8, [R("TT", L, L)], [R("TTc", 16, 16)])
+    claim_forms(4, 1)
+    parents(0)
+    for e in (1, 2, 3):
+        gath(R("Bf", L, L * e), R("Btab", 4 * L, 512 + L * (e - 1)), R("el", 16))
+        lot_forms(4 + e, R("Bf", L, L * e), e)
+    hot[0] = -HOT
+    for j in range(3):
+        gath(R("ctab", L, L * (j + 1)), R("btab", 4 * L, L * j), R("el", 16))
+    dma(lambda T: T.yv[:, 0:L], lambda T: T["ctab"][0::16, L:2 * L], 8, [R("ctab", L, L)], [])
+    hot[0] = HOT
+    for e in range(4):
+        trial(1, e, None)
+    claims(1)
+    for e in range(4):
+        for c in range(NCH):
+            hot[0] = -CO[1][c]
+            trial(1, e, c)
+    hot[0] = 0.0
+    prices(1)
+    for c in range(NCH):
+        copy(R("yhf", CW, L + CW * c), R("Lr", CW, L + CW * c))
+        if c % 2:
+            o = L + 128 * (c // 2)
+            dma(lambda T, o=o: T.yh[:, o:o + 128], lambda T, o=o: T["yhf"][:, o:o + 128], 64, [R("yhf", 128, o)], [])
+    parents(1)
+    for h in range(2):
+        gath(R("par", 128, 128 * h), R("ctab", 4 * L), R("el", 8, 16 + 8 * h))
+        dma(lambda T, h=h: T.yv[:, L + 128 * h:L + 128 * h + 128], lambda T, h=h: T["par"][0::16, 128 * h:128 * h + 128], 4, [R("par", 128, 128 * h)], [])
+    return ops
+
+
+def depend(ops):
+    acc, deps = {}, []
+    for i, o in enumerate(ops):
+        d = set()
+        for wr, rs in ((False, o["rd"]), (True, o["wr"])):
+            for r in rs:
+                for (j, a, b, w) in acc.get(r[0], []):
+                    bank = r[0][:2] == "pb" and ops[j]["q"] != o["q"]
+                    if j != i and (bank or ((w or wr) and a < r[2] and r[1] < b)):
+                        d.add(j)
+        for wr, rs in ((False, o["rd"]), (True, o["wr"])):
+            for r in rs:
+                lst = acc.setdefault(r[0], [])
+                if wr and r[0][:2] != "pb" and len(r) == 3:
+                    lst[:] = [e for e in lst if not (r[1] <= e[1] and e[2] <= r[2] and e[0] in d)]
+                lst.append((i, r[1], r[2], wr))
+        deps.append(sorted(d))
+    return deps
+
+
+def schedule(ops, deps):
+    n = len(ops)
+    succ = [[] for _ in range(n)]
+    for i, d in enumerate(deps):
+        for j in d:
+            succ[j].append(i)
+    lev = [0.0] * n
+    for i in range(n - 1, -1, -1):
+        lev[i] = ops[i]["cost"] + max([lev[k] + LAT for k in succ[i]] or [0.0])
+    wgt = [lev[i] + ops[i]["hot"] + JIT * ((i + 1) * MIX % 1009) / 1009.0 for i in range(n)]
+    left = [len(d) for d in deps]
+    ready = [0.0] * n
+    cand, free, order = {}, {}, []
+    for i in range(n):
+        if not left[i]:
+            cand.setdefault(ops[i]["q"], []).append(i)
+    while True:
+        best = None
+        for q, l in cand.items():
+            if l:
+                t = max(free.get(q, 0.0), min(ready[i] for i in l))
+                if best is None or t < best[0]:
+                    best = (t, q)
+        if best is None:
+            break
+        t, q = best
+        i = max((i for i in cand[q] if ready[i] <= t + (DH if ops[i]["hot"] > 100 else DM) + 1e-9), key=lambda i: (wgt[i], -i))
+        t = max(t, ready[i])
+        cand[q].remove(i)
+        o = ops[i]
+        fin = t + o["cost"]
+        if o["kind"] == "d":
+            free["dma"] = max(free.get("dma", 0.0), t) + o["cost"] - 2.0
+            fin = free["dma"] + 2.0
+        free[q] = t + (0.1 if o["kind"] == "d" else o["cost"])
+        order.append(i)
+        for k in succ[i]:
+            left[k] -= 1
+            ready[k] = max(ready[k], fin + LAT)
+            if not left[k]:
+                cand.setdefault(ops[k]["q"], []).append(k)
+    assert len(order) == n
+    return order
+
+
+PLAN = {}
+
+
+def plan():
+    if "ops" not in PLAN:
+        PLAN["ops"] = build()
+        PLAN["deps"] = depend(PLAN["ops"])
+        PLAN["order"] = schedule(PLAN["ops"], PLAN["deps"])
+    return PLAN["ops"], PLAN["deps"], PLAN["order"]
+
+
+def routes(cores, topo):
+    out = []
+    for c in cores:
+        peers = [d for d in cores if d != c and topo.same_plane(c, d)]
+        far = [d for d in cores if d != c and not topo.same_plane(c, d)]
+        mine = sorted(peers + [c]).index(c)
+        hop = {}
+        for k, d in enumerate(far):
+            own = (mine + k) % 2 == 0
+            hop[d] = [h for h in topo.cores_of(c) if h not in cores and topo.may_write(h, d) and (topo.die(h) == topo.die(c)) == own][0]
+        out.append((peers, hop))
+    return out
+
+
+def slot(cores, src, dst, topo):
+    rest = [c for c in cores if c != dst]
+    return sorted(rest, key=lambda c: (not topo.same_plane(c, dst), c)).index(src)
+
+
+def bits(es):
+    return sum(1 << e for e in es)
+
+
+def onchip(c, peers, topo, h):
+    off = topo.engines(c, peers[0])
+    return [e for e in topo.engines(c, h) if e not in off]
+
+
+def hand_on(g, core, T, topo):
+    cores = list(T.cores)
+    for c, (peers, hop) in zip(cores, routes(cores, topo)):
+        for d, h in hop.items():
+            if h != core:
+                continue
+            es, into = topo.engines(core, d), onchip(c, peers, topo, h)
+            rid, pid = topo.addr(d, core)
+            k = slot(cores, c, d, topo)
+            for t in range(2):
+                for b in range(NB):
+                    g.wait_ge(T.sem["hin%d_%d" % (t, b)], len(into))
+                    o = k * W + BW * b
+                    g.remote_dma(T["LO%d" % t][:, o:o + BW], T["HB"][:, t * W + BW * b:t * W + BW * b + BW],
+                                 T.sem["far%d_%d" % (t, b)], T.sem["hs"], pid, rid, bits(es))
+            g.wait_ge(T.sem["hs"], 2 * NB * len(es))
+
+
+def rank_program(g, core, T, topo):
+    if T.rank_of(core) is None:
+        hand_on(g, core, T, topo)
+        return
+    cores = list(T.cores)
+    rt = routes(cores, topo)
+    peers, hop = rt[T.rank_of(core)]
+    ops, deps, order = plan()
+    eng = {"v": g.vector, "s": g.scalar, "t": g.tensor, "y": g.sync, "g": g}
+    sent = [0]
+
+    def send(g_, T_, t, b):
+        p, hs = peers[0], list(hop.values())
+        src = T["O%d" % t][:, BW * b:BW * b + BW]
+        dst = lambda h: DstId(rid=topo.addr(h, core)[0], pnc=topo.addr(h, core)[1])
+        k = slot(cores, core, p, topo) * W + BW * b
+        e0, e1 = topo.engines(core, p), onchip(core, peers, topo, hs[0])
+        g.remote_dma_fused([
+            RemoteDMATransfer(dst_ids=[dst(p)], dma_engine_mask=bits(e0), remote_sem=T.sem["arr%d_%d" % (t, b)],
+                              srcs=[src], dsts=[T["LO%d" % t][:, k:k + BW]]),
+            RemoteDMATransfer(dst_ids=[dst(h) for h in hs], dma_engine_mask=bits(e1), remote_sem=T.sem["hin%d_%d" % (t, b)],
+                              srcs=[src], dsts=[T["HB"][:, t * W + BW * b:t * W + BW * b + BW] for h in hs])],
+            local_sem=T.sem["snd"])
+        sent[0] += len(e0) + len(e1)
+
+    arrive = {"a": len(topo.engines(peers[0], core)), "f": sum(len(topo.engines(h[core], core)) for _, h in rt if core in h)}
+    X = {"send": send}
+    cnt = {"v": 0, "s": 0, "t": 0, "g": 0}
+    clock = {q: {} for q in eng}
+    done = {}
+    pos = {i: k for k, i in enumerate(order)}
+    nd = 0
+    for i in order:
+        o = ops[i]
+        if o["kind"] == "x":
+            n = arrive[o["fn"][0]]
+            done[i] = (o["fn"], n, {o["fn"]: n})
+            continue
+        q = o["q"]
+        ck = clock[q]
+        for j in sorted(deps[i], key=lambda j: -pos[j]):
+            if j in done:
+                s, n, c2 = done[j]
+                if ck.get(s, 0) < n:
+                    eng[q].wait_ge(T.sem[s], n)
+                    for k, v in c2.items():
+                        ck[k] = max(ck.get(k, 0), v)
+        ins = o["fn"](g, T, X)
+        if o["kind"] == "c":
+            cnt[q] += 1
+            s, n = "q" + q, cnt[q]
+            ins.then_inc(T.sem[s], 1)
+        elif o["kind"] == "d":
+            s, n = "d%d" % nd, 16
+            nd += 1
+            ins.then_inc(T.sem[s], 16)
+        else:
+            continue
+        c2 = dict(ck)
+        c2[s] = n
+        done[i] = (s, n, c2)
+    for q, n in cnt.items():
+        g.wait_ge(T.sem["q" + q], n)
+    for k in range(nd):
+        g.wait_ge(T.sem["d%d" % k], 16)
+    g.wait_ge(T.sem["snd"], sent[0])

@@ -1,57 +1,49 @@
 from concourse.bass import DstId, RemoteDMATransfer
 from concourse.mybir import AluOpType, ActivationFunctionType
 
-OFFS, BIG = 131072, 16384
+BIG = 16384
 W, L, H0 = 2048, 256, 768
 NCH, CW = 4, 64
-NB = 2
+NB = 4
 BW = W // NB
 BF, F32, I32, U16, F16 = "bfloat16", "float32", "int32", "uint16", "float16"
-CYC = 0.83e-3 * 1.2
-LAT, HOT, XT, XT1, FP = 0.1, 500.0, 14.0, 14.0, 0.6
-DH, DM = 0.1, 0.05
-SMH, JIT, MIX = 2.0, 0.3, 933
-CO = ((0, 0, 0, 0), (0, -1.6, 0, 0))
-SPLIT = 2
+CFG = {"cyc": 0.83e-3 * 1.15, "g": 1.55, "lat": 0.1, "hot": 500.0, "it": 3, "xt": (13.0, 13.0), "xs": 1.5, "rep": False, "dh": 0.1, "dm": 0.05, "pr": ("SVSV", "VMVM"), "of": ("SSSS", "SSSS"),
+       "av": "", "route": "B", "yw": 1, "sw": 1, "split": (2, 2, 1, 1, 2, 2, 1, 1), "ch": (20.0, 0.0), "ph": 0.0, "smh": 2.0, "yh": 0.0, "co": ((0, 0, 0, 0), (0, 0, 0, 0))}
 
 SCRATCH = {
-    "P0": ("sbuf", [128, W], BF), "P1": ("sbuf", [128, W], BF), "P2": ("sbuf", [128, W], BF),
-    "ps0": ("sbuf", [128, W], BF), "ps1": ("sbuf", [128, W], BF),
-    "pk": ("sbuf", [128, H0], I32), "pv": ("sbuf", [128, H0], I32), "lt": ("sbuf", [128, L], I32),
-    "lc": ("sbuf", [128, 16], I32), "ac": ("sbuf", [128, 16], I32),
+    "PW0": ("sbuf", [128, 4 * W], BF), "PW1": ("sbuf", [128, 4 * W], BF), "P2": ("sbuf", [128, W], BF),
+    "pk": ("sbuf", [128, H0], I32), "pv": ("sbuf", [128, H0], I32), "PK": ("sbuf", [128, H0], F32), "ac": ("sbuf", [128, 16], I32),
     "ic": ("sbuf", [128, 1], I32), "wc": ("sbuf", [128, 1], I32), "sc": ("sbuf", [128, 2], I32),
-    "icf": ("sbuf", [128, 1], F32), "wcf": ("sbuf", [128, 1], F32), "scf": ("sbuf", [128, 2], F32), "mo": ("sbuf", [128, 1], F32),
+    "icf": ("sbuf", [128, 1], F32), "wcf": ("sbuf", [128, 1], F32), "scf": ("sbuf", [128, 2], F32), "cst": ("sbuf", [128, 4], F32),
     "ip": ("sbuf", [128, 1], I32), "im": ("sbuf", [128, 128], I32), "on": ("sbuf", [128, W], BF),
     "pg": ("sbuf", [128, 1], I32), "pgf": ("sbuf", [128, 1], F32), "pg16": ("sbuf", [128, 1], F32), "ipf": ("sbuf", [128, 1], F32),
-    "pl": ("sbuf", [128, 1], I32), "plf": ("sbuf", [128, 1], F32), "mg": ("sbuf", [128, 128], I32),
-    "Z": ("sbuf", [128, 144], BF), "Zh": ("sbuf", [128, 144], F16), "BR": ("sbuf", [128, 128], F16),
+    "mg": ("sbuf", [128, 128], I32), "i16": ("sbuf", [128, 16], F32), "LV": ("sbuf", [128, 80], F32),
+    "Z": ("sbuf", [128, 144], BF), "Zh": ("sbuf", [128, 144], F16), "NG": ("sbuf", [128, 128], BF),
     "BDw": ("sbuf", [128, 128], BF), "IB": ("sbuf", [128, 128], BF), "IL": ("sbuf", [128, 128], BF),
-    "ID": ("sbuf", [128, 128], BF), "DG": ("sbuf", [128, 128], BF), "E": ("sbuf", [128, W], BF),
-    "scd": ("sbuf", [128, 1024], BF), "LT": ("sbuf", [128, 16], F32),
-    "pvh": ("sbuf", [128, H0], F16), "vt": ("sbuf", [128, H0], F32), "btab": ("sbuf", [128, 6 * L], F32),
-    "Btab": ("sbuf", [128, 512 + 6 * L], F32), "bh": ("sbuf", [128, 6 * L], F16), "lst": ("sbuf", [128, 6 * 16], U16),
-    "A16": ("sbuf", [128, 8 * L], U16), "AC": ("sbuf", [128, 8 * L], F32), "Bf": ("sbuf", [128, 4 * L], F32),
+    "ID": ("sbuf", [128, 128], BF), "IDh": ("sbuf", [128, 128], F16), "NI": ("sbuf", [128, 128], BF), "DG": ("sbuf", [128, 128], BF),
+    "E": ("sbuf", [128, W], BF), "WP": ("sbuf", [128, 512], BF), "scd": ("sbuf", [128, 1024], BF),
+    "bh": ("sbuf", [128, 6 * L], F16), "lst": ("sbuf", [128, 8 * 16], U16), "B": ("sbuf", [128, 160], F32),
+    "A16": ("sbuf", [128, 8 * L], U16), "AC": ("sbuf", [128, 8 * L], F32),
     "A16c": ("sbuf", [128, 8 * 16], U16), "ACc": ("sbuf", [128, 8 * 16], F32),
     "T16": ("sbuf", [128, 2 * L], U16), "TT": ("sbuf", [128, 2 * L], I32), "Lr": ("sbuf", [128, 2 * L], I32),
     "T16c": ("sbuf", [128, 32], U16), "TTc": ("sbuf", [128, 32], I32), "Lc": ("sbuf", [128, 16], I32),
-    "x": ("sbuf", [128, 4096 + 256], BF), "mk": ("sbuf", [128, 4096 + 256], BF), "sm": ("sbuf", [128, 4096], BF),
-    "yhf": ("sbuf", [128, 2 * L], F32), "Q": ("sbuf", [128, L], I32),
-    "w1": ("sbuf", [128, L], I32), "w2": ("sbuf", [128, L], I32), "w3": ("sbuf", [128, L], I32), "w4": ("sbuf", [128, L], I32),
-    "w5": ("sbuf", [128, L], I32),
-    "hi": ("sbuf", [128, 2 * L], I32), "hb": ("sbuf", [128, 2 * L], BF), "hm": ("sbuf", [128, 512], BF),
-    "Y": ("sbuf", [128, 4 * 144], BF), "e1": ("sbuf", [128, 32], F32), "e2": ("sbuf", [128, 32], F32), "e3": ("sbuf", [128, 32], F32),
-    "el": ("sbuf", [128, 32], U16), "ctab": ("sbuf", [128, 4 * L], F32), "par": ("sbuf", [128, L], F32),
+    "Y": ("sbuf", [128, 8 * 4096], BF), "Yc": ("sbuf", [128, 8 * L], BF), "mk": ("sbuf", [128, 4096 + 256], BF),
+    "X": ("sbuf", [128, 4096], BF), "sm": ("sbuf", [128, 4096], BF),
+    "yhf": ("sbuf", [128, 2 * L], F32), "w1": ("sbuf", [128, L], I32), "w2": ("sbuf", [128, L], I32), "w3": ("sbuf", [128, L], I32),
+    "w4": ("sbuf", [128, L], I32),
+    "hb": ("sbuf", [128, 2 * L], BF), "ht": ("sbuf", [128, 2 * L], BF), "hm": ("sbuf", [128, 2 * L], BF),
+    "mb": ("sbuf", [128, 160], F16), "ph": ("sbuf", [128, 32], F16), "par": ("sbuf", [128, 2 * L], F32),
     "hl": ("sbuf", [128, 64], I32), "hlb": ("sbuf", [128, 64], F32),
     "OH": ("sbuf", [128, 16 * 128], BF), "OL": ("sbuf", [128, 16 * 128], BF), "C": ("sbuf", [128, 256], BF),
-    "O0": ("sbuf", [128, W], BF), "O1": ("sbuf", [128, W], BF), "N16": ("sbuf", [128, W], F16),
+    "O0": ("sbuf", [128, W], BF), "O1": ("sbuf", [128, W], BF), "N16": ("sbuf", [128, W], F16), "D": ("sbuf", [128, W], BF),
     "LO0": ("sbuf", [128, 3 * W], BF), "LO1": ("sbuf", [128, 3 * W], BF),
-    "HB": ("sbuf", [128, 2 * W], BF),
+    "HB": ("sbuf", [128, 2 * BW], BF),
 }
 for _i in range(8):
     SCRATCH["pb%d" % _i] = ("psum", [128, 512], F32)
-ND = 48
-SEMAPHORES = ["qv", "qs", "qt", "qg", "snd", "hs"] + ["d%d" % i for i in range(ND)] + \
-    ["%s%d_%d" % (n, t, b) for n in ("arr", "far", "hin") for t in range(2) for b in range(NB)]
+ND = 56
+SEMAPHORES = ["qv", "qs", "qt", "qg", "snd", "hs", "hin0", "hin1"] + ["d%d" % i for i in range(ND)] + \
+    ["%s%d_%d" % (n, t, b) for n in ("arr", "far") for t in range(2) for b in range(NB)]
 
 A = AluOpType
 AF = ActivationFunctionType
@@ -60,6 +52,7 @@ AF = ActivationFunctionType
 def build():
     ops = []
     hot = [0.0]
+    CYC, HOT = CFG["cyc"], CFG["hot"]
 
     def add(q, cost, fn, rd, wr, kind="c", tag=""):
         ops.append({"q": q, "cost": cost, "fn": fn, "rd": rd, "wr": wr, "kind": kind, "tag": tag, "hot": hot[0]})
@@ -68,18 +61,18 @@ def build():
         return max(64, n * cyc) * CYC + 0.01
 
     def ga(n):
-        return n * 1.55 * CYC + 0.06
+        return n * CFG["g"] * CYC + 0.06
 
-    def S(T, r):
-        return T[r[0]][:, r[1]:r[2]] if len(r) == 3 else T[r[0]][:, r[1]:r[2]:r[3]]
+    def S(T, r, p=128):
+        return T[r[0]][0:p, r[1]:r[2]] if len(r) == 3 else T[r[0]][0:p, r[1]:r[2]:r[3]]
 
     def n_of(r):
         return len(range(*r[1:]))
 
-    def copy(out, in_, cyc=1.0, tag=""):
-        add("v", vc(n_of(out), cyc), lambda g, T, X: g.vector.tensor_copy(S(T, out), S(T, in_)), [in_], [out], tag=tag)
+    def copy(out, in_, cyc=1.0):
+        add("v", vc(n_of(out), cyc), lambda g, T, X: g.vector.tensor_copy(S(T, out), S(T, in_)), [in_], [out])
 
-    def ts(out, in_, s1, op0, s2=None, op1=None, cyc=1.0, tag=""):
+    def ts(out, in_, s1, op0, s2=None, op1=None, cyc=1.0):
         rd = [in_] + [s for s in (s1, s2) if isinstance(s, tuple)]
 
         def fn(g, T, X):
@@ -88,315 +81,356 @@ def build():
             if op1 is None:
                 return g.vector.tensor_scalar(S(T, out), S(T, in_), a, None, op0)
             return g.vector.tensor_scalar(S(T, out), S(T, in_), a, b, op0, op1)
-        add("v", vc(n_of(out), cyc), fn, rd, [out], tag=tag)
+        add("v", vc(n_of(out), cyc), fn, rd, [out])
 
-    def tt(out, a, b, op, tag=""):
+    def tt(out, a, b, op):
         two = 1.0 if (a[0][:2] == "pb" or b[0][:2] == "pb") else 2.0
-        add("v", vc(n_of(out), two), lambda g, T, X: g.vector.tensor_tensor(S(T, out), S(T, a), S(T, b), op), [a, b], [out], tag=tag)
+        add("v", vc(n_of(out), two), lambda g, T, X: g.vector.tensor_tensor(S(T, out), S(T, a), S(T, b), op), [a, b], [out])
 
-    def act(out, in_, bias=0.0, tag=""):
+    def scan(out, in_):
+        n = n_of(out)
+        add("v", vc(n, 0.5), lambda g, T, X: g.vector.tensor_tensor_scan(S(T, out), T["scd"][:, 0:n], S(T, in_), 0.0, A.mult, A.max),
+            [("scd", 0, n), in_], [out])
+
+    def vgath(out, win, off):
+        add("v", ga(n_of(out)), lambda g, T, X: g.vector.tensor_copy(S(T, out), S(T, win).indirect(S(T, off))), [win, off], [out])
+
+    def act(out, in_, bias=0.0, scale=1.0, f=AF.Copy, off=None, p=128):
         def fn(g, T, X):
-            if bias:
-                return g.scalar.activation(S(T, out), S(T, in_), AF.Copy, bias=bias)
-            return g.scalar.activation(S(T, out), S(T, in_), AF.Copy)
-        add("s", n_of(out) * CYC + 0.06, fn, [in_], [out], tag=tag)
+            i = S(T, in_).indirect(S(T, off)) if off else S(T, in_, p)
+            return g.scalar.activation(S(T, out, p), i, f, bias=S(T, bias) if isinstance(bias, tuple) else bias, scale=scale)
+        add("s", ga(n_of(out)) if off else max(64, n_of(out)) * CYC + 0.03, fn, [r for r in (in_, bias, off) if isinstance(r, tuple)], [out])
 
-    def relu(out, in_, bias, scale, tag=""):
-        add("s", n_of(out) * CYC + 0.06, lambda g, T, X: g.scalar.activation(S(T, out), S(T, in_), AF.Relu, bias=S(T, bias), scale=scale),
-            [in_, bias], [out], tag=tag)
-
-    def gath(out, win, off, tag="", comp=False):
-        def fn(g, T, X):
-            i = S(T, win).indirect(S(T, off))
-            if comp:
-                return g.scalar.activation(S(T, out), i, AF.Copy, bias=255.0, scale=-1.0)
-            return g.scalar.activation(S(T, out), i, AF.Copy)
-        add("s", ga(n_of(out)), fn, [win, off], [out], tag=tag)
-
-    def mm(out, pairs, tag="", k=128, first=True, last=True):
+    def mms(groups, m=128):
         def fn(g, T, X):
             r = None
-            for i, (l, h) in enumerate(pairs):
-                a, b = (S(T, l), S(T, h)) if k == 128 else (T[l[0]][0:k, l[1]:l[2]], T[h[0]][0:k, h[1]:h[2]])
-                r = g.tensor.matmul(S(T, out), a, b, first and i == 0, last and i == len(pairs) - 1)
+            for out, pairs in groups:
+                for i, (l, h) in enumerate(pairs):
+                    r = g.tensor.matmul(S(T, out, m), S(T, l), S(T, h), i == 0, i == len(pairs) - 1)
             return r
-        add("t", sum(max(64, n_of(h)) for l, h in pairs) * CYC + 0.06, fn, [p for lh in pairs for p in lh], [out], tag=tag)
+        add("t", sum(max(min(64, m), n_of(h)) for _, ps in groups for l, h in ps) * CYC + 0.03, fn,
+            [p for _, ps in groups for lh in ps for p in lh], [o for o, _ in groups])
 
-    def dma(out, in_, kb, rd, wr, q="y", tag=""):
+    def mm(out, pairs):
+        mms([(out, pairs)])
+
+    def dma(out, in_, kb, rd, wr, q="y"):
         def fn(g, T, X):
             return (g.sync if q == "y" else g.scalar).dma_start(out(T), in_(T))
-        add(q, 2.0 + kb / 180.0, fn, rd, wr, kind="d", tag=tag)
+        add(q, 2.0 + kb / 200.0, fn, rd, wr, kind="d")
 
     def iota(out, pattern, base, cm, small=False):
-        n = n_of(out)
-
         def fn(g, T, X):
             if small:
                 return g.iota(S(T, out), pattern, base, cm, allow_small_or_imprecise_dtypes=True)
             return g.iota(S(T, out), pattern, base, cm)
-        add("g", 0.15 + 2 * n * CYC, fn, [], [out])
+        add("g", 0.15 + 2 * n_of(out) * CYC, fn, [], [out])
 
-    def select(out, in_, pattern, cmp, cm):
-        add("g", 0.17 + 2 * n_of(out) * CYC, lambda g, T, X: g.affine_select(S(T, out), S(T, in_), pattern, cmp, 0.0, 0, cm), [in_], [out])
+    def select(out, in_, pattern, cmp, cm, base=0):
+        add("g", 0.17 + 2 * n_of(out) * CYC, lambda g, T, X: g.affine_select(S(T, out), S(T, in_), pattern, cmp, 0.0, base, cm), [in_], [out])
 
-    def mset(out, v):
-        add("v", vc(n_of(out), 0.5), lambda g, T, X: g.vector.memset(S(T, out), v), [], [out])
+    def mset(out, v, cyc=0.5):
+        add("v", vc(n_of(out), cyc), lambda g, T, X: g.vector.memset(S(T, out), v), [], [out])
 
     R = lambda b, n, a=0: (b, a, a + n)
+    con = [float(2048 * (e + 1)) for e in range(4)]
+    P = [R("PW0", W), R("PW1", W)]
 
-    hot[0] = 2000.0
-    dma(lambda T: T["pv"][0:8, :], lambda T: T.prev[:], 24, [], [R("pv", H0)], q="s")
-    hot[0] = 1990.0
-    dma(lambda T: T["lc"][:], lambda T: T.lots[0::16, :], 8, [], [R("lc", 16)])
-    hot[0] = 1985.0
-    dma(lambda T: T["P0"][:, 0:W], lambda T: T.price[:], 512, [], [R("P0", W)], q="s")
-    hot[0] = 1980.0
-    dma(lambda T: T["sc"][:], lambda T: T.slack[:], 1, [], [R("sc", 2)])
-    dma(lambda T: T["ac"][:], lambda T: T.packs[0::16, H0 - L:H0], 8, [], [R("ac", 16)])
-    dma(lambda T: T["lt"][:], lambda T: T.lots[:], 128, [], [R("lt", L)])
-    hot[0] = 1970.0
-    dma(lambda T: T["pk"][:], lambda T: T.packs[:], 384, [], [R("pk", H0)])
-    hot[0] = 0.0
-    dma(lambda T: T["wc"][:], lambda T: T.wt[:], 1, [], [R("wc", 1)])
-    dma(lambda T: T["ic"][:], lambda T: T.inc[:], 1, [], [R("ic", 1)])
+    hot[0] = 9000.0
+    mset(R("pv", H0), 0, 1.0)
+    loads = [("TTc", 0, 16, lambda T: T.lots[0::16, :], 8), ("ac", 0, 16, lambda T: T.packs[0::16, H0 - L:H0], 8), ("sc", 0, 2, lambda T: T.slack[:], 1),
+             ("PW0", 0, W, lambda T: T.price[:], 512), ("pv", 0, H0, lambda T: T.prev[:], 24), ("pk", H0 - L, L, lambda T: T.packs[:, H0 - L:H0], 128),
+             ("TT", 0, L, lambda T: T.lots[:], 128), ("pk", 0, H0 - L, lambda T: T.packs[:, 0:H0 - L], 256),
+             ("wc", 0, 1, lambda T: T.wt[:], 1), ("ic", 0, 1, lambda T: T.inc[:], 1)]
+    for k, (b, a, n, src, kb) in enumerate(loads):
+        dma(lambda T, b=b, a=a, n=n: T[b][0::16 if b == "pv" else 1, a:a + n], src, kb, [], [R(b, n, a)])
+        ops[-1]["at"] = 0.15 * k + (k > 3)
+    for k in (1, 2, 3) if CFG["rep"] else ():
+        dma(lambda T, k=k: T["PW0"][:, k * W:k * W + W], lambda T: T.price[:], 512, [R("pk", H0)], [R("PW0", W, k * W)])
+    hot[0] = HOT
     iota(R("ip", 1), [[1, 1]], 0, 1)
     iota(R("im", 128), [[1, 128]], 0, 0)
-    iota(R("btab", L), [[1, L]], H0 - L, 0, True)
+    iota(R("on", 128), [[0, 128]], 1, 0, True)
+    hot[0] = 0.0
     iota(R("IL", 128), [[1, 128]], 0, 0, True)
-    iota(R("on", W), [[0, W]], 1, 0, True)
+    iota(R("on", W - 128, 128), [[0, W - 128]], 1, 0, True)
     select(R("ID", 128), R("on", 128), [[-1, 128]], A.is_equal, 1)
-    select(R("scd", 1024), R("on", 1024), [[0, 64], [1, 16]], A.not_equal, 0)
     select(R("E", W), R("on", W), [[-1, 16], [-16, 8], [0, 16]], A.is_equal, 1)
-    hot[0] = -HOT
-    iota(R("ctab", L), [[1, L]], H0, 0, True)
-    hot[0] = HOT
+    select(R("scd", 1024), R("on", 1024), [[0, 64], [1, 16]], A.not_equal, 0)
+    iota(R("i16", 16), [[16, 16]], H0 - L, 1, True)
+    iota(R("LV", 80), [[1, 5], [0, 16]], 129, 0, True)
+    for h in range(2):
+        for k in range(2):
+            select(R("WP", 128, 128 * (2 * h + k)), R("on", 128), [[-32, 4], [1000, 2], [-1, 16]], A.is_equal, 1, -16 * h - 1000 * k)
+    hot[0] = 5 * HOT
     mset(R("Z", 144), 0.0)
+    mset(R("NG", 128), -BIG / 16.0)
+    for k, v in enumerate((-256.0, -1.0, 384.0, 129.0)):
+        mset(R("cst", 1, k), v)
     ts(R("pg", 1), R("ip", 1), 4, A.logical_shift_right)
     copy(R("ipf", 1), R("ip", 1))
     copy(R("pgf", 1), R("pg", 1))
     ts(R("mg", 128), R("im", 128), 4, A.logical_shift_right)
     ts(("Z", 15, 128, 16), R("im", 8), R("pgf", 1), A.is_equal, float(BIG), A.mult)
-    ts(R("BR", 128), R("mg", 128), R("ipf", 1), A.is_equal)
-    ts(R("Zh", 144), R("Z", 144), 1.0 / BIG, A.mult)
-    hot[0] = 0.0
-    mset(R("mo", 1), -256.0)
+    ts(R("Zh", 144), R("Z", 144), 1.0 / BIG, A.mult, cyc=0.5)
     ts(R("pg16", 1), R("pg", 1), 16.0, A.mult)
     ts(R("IB", 128), R("im", 128), R("pg16", 1), A.subtract)
+    ts(R("NI", 128), R("im", 128), R("ipf", 1), A.is_equal, -1.0, A.mult)
+    ts(R("IDh", 128), R("im", 128), R("ipf", 1), A.is_equal)
+    hot[0] = 0.0
+    ts(R("B", 16, 16), R("i16", 16), R("pg16", 1), A.subtract)
+    ts(R("B", 16, 96), R("i16", 16), R("pg16", 1), A.subtract, float(L), A.add)
     ts(R("icf", 1), R("ic", 1), 1.0 / 64, A.mult)
     ts(R("DG", 128), R("im", 128), R("ipf", 1), A.is_equal, R("icf", 1), A.mult)
     copy(R("wcf", 1), R("wc", 1))
     ts(R("BDw", 128), R("mg", 128), R("pgf", 1), A.is_equal, R("wcf", 1), A.mult)
-    ts(R("pl", 1), R("ip", 1), 15, A.bitwise_and)
-    copy(R("plf", 1), R("pl", 1))
-    ts(R("LT", 16), R("im", 16), 16.0, A.mult, R("plf", 1), A.add)
-    ts(R("LT", 16), R("LT", 16), -256.0, A.add)
-    mset(R("Y", 576), 0.0)
-    con = [float(2048 * (e + 1) + OFFS) for e in range(4)]
+    ts(R("scf", 1, 1), R("sc", 1, 1), -1.0, A.mult)
     hot[0] = 4 * HOT
-    copy(R("T16c", 16), R("lc", 16))
-    hot[0] = 3 * HOT
+    copy(R("scf", 1), R("sc", 1))
     copy(R("A16c", 16), R("ac", 16))
-    ts(R("scf", 2), R("sc", 2), -1.0, A.mult, 255.0, A.add)
-    relu(R("ps0", W), R("P0", W), R("scf", 1), -1.0, tag="ps0")
+    copy(R("T16c", 16), R("TTc", 16))
     ts(R("ACc", 16), R("ac", 16), con[0], A.add)
-    ts(R("TTc", 16), R("lc", 16), float(OFFS), A.add)
-    hot[0] = HOT
-    for o, n in ((512, 256), (0, 512)):
-        add("v", vc(n), lambda g, T, X, o=o, n=n: g.vector.tensor_copy(T["pvh"][0:8, o:o + n], T["pv"][0:8, o:o + n]), [R("pv", n, o)], [R("pvh", n, o)])
-    mm(R("pb1", 256), [(R("BR", 128), R("pvh", 256, 512))], k=8)
-    mm(R("pb0", 512), [(R("BR", 128), R("pvh", 512))], k=8)
-    copy(R("bh", L, L), R("pb1", 256))
-    act(R("vt", 256, 512), R("pb1", 256))
-    act(R("vt", 512), R("pb0", 512))
+    hot[0] = 3 * HOT
+    for h in range(2):
+        copy(R("A16", 128, 128 * h), R("pk", 128, H0 - L + 128 * h))
+        copy(R("T16", 128, 128 * h), R("TT", 128, 128 * h))
     hot[0] = 2 * HOT
-    copy(R("T16", L), R("lt", L))
-    copy(R("A16", L), R("pk", L, H0 - L))
-    hot[0] = HOT
-    copy(R("Btab", H0), R("pk", H0))
+    copy(R("bh", L), R("pv", L, H0 - L))
+    copy(R("PK", L, H0 - L), R("pk", L, H0 - L))
+    copy(R("PK", H0 - L), R("pk", H0 - L))
     hot[0] = 0.0
-    ts(R("TT", L), R("lt", L), float(OFFS), A.add)
-    act(R("AC", L), R("Btab", L, 512), con[0])
-    hot[0] = -HOT
-    act(R("btab", L, L), R("vt", L, 512))
+    act(R("AC", L), R("PK", L, H0 - L), con[0])
 
-    def lot_forms(i, src, e):
-        copy(R("A16", L, L * i), src, tag="A16")
-        act(R("AC", L, L * i), src, con[e], tag="AC")
-        claim_forms(i, i // 4)
+    bank = lambda c: "pb%d" % (2 + c - c % CFG["sw"])
 
-    def claim_forms(i, t):
-        src, a = ("T16", 0) if i == 4 else ("A16", L * i)
-        dma(lambda T: T["A16c"][:, 16 * i:16 * i + 16], lambda T: T[src][t::16, a:a + L], 8, [R(src, L, a)], [R("A16c", 16, 16 * i)])
+    def claim_forms(i):
+        t = i // 4
+        dma(lambda T: T["A16c"][:, 16 * i:16 * i + 16], lambda T: T["A16"][t::16, L * i:L * i + L], 8, [R("A16", L, L * i)], [R("A16c", 16, 16 * i)])
         dma(lambda T: T["ACc"][:, 16 * i:16 * i + 16], lambda T: T["AC"][t::16, L * i:L * i + L], 8, [R("AC", L, L * i)], [R("ACc", 16, 16 * i)])
 
-    def chain(e):
-        hot[0] = HOT if e < 4 else 0.0
-        mm(R("pb7", 16), [(R("Zh", 128, 15 - s), ("bh", L * e + s, L * e + L, 16)) for s in range(16)], tag="list")
-        ts(R("lst", 16, 16 * e), R("pb7", 16), 1.0 / 16, A.mult)
-        if e < 5:
-            gath(R("btab", L, L * (e + 1)), R("vt", H0), R("lst", 16, 16 * e))
-            copy(R("bh", L, L * (e + 1)), R("btab", L, L * (e + 1)))
-        gath(R("Btab", L, 512 + L * e), R("Btab", H0), R("lst", 16, 16 * e))
-        if e < 4:
-            lot_forms(e, R("Btab", L, 512 + L * e), e)
+    def package(i):
+        t, e = i // 4, i % 4
+        ls = R("lst", 16, 16 * i)
+        if e < 3:
+            row = R("bh", L, L * (3 * t + e))
+            vgath(row, R("pv", H0), ls)
+            as_list(i + 1, row)
+        if str(i) in CFG["av"]:
+            vgath(R("A16", L, L * i), R("pk", H0), ls)
+            ts(R("AC", L, L * i), R("A16", L, L * i), con[e], A.add)
+        else:
+            act(R("AC", L, L * i), R("PK", H0), con[e], off=ls)
+            ts(R("A16", L, L * i), R("AC", L, L * i), -con[e], A.add)
+        claim_forms(i)
+
+    def as_list(i, row):
+        t, e = i // 4, i % 4
+        mm(R("pb7", 16), [(R("Zh", 128, 15 - s), (row[0], row[1] + s, row[2], 16)) for s in range(16)])
+        copy(R("lst", 16, 16 * i), R("pb7", 16))
+        h0 = hot[0]
         hot[0] = 0.0
+        for k in ((e + 1,), (0, 4))[e == 3]:
+            copy(R("B", 16, 80 * t + 16 * k), R("lst", 16, 16 * i))
+        hot[0] = h0
 
-    for e in range(1, 4):
-        chain(e)
-
-    def trial(t, e, c):
+    def ahead(t, e, c, k=1):
         i = 4 * t + e
         if c is None:
-            w, xo, pb, parts = 16, 4096, "pb6", 1
-            a16, acd, t16, tcd, l = R("A16c", 16, 16 * i), R("ACc", 16, 16 * i), R("T16c", 16, 16 * t), R("TTc", 16, 16 * t), R("Lc", 16)
+            act(R("Yc", L, L * i), P[t], R("scf", 1, t), f=AF.Identity, off=R("A16c", 16, 16 * i))
         else:
-            w, xo, pb, parts = CW, 16 * CW * c, "pb%d" % (2 + c % 4), SPLIT
-            a16, acd = R("A16", w, L * i + w * c) if i != 4 else R("T16", w, w * c), R("AC", w, L * i + w * c)
-            t16, tcd, l = R("T16", w, L * t + w * c), R("TT", w, L * t + w * c), R("Lr", w, L * t + w * c)
-        n, ps = 16 * w, "ps%d" % t
-        tag = "t%d%d%s" % (t, e, c)
-        for s in range(parts):
-            nn, ww = n // parts, w // parts
-            xs, ts_, as_ = R("x", nn, xo + nn * s), R(t16[0], ww, t16[1] + ww * s), R(a16[0], ww, a16[1] + ww * s)
-            gath(xs, R("P%d" % t, W), ts_, tag="x" + tag, comp=True)
-            add("v", ga(nn), lambda g, T, X, xs=xs, as_=as_: g.vector.tensor_tensor(T["mk"][:, xs[1]:xs[2]], T[ps][:, 0:W].indirect(S(T, as_)), S(T, xs), A.is_gt),
-                [R(ps, W), as_, xs], [("mk", xs[1], xs[2])], tag="m" + tag)
-        mm(R(pb, w), [(R("Z", 128, 15 - k), ("mk", xo + k, xo + n, 16)) for k in range(16)], tag="c" + tag)
+            act(R("Y", 16 * CW * k, 4096 * i + 16 * CW * c), P[t], R("scf", 1, t), f=AF.Identity, off=R("A16", CW * k, L * i + CW * c))
+
+    def compare(t, e, c):
+        i = 4 * t + e
+        if c is None:
+            w, mo, y, win, off, out = 16, 4096, R("Yc", L, L * i), P[t], R("T16c", 16, 16 * t), R("pb6", 16)
+        else:
+            w, mo, win, off = CW, 16 * CW * c, R("PW%d" % t, W * (e + 1) if CFG["rep"] else W), R("T16", CW, L * t + CW * c)
+            y, out = R("Y", 16 * w, 4096 * i + mo), R(bank(c), w, w * (c % CFG["sw"]))
+        n = 16 * w
+        k = 1 if c is None else CFG["split"][i]
+        for j in range(k):
+            m, o, yy = R("mk", n // k, mo + n // k * j), R(off[0], w // k, off[1] + w // k * j), R(y[0], n // k, y[1] + n // k * j)
+            add("v", ga(n // k), lambda g, T, X, m=m, o=o, yy=yy: g.vector.tensor_tensor(S(T, m), S(T, win).indirect(S(T, o)), S(T, yy), (A.is_gt, A.is_lt)[t]),
+                [win, o, yy], [m])
+        mm(out, [(R("NG", 128), R("on", w))] + [(R("Z", 128, 15 - k), ("mk", mo + k, mo + n, 16)) for k in range(16)])
+
+    def revert(t, e, c, k=1):
+        i = 4 * t + e
+        if c is None:
+            pb, w, o = "pb6", 16, 0
+            a, tc, t16 = R("ACc", 16, 16 * i), R("TTc", 16, 16 * t), R("T16c", 16, 16 * t)
+        else:
+            pb, w, o = bank(c), CW * k, 0
+            a, tc, t16 = R("AC", w, L * i + CW * c), R("TT", w, L * t + CW * c), R("T16", w, L * t + CW * c)
         h0 = hot[0]
-        hot[0] += SMH if c is not None else 0.0
-        tt(R(pb, w, 128), R(pb, w), acd, A.min)
-        tt(tcd, R(pb, w, 128), tcd, A.max)
-        if c is not None or e < 3:
-            ts(l, tcd, 2047, A.bitwise_and)
-        if e < 3 or (t == 0 and c is not None):
-            copy(t16, l)
+        hot[0] += CFG["smh"]
+        tt(R(pb, w, 128 + o), R(pb, w, o), a, A.min)
+        tt(tc, R(pb, w, 128 + o), tc, A.max)
+        if e < 3 and c is None:
+            ts(R("Lc", 16), tc, 2047, A.bitwise_and)
+            copy(t16, R("Lc", 16))
+        elif e < 3 and CFG["rep"]:
+            copy(t16, tc)
+        elif e < 3:
+            ts(R("Lr", w, tc[1]), tc, 2047, A.bitwise_and)
+            copy(t16, R("Lr", w, tc[1]))
         hot[0] = h0
 
     def claims(t):
-        P, O, LO = "P%d" % t, "O%d" % t, "LO%d" % t
+        O, LO = "O%d" % t, "LO%d" % t
         ts(R("hl", 16, 32 * t), R("TTc", 16, 16 * t), 7, A.logical_shift_right, 15, A.bitwise_and)
         ts(R("hl", 16, 32 * t + 16), R("TTc", 16, 16 * t), 127, A.bitwise_and)
         copy(R("hlb", 32, 32 * t), R("hl", 32, 32 * t))
         for s in range(16):
             ts(R("OH", 128, 128 * s), R("IB", 128), R("hlb", 1, 32 * t + s), A.is_equal, cyc=0.5)
             ts(R("OL", 128, 128 * s), R("IL", 128), R("hlb", 1, 32 * t + 16 + s), A.is_equal, cyc=0.5)
-        mm(R("pb7", 128), [(R("OH", 128, 128 * s), R("OL", 128, 128 * s)) for s in range(16)], tag="C%d" % t)
-        if t == 0:
-            ts(R("C", 128), R("pb7", 128), 1.0, A.min, 256.0, A.mult)
-        else:
-            ts(R("C", 128, 128), R("pb7", 128), 1.0, A.min)
-        for b in range(4):
-            pb, o = "pb%d" % (b % 2), 512 * b
-
-            def fn(g, T, X, o=o, pb=pb):
-                r = None
-                for h in range(0, 512, 128):
-                    if t == 0:
-                        g.tensor.matmul(T[pb][:, h:h + 128], T["ID"][:], T[P][:, o + h:o + h + 128], True, False)
-                    r = g.tensor.matmul(T[pb][:, h:h + 128], T["E"][:, o + h:o + h + 128], T["C"][:, 128 * t:128 * t + 128], t == 1, True)
-                return r
-            add("t", 512 * CYC * (2 - t), fn, [R("ID", 128), R(P, 512, o), R("E", 512, o), R("C", 128, 128 * t)], [R(pb, 512)], tag="F")
-            if t == 0:
-                relu(R(O, 512, o), R(pb, 512), R("mo", 1), 1.0, tag="O")
+        for h in range(4):
+            add("t", 512 * CYC, lambda g, T, X, h=h: [g.tensor.matmul(T["pb6"][:, 0:128], T["OH"][:, 128 * s:128 * s + 128], T["OL"][:, 128 * s:128 * s + 128],
+                                                                      s == 0, s == 15) for s in range(4 * h, 4 * h + 4)][-1],
+                [R("OH", 512, 512 * h), R("OL", 512, 512 * h), R("pb6", 128)][:2 + (h > 0)], [R("pb6", 128)])
+        ts(R("C", 128, 128 * t), R("pb6", 128), 1.0, A.min, 256.0, A.mult)
+        for b in range(NB):
+            pb, o = "pb%d" % (b % 2), BW * b
+            mms([(R(pb, 128, h), [(R(("ID", "NI")[t], 128), R(P[t][0], 128, o + h)), (R("E", 128, o + h), R("C", 128, 128 * t))]) for h in range(0, BW, 128)])
+            if CFG["of"][t][b] == "S":
+                act(R(O, BW, o), R(pb, BW), R("cst", 1, t), f=AF.Relu)
             else:
-                tt(R(O, 512, o), R(pb, 512), R(P, 512, o), A.mult, tag="O")
-            if (b + 1) * 512 % BW == 0:
-                k = ((b + 1) * 512 - 1) // BW
-                add("g", 1.0, lambda g, T, X, k=k: X["send"](g, T, t, k), [R(O, BW, BW * k)], [("wire%d" % t, k, k + 1)], kind="r", tag="send")
-                for far in (0, 1):
-                    add("x%d%d%d" % (far, t, k), ((XT, XT1)[t] + 3.0 * k) * (FP, 1.0)[far], "%s%d_%d" % (("arr", "far")[far], t, k), [("wire%d" % t, k, k + 1)],
-                        [R(LO, BW, q * W + BW * k) for q in ((0,), (1, 2))[far]], kind="x", tag="arrive")
+                ts(R(O, BW, o), R(pb, BW), (-256.0, -1.0)[t], A.add, 0.0, A.max)
+            add("g", 0.6, lambda g, T, X, b=b: X["send"](g, T, t, b), [R(O, BW, o)], [("wire%d" % t, b, b + 1)], kind="r")
+            for far in ((0, 1) if CFG["route"] == "A" else (1,)):
+                add("x%d%d%d" % (far, t, b), CFG["xt"][t] * (0.6, 1.0)[far] + CFG["xs"] * b, "%s%d_%d" % (("arr", "far")[far], t, b), [("wire%d" % t, b, b + 1)],
+                    [R(LO, BW, q * W + o) for q in (((0,), (1, 2))[far] if CFG["route"] == "A" else (0, 1, 2))], kind="x")
 
     def prices(t):
-        P, N, LO = "P%d" % t, "P%d" % (t + 1), "LO%d" % t
-        for b in range(4):
-            o, pb = 512 * b, "pb%d" % (b % 2)
-            mm(R(pb, 512), [(R("ID", 128), R(P, 512, o)), (R("DG", 128), R(LO, 512, o))], tag="W1", last=False)
-            mm(R(pb, 512), [(R("DG", 128), R(LO, 512, q * W + o)) for q in (1, 2)], tag="W2", first=False)
-            ts(R("N16", 512, o), R(pb, 512), 1025.0 - 63.0 / 128, A.add, 1280.0, A.min)
-            ts(R(N, 512, o), R("N16", 512, o), -1025.0, A.add, cyc=0.5)
-            if t == 0:
-                relu(R("ps1", 512, o), R(N, 512, o), R("scf", 1, 1), -1.0, tag="ps1")
+        LO, I = "LO%d" % t, R(("ID", "NI")[t], 128)
+        for b in range(NB):
+            o, pb, how = BW * b, "pb%d" % (b % 2), CFG["pr"][t][b]
+            new, old = R(("PW1", "P2")[t], BW, o), R(P[t][0], BW, o)
+            s = [(R("DG", 128), R(LO, BW, q * W + o)) for q in range(3)]
+            if how == "V":
+                mm(R(pb, BW), [(I, old)] + s)
+                ts(R("N16", BW, o), R(pb, BW), 1025.0 + 255 * t - 63.0 / 128, A.add, 1280.0, A.min)
+                if t == 0:
+                    ts(new, R("N16", BW, o), -1.0, A.mult, 1280.0, A.add, cyc=0.5)
+                else:
+                    ts(new, R("N16", BW, o), -1025.0, A.add, cyc=0.5)
             else:
-                dma(lambda T, o=o: T.yp[:, o:o + 512], lambda T, o=o: T["P2"][:, o:o + 512], 128, [R("P2", 512, o)], [], q="ys"[b % 2])
+                mm(R(pb, BW), s)
+                act(R("D", BW, o), R(pb, BW), 129.0 - 63.0 / 128)
+                mm(R(pb, BW), [(I, old), (R("ID", 128), R("D", BW, o))])
+                if t == 0:
+                    act(new, R(pb, BW), R("cst", 1, 2), -1.0, AF.Relu)
+                elif how == "M":
+                    ts(new, R(pb, BW), 126.0, A.add, 255.0, A.min)
+                else:
+                    act(R("D", BW, o), R(pb, BW), R("cst", 1, 3), -1.0, AF.Relu)
+                    act(new, R("D", BW, o), 255.0, -1.0)
+            if t == 1:
+                dma(lambda T, o=o: T.yp[:, o:o + BW], lambda T, o=o: T["P2"][:, o:o + BW], 128, [R("P2", BW, o)], [])
+        if t == 0 and CFG["rep"]:
+            for k in (1, 2, 3):
+                dma(lambda T, k=k: T["PW1"][:, k * W:k * W + W], lambda T: T["PW1"][:, 0:W], 512, [P[1]], [R("PW1", W, k * W)])
+
+    def closing(t, c, k):
+        w = CW * k
+        r = lambda b: R(b, w, L * t + CW * c)
+        ts(r("Lr"), r("TT"), 2047, A.bitwise_and)
+        if t == 0:
+            copy(R("A16", w, 4 * L + CW * c), r("Lr"))
+        if (c + k) % 2 == 0:
+            o = L * t + CW * (c + k - 2)
+            hb, ht, yf = R("hb", 128, o), R("ht", 128, o), R("yhf", 128, o)
+            ts(hb, R("TT", 128, o), 1.0 / 2048, A.mult, 129.0 - 2047.0 / 4096, A.add)
+            add("v", vc(128, 0.5), lambda g, T, X: g.vector.transpose(S(T, ht), S(T, hb)), [hb], [ht])
+            scan(R("hm", 128, o), ht)
+            copy(yf, R("Lr", 128, o))
+            if t == 0:
+                act(R("AC", 128, 4 * L + o), yf, con[0])
+            dma(lambda T: T.yh[:, o:o + 128], lambda T: S(T, yf), 64, [yf], [])
 
     def parents(t):
-        for h in range(2):
-            o, k = L * t + 128 * h, 2 * t + h
-            ts(R("hi", 128, o), R("TT", 128, o), 11, A.logical_shift_right, 7, A.bitwise_and)
-            copy(R("hb", 128, o), R("hi", 128, o))
-            mm(R("pb7", 128), [(R("hb", 128, o), R("ID", 128))], tag="hT")
-            add("v", vc(128), lambda g, T, X, k=k: g.vector.tensor_tensor_scan(T["hm"][:, 128 * k:128 * k + 128], T["scd"][:, 0:128], T["pb7"][:, 0:128], 0.0, A.mult, A.max),
-                [R("scd", 128), R("pb7", 128)], [R("hm", 128, 128 * k)])
-            ts(("Y", 144 * k + 15, 144 * k + 128, 16), ("hm", 128 * k + 15, 128 * k + 128, 16), 256.0, A.mult)
-            y, q, p = 144 * k, 16 * t + 8 * h, R("pb7", 8, 256)
-            mm(p, [(R("Y", 128, y + 15 - s), ("ID", s, 128, 16)) for s in range(16)], tag="elist")
-            ts(R("e1", 8, q), p, 0.0, A.is_equal, 1024.0, A.mult)
-            tt(R("e2", 8, q), p, R("LT", 8, 8 * h), A.add)
-            tt(R("e3", 8, q), R("e2", 8, q), R("e1", 8, q), A.add)
-            copy(R("el", 8, q), R("e3", 8, q))
+        o = L * t
+        mms([(("pb7", 256 + 16 * l + h, 256 + 16 * l + 16, 2), [(R("WP", 128, 128 * (2 * h + k)), ("hm", o + 16 * k + 15, o + L, 32)) for k in range(2)])
+             for l in range(5) for h in range(2)])
+        tt(R("pb7", 80, 384), R("pb7", 80, 256), R("LV", 80), A.is_equal)
+        tt(R("mb", 80, 80 * t), R("pb7", 80, 384), R("B", 80, 80 * t), A.mult)
+        mm(R("pb7", 16, 32), [(R("IDh", 128), R("mb", 16, 80 * t + 16 * l)) for l in range(5)])
+        if t == 0:
+            copy(R("lst", 16, 80), R("pb7", 16, 32))
+        copy(R("ph", 16, 16 * t), R("pb7", 16, 32))
+        if t == 0:
+            copy(R("B", 16, 80 + 32), R("lst", 16, 80))
+
+    def parents_out(t):
+        o = L * t
+        mms([(("pb7", 256 + s, 512, 16), [(("IDh", s, 128, 16), R("ph", 16, 16 * t))]) for s in range(16)], 8)
+        act(R("par", L, o), R("pb7", L, 256), p=8)
+        dma(lambda T: T.yv[:, o:o + L], lambda T: T["par"][0:8, o:o + L], 8, [R("par", L, o)], [])
+
+    def next_lots(c, k):
+        w = CW * k
+        r = lambda b, a=0: R(b, w, a + CW * c)
+        u = R(bank(c), w, 256)
+        mm(u, [(R("BDw", 128), ("sm", 16 * CW * c + 15, 16 * (CW * c + w), 16))])
+        copy(r("w1"), u)
+        ts(r("w2"), r("w1"), 1023, A.bitwise_and)
+        ts(u, r("w2"), 2.0, A.mult, 33.0, A.add)
+        tt(r("w3"), u, r("Lr"), A.mult)
+        ts(r("w4"), r("w3"), 2464.0, A.add)
+        ts(r("TT", L), r("w4"), 5, A.logical_shift_right, 2047, A.bitwise_and)
+        copy(r("T16", L), r("TT", L))
+
+    def early(t):
+        hot[0] = HOT
+        for e in range(4):
+            if e:
+                package(4 * t + e)
+            ahead(t, e, None)
+            compare(t, e, None)
+            revert(t, e, None)
+        claims(t)
+
+    def trials(t):
+        sw = CFG["sw"]
+        for e in range(4):
+            for c in range(NCH):
+                hot[0] = CFG["yh"] - CFG["co"][t][c]
+                if c % CFG["yw"] == 0:
+                    ahead(t, e, c, CFG["yw"])
+                hot[0] = -CFG["co"][t][c]
+                compare(t, e, c)
+                if (c + 1) % sw == 0:
+                    revert(t, e, c + 1 - sw, sw)
+        for c in range(0, NCH, sw):
+            hot[0] = CFG["ch"][t]
+            closing(t, c, sw)
+            if t == 0:
+                for j in range(c, c + sw):
+                    n = 16 * CW
+                    act(R("X", n, n * j), P[0], off=R("A16", CW, 4 * L + CW * j))
+                    scan(R("sm", n, n * j), R("X", n, n * j))
+                next_lots(c, sw)
+        hot[0] = 0.0
 
     hot[0] = HOT
-    for e in range(4):
-        trial(0, e, None)
-    claims(0)
-    chain(4)
-    chain(5)
-    for e in range(4):
-        for c in range(NCH):
-            hot[0] = -CO[0][c]
-            trial(0, e, c)
-    hot[0] = 0.0
+    as_list(1, R("bh", L))
+    early(0)
+    trials(0)
+    hot[0] = CFG["ph"]
     prices(0)
-    for c in range(NCH):
-        r = lambda b, k=0: R(b, CW, k + CW * c)
-        n = 16 * CW
-        gath(R("x", n, n * c), R("P0", W), r("T16"), tag="x04%d" % c)
-        add("v", vc(n, 0.5), lambda g, T, X, c=c, n=n: g.vector.tensor_tensor_scan(T["sm"][:, n * c:n * c + n], T["scd"][:, 0:n], T["x"][:, n * c:n * c + n], 0.0, A.mult, A.max),
-            [R("scd", n), R("x", n, n * c)], [R("sm", n, n * c)], tag="scan")
-        mm(R("pb7", CW), [(R("BDw", 128), ("sm", n * c + 15, n * c + n, 16))], tag="u")
-        ts(r("w1"), R("pb7", CW), 2.0, A.mult, 1.0, A.add)
-        ts(r("w2"), r("w1"), 2047, A.bitwise_and)
-        ts(r("Q"), r("w2"), 32.0, A.add)
-        tt(r("w3"), r("Q"), r("Lr"), A.mult)
-        ts(r("w4"), r("w3"), 2464.0, A.add)
-        ts(r("w5"), r("w4"), 5, A.logical_shift_right, 2047, A.bitwise_and)
-        copy(r("T16", L), r("w5"))
-        ts(r("TT", L), r("w5"), float(OFFS), A.add)
-        copy(r("yhf"), r("Lr"))
-        act(r("AC", 4 * L), r("yhf"), con[0])
-    dma(lambda T: T.yh[:, 0:L], lambda T: T["yhf"][:, 0:L], 128, [R("yhf", L)], [])
-    hot[0] = HOT / 2
+    hot[0] = HOT
     dma(lambda T: T["T16c"][:, 16:32], lambda T: T["T16"][1::16, L:2 * L], 8, [R("T16", L, L)], [R("T16c", 16, 16)])
     dma(lambda T: T["TTc"][:, 16:32], lambda T: T["TT"][1::16, L:2 * L], 8, [R("TT", L, L)], [R("TTc", 16, 16)])
-    claim_forms(4, 1)
+    claim_forms(4)
     parents(0)
-    for e in (1, 2, 3):
-        gath(R("Bf", L, L * e), R("Btab", 4 * L, 512 + L * (e - 1)), R("el", 16))
-        lot_forms(4 + e, R("Bf", L, L * e), e)
-    hot[0] = -HOT
-    for j in range(3):
-        gath(R("ctab", L, L * (j + 1)), R("btab", 4 * L, L * j), R("el", 16))
-    dma(lambda T: T.yv[:, 0:L], lambda T: T["ctab"][0::16, L:2 * L], 8, [R("ctab", L, L)], [])
-    hot[0] = HOT
-    for e in range(4):
-        trial(1, e, None)
-    claims(1)
-    for e in range(4):
-        for c in range(NCH):
-            hot[0] = -CO[1][c]
-            trial(1, e, c)
+    early(1)
     hot[0] = 0.0
+    parents_out(0)
+    trials(1)
     prices(1)
-    for c in range(NCH):
-        copy(R("yhf", CW, L + CW * c), R("Lr", CW, L + CW * c))
-        if c % 2:
-            o = L + 128 * (c // 2)
-            dma(lambda T, o=o: T.yh[:, o:o + 128], lambda T, o=o: T["yhf"][:, o:o + 128], 64, [R("yhf", 128, o)], [])
     parents(1)
-    for h in range(2):
-        gath(R("par", 128, 128 * h), R("ctab", 4 * L), R("el", 8, 16 + 8 * h))
-        dma(lambda T, h=h: T.yv[:, L + 128 * h:L + 128 * h + 128], lambda T, h=h: T["par"][0::16, 128 * h:128 * h + 128], 4, [R("par", 128, 128 * h)], [])
+    parents_out(1)
     return ops
 
 
@@ -421,7 +455,7 @@ def depend(ops):
 
 
 def schedule(ops, deps):
-    n = len(ops)
+    n, LAT = len(ops), CFG["lat"]
     succ = [[] for _ in range(n)]
     for i, d in enumerate(deps):
         for j in d:
@@ -429,9 +463,9 @@ def schedule(ops, deps):
     lev = [0.0] * n
     for i in range(n - 1, -1, -1):
         lev[i] = ops[i]["cost"] + max([lev[k] + LAT for k in succ[i]] or [0.0])
-    wgt = [lev[i] + ops[i]["hot"] + JIT * ((i + 1) * MIX % 1009) / 1009.0 for i in range(n)]
+    wgt = [lev[i] + ops[i]["hot"] for i in range(n)]
     left = [len(d) for d in deps]
-    ready = [0.0] * n
+    ready = [o.get("at", 0.0) for o in ops]
     cand, free, order = {}, {}, []
     for i in range(n):
         if not left[i]:
@@ -446,7 +480,7 @@ def schedule(ops, deps):
         if best is None:
             break
         t, q = best
-        i = max((i for i in cand[q] if ready[i] <= t + (DH if ops[i]["hot"] > 100 else DM) + 1e-9), key=lambda i: (wgt[i], -i))
+        i = max((i for i in cand[q] if ready[i] <= t + (CFG["dh"] if ops[i]["hot"] > 100 else CFG["dm"]) + 1e-9), key=lambda i: (wgt[i], -i))
         t = max(t, ready[i])
         cand[q].remove(i)
         o = ops[i]
@@ -454,7 +488,7 @@ def schedule(ops, deps):
         if o["kind"] == "d":
             free["dma"] = max(free.get("dma", 0.0), t) + o["cost"] - 2.0
             fin = free["dma"] + 2.0
-        free[q] = t + (0.1 if o["kind"] == "d" else o["cost"])
+        free[q] = t + (0.06 if o["kind"] == "d" else o["cost"])
         order.append(i)
         for k in succ[i]:
             left[k] -= 1
@@ -465,6 +499,40 @@ def schedule(ops, deps):
     return order
 
 
+def place(seq, before, dur, lag, res, at):
+    start, busy = {}, {}
+    for i in seq:
+        t = max([at[i]] + [start[j] + dur[j] + lag(i, j) for j in before[i]])
+        l = busy.setdefault(res[i], [])
+        for k in range(len(l) + 1):
+            if k == len(l) or t + dur[i] <= l[k][0] + 1e-9:
+                break
+            t = max(t, l[k][1])
+        l.insert(k, (t, t + dur[i]))
+        start[i] = t
+    return start
+
+
+def justify(ops, deps, seq):
+    n = len(ops)
+    succ = [[] for _ in range(n)]
+    for i, d in enumerate(deps):
+        for j in d:
+            succ[j].append(i)
+    dur = [o["cost"] - 2.0 * (o["kind"] == "d") for o in ops]
+    lag = [CFG["lat"] + 2.0 * (o["kind"] == "d") for o in ops]
+    res = [o["q"] for o in ops]
+    best = None
+    for _ in range(CFG["it"]):
+        st = place(seq, deps, dur, lambda i, j: lag[j], res, [o.get("at", 0.0) for o in ops])
+        end = max(st[i] + dur[i] + lag[i] for i in range(n))
+        if best is None or end < best[0]:
+            best = (end, sorted(range(n), key=lambda i: (st[i], i)))
+        rs = place(sorted(range(n), key=lambda i: (-st[i] - dur[i] - lag[i], -i)), succ, dur, lambda i, j: lag[i], res, lag)
+        seq = sorted(range(n), key=lambda i: (-rs[i] - dur[i], i))
+    return best[1]
+
+
 PLAN = {}
 
 
@@ -472,54 +540,52 @@ def plan():
     if "ops" not in PLAN:
         PLAN["ops"] = build()
         PLAN["deps"] = depend(PLAN["ops"])
-        PLAN["order"] = schedule(PLAN["ops"], PLAN["deps"])
+        PLAN["order"] = justify(PLAN["ops"], PLAN["deps"], schedule(PLAN["ops"], PLAN["deps"]))
     return PLAN["ops"], PLAN["deps"], PLAN["order"]
 
 
-def routes(cores, topo):
-    out = []
-    for c in cores:
-        peers = [d for d in cores if d != c and topo.same_plane(c, d)]
-        far = [d for d in cores if d != c and not topo.same_plane(c, d)]
-        mine = sorted(peers + [c]).index(c)
-        hop = {}
-        for k, d in enumerate(far):
-            own = (mine + k) % 2 == 0
-            hop[d] = [h for h in topo.cores_of(c) if h not in cores and topo.may_write(h, d) and (topo.die(h) == topo.die(c)) == own][0]
-        out.append((peers, hop))
-    return out
+def helpers(c, cores, topo):
+    hs = [h for h in topo.cores_of(c) if h not in cores and all(topo.may_write(h, d) for d in cores if d != c)]
+    far = [h for h in hs if topo.die(h) != topo.die(c)]
+    near = [h for h in hs if topo.die(h) == topo.die(c)]
+    return [h for pair in zip(far, near) for h in pair]
 
 
-def slot(cores, src, dst, topo):
-    rest = [c for c in cores if c != dst]
-    return sorted(rest, key=lambda c: (not topo.same_plane(c, dst), c)).index(src)
+def others(cores, dst, topo):
+    return sorted((c for c in cores if c != dst), key=lambda c: (not topo.same_plane(c, dst), c))
 
 
 def bits(es):
     return sum(1 << e for e in es)
 
 
-def onchip(c, peers, topo, h):
-    off = topo.engines(c, peers[0])
+def into(c, h, cores, topo):
+    if CFG["route"] == "B":
+        return topo.engines(c, h)
+    off = topo.engines(c, others(cores, c, topo)[0])
     return [e for e in topo.engines(c, h) if e not in off]
+
+
+def dst_id(d, src, topo):
+    return DstId(rid=topo.addr(d, src)[0], pnc=topo.addr(d, src)[1])
 
 
 def hand_on(g, core, T, topo):
     cores = list(T.cores)
-    for c, (peers, hop) in zip(cores, routes(cores, topo)):
-        for d, h in hop.items():
-            if h != core:
-                continue
-            es, into = topo.engines(core, d), onchip(c, peers, topo, h)
-            rid, pid = topo.addr(d, core)
-            k = slot(cores, c, d, topo)
-            for t in range(2):
-                for b in range(NB):
-                    g.wait_ge(T.sem["hin%d_%d" % (t, b)], len(into))
-                    o = k * W + BW * b
-                    g.remote_dma(T["LO%d" % t][:, o:o + BW], T["HB"][:, t * W + BW * b:t * W + BW * b + BW],
-                                 T.sem["far%d_%d" % (t, b)], T.sem["hs"], pid, rid, bits(es))
-            g.wait_ge(T.sem["hs"], 2 * NB * len(es))
+    for c in cores:
+        hs = helpers(c, cores, topo)
+        if core not in hs:
+            continue
+        b = hs.index(core)
+        to = others(cores, c, topo)[CFG["route"] == "A":]
+        es = topo.engines(core, to[0])
+        for t in range(2):
+            g.wait_ge(T.sem["hin%d" % t], len(into(c, core, cores, topo)))
+            at = [others(cores, d, topo).index(c) * W + BW * b for d in to]
+            g.remote_dma_fused([RemoteDMATransfer(dst_ids=[dst_id(d, core, topo) for d in to], dma_engine_mask=bits(es), remote_sem=T.sem["far%d_%d" % (t, b)],
+                                                  srcs=[T["HB"][:, t * BW:t * BW + BW]], dsts=[T["LO%d" % t][:, o:o + BW] for o in at])],
+                               local_sem=T.sem["hs"])
+        g.wait_ge(T.sem["hs"], 2 * len(es))
 
 
 def rank_program(g, core, T, topo):
@@ -527,27 +593,25 @@ def rank_program(g, core, T, topo):
         hand_on(g, core, T, topo)
         return
     cores = list(T.cores)
-    rt = routes(cores, topo)
-    peers, hop = rt[T.rank_of(core)]
+    hs, rest = helpers(core, cores, topo), others(cores, core, topo)
     ops, deps, order = plan()
     eng = {"v": g.vector, "s": g.scalar, "t": g.tensor, "y": g.sync, "g": g}
     sent = [0]
 
     def send(g_, T_, t, b):
-        p, hs = peers[0], list(hop.values())
-        src = T["O%d" % t][:, BW * b:BW * b + BW]
-        dst = lambda h: DstId(rid=topo.addr(h, core)[0], pnc=topo.addr(h, core)[1])
-        k = slot(cores, core, p, topo) * W + BW * b
-        e0, e1 = topo.engines(core, p), onchip(core, peers, topo, hs[0])
-        g.remote_dma_fused([
-            RemoteDMATransfer(dst_ids=[dst(p)], dma_engine_mask=bits(e0), remote_sem=T.sem["arr%d_%d" % (t, b)],
-                              srcs=[src], dsts=[T["LO%d" % t][:, k:k + BW]]),
-            RemoteDMATransfer(dst_ids=[dst(h) for h in hs], dma_engine_mask=bits(e1), remote_sem=T.sem["hin%d_%d" % (t, b)],
-                              srcs=[src], dsts=[T["HB"][:, t * W + BW * b:t * W + BW * b + BW] for h in hs])],
-            local_sem=T.sem["snd"])
-        sent[0] += len(e0) + len(e1)
+        src, es = T["O%d" % t][:, BW * b:BW * b + BW], into(core, hs[b], cores, topo)
+        tr = [RemoteDMATransfer(dst_ids=[dst_id(hs[b], core, topo)], dma_engine_mask=bits(es), remote_sem=T.sem["hin%d" % t],
+                                srcs=[src], dsts=[T["HB"][:, t * BW:t * BW + BW]])]
+        sent[0] += len(es)
+        if CFG["route"] == "A":
+            e0 = topo.engines(core, rest[0])
+            tr.append(RemoteDMATransfer(dst_ids=[dst_id(rest[0], core, topo)], dma_engine_mask=bits(e0), remote_sem=T.sem["arr%d_%d" % (t, b)],
+                                        srcs=[src], dsts=[T["LO%d" % t][:, BW * b:BW * b + BW]]))
+            sent[0] += len(e0)
+        g.remote_dma_fused(tr, local_sem=T.sem["snd"])
 
-    arrive = {"a": len(topo.engines(peers[0], core)), "f": sum(len(topo.engines(h[core], core)) for _, h in rt if core in h)}
+    arrive = {"a": len(topo.engines(rest[0], core)),
+              "f": sum(len(topo.engines(helpers(c, cores, topo)[0], core)) for c in rest[CFG["route"] == "A":])}
     X = {"send": send}
     cnt = {"v": 0, "s": 0, "t": 0, "g": 0}
     clock = {q: {} for q in eng}

@@ -1,40 +1,44 @@
 from concourse.bass import DstId, RemoteDMATransfer
 from concourse.mybir import AluOpType, ActivationFunctionType
 
-BIG = 16384
+BIG, WORLD = 16384, 256
 W, L, H0 = 2048, 256, 768
 NCH, CW = 4, 64
 NB = 4
 BW = W // NB
 BF, F32, I32, U16, F16 = "bfloat16", "float32", "int32", "uint16", "float16"
-CFG = {"cyc": 0.83e-3 * 1.15, "g": 1.55, "lat": 0.1, "hot": 500.0, "it": 3, "xt": (13.0, 13.0), "xs": 1.5, "rep": False, "dh": 0.1, "dm": 0.05, "pr": ("SVSV", "VMVM"), "of": ("SSSS", "SSSS"),
-       "av": "", "route": "B", "yw": 1, "sw": 1, "split": (2, 2, 1, 1, 2, 2, 1, 1), "ch": (20.0, 0.0), "ph": 0.0, "smh": 2.0, "yh": 0.0, "co": ((0, 0, 0, 0), (0, 0, 0, 0))}
+CFG = {"cyc": 0.88e-3, "g": 1.5, "pe": 0.5, "lat": 0.24, "pd": (40.0, 90.0), "xt": (18.0, 14.0), "xs": 1.5, "rep": (2, 3, 6, 7), "rg": (3, 2), "pr": ("SSSV", "SSVV"), "of": ("SSSS", "SSSS"),
+       "av": "1", "route": "C", "np": (8, 4, 1, 2, 8, 4, 1, 1), "ns": 4, "pp": 320, "it": 2, "t0": (6.0, 43.0), "sl": (1.8, 1.8), "sd": (16.0, 54.0), "end": 88.0, "xv": (5, 7), "pre": True, "nd": 10.0, "off": ((), ()), "th": False, "sg": (), "sw": 1, "tp": False, "cs": (), "ap": (), "td": (1, 2, 3), "one": True,
+       "ord": ((0, 1, 2, 3, 10, 11, 20, 21, 12, 13, 30, 31, 22, 23, 32, 33), (0, 1, 10, 2, 11, 20, 3, 12, 21, 30, 13, 22, 31, 23, 32, 33))}
 
 SCRATCH = {
     "PW0": ("sbuf", [128, 4 * W], BF), "PW1": ("sbuf", [128, 4 * W], BF), "P2": ("sbuf", [128, W], BF),
     "pk": ("sbuf", [128, H0], I32), "pv": ("sbuf", [128, H0], I32), "PK": ("sbuf", [128, H0], F32), "ac": ("sbuf", [128, 16], I32),
     "ic": ("sbuf", [128, 1], I32), "wc": ("sbuf", [128, 1], I32), "sc": ("sbuf", [128, 2], I32),
-    "icf": ("sbuf", [128, 1], F32), "wcf": ("sbuf", [128, 1], F32), "scf": ("sbuf", [128, 2], F32), "cst": ("sbuf", [128, 4], F32),
-    "ip": ("sbuf", [128, 1], I32), "im": ("sbuf", [128, 128], I32), "on": ("sbuf", [128, W], BF),
+    "icf": ("sbuf", [128, 1], F32), "wcf": ("sbuf", [128, 1], F32), "scf": ("sbuf", [128, 2], F32), "cst": ("sbuf", [128, 8], F32), "Z2": ("sbuf", [128, 144], BF),
+    "sg": ("sbuf", [128, L], BF), "KI": ("sbuf", [128, 128], BF), "NK": ("sbuf", [128, 128], BF), "I32": ("sbuf", [128, 128], F32),
+    "ip": ("sbuf", [128, 1], I32), "im": ("sbuf", [128, 128], I32), "on": ("sbuf", [128, 1024], BF),
     "pg": ("sbuf", [128, 1], I32), "pgf": ("sbuf", [128, 1], F32), "pg16": ("sbuf", [128, 1], F32), "ipf": ("sbuf", [128, 1], F32),
-    "mg": ("sbuf", [128, 128], I32), "i16": ("sbuf", [128, 16], F32), "LV": ("sbuf", [128, 80], F32),
+    "mg": ("sbuf", [128, 128], I32), "pl": ("sbuf", [128, 1], F32), "Z1": ("sbuf", [128, 144], BF), "th": ("sbuf", [128, L], F16),
+    "Z0": ("sbuf", [128, 144], BF), "ah": ("sbuf", [128, 2 * L], F16), "LV": ("sbuf", [128, 80], F32),
+    "q1": ("sbuf", [128, 6], F32), "ql": ("sbuf", [128, 6], U16), "hq": ("sbuf", [128, 160], BF),
     "Z": ("sbuf", [128, 144], BF), "Zh": ("sbuf", [128, 144], F16), "NG": ("sbuf", [128, 128], BF),
-    "BDw": ("sbuf", [128, 128], BF), "IB": ("sbuf", [128, 128], BF), "IL": ("sbuf", [128, 128], BF),
-    "ID": ("sbuf", [128, 128], BF), "IDh": ("sbuf", [128, 128], F16), "NI": ("sbuf", [128, 128], BF), "DG": ("sbuf", [128, 128], BF),
+    "BDw": ("sbuf", [128, 128], BF), "IB": ("sbuf", [128, 128], BF), "IL": ("sbuf", [128, 130], BF),
+    "ID": ("sbuf", [128, 128], BF), "M2": ("sbuf", [128, 128], BF), "TF": ("sbuf", [128, 2 * L], F32), "NI": ("sbuf", [128, 128], BF), "DG": ("sbuf", [128, 128], BF),
     "E": ("sbuf", [128, W], BF), "WP": ("sbuf", [128, 512], BF), "scd": ("sbuf", [128, 1024], BF),
     "bh": ("sbuf", [128, 6 * L], F16), "lst": ("sbuf", [128, 8 * 16], U16), "B": ("sbuf", [128, 160], F32),
     "A16": ("sbuf", [128, 8 * L], U16), "AC": ("sbuf", [128, 8 * L], F32),
     "A16c": ("sbuf", [128, 8 * 16], U16), "ACc": ("sbuf", [128, 8 * 16], F32),
     "T16": ("sbuf", [128, 2 * L], U16), "TT": ("sbuf", [128, 2 * L], I32), "Lr": ("sbuf", [128, 2 * L], I32),
     "T16c": ("sbuf", [128, 32], U16), "TTc": ("sbuf", [128, 32], I32), "Lc": ("sbuf", [128, 16], I32),
-    "Y": ("sbuf", [128, 8 * 4096], BF), "Yc": ("sbuf", [128, 8 * L], BF), "mk": ("sbuf", [128, 4096 + 256], BF),
+    "Y": ("sbuf", [128, 6 * 4096], BF), "Yc": ("sbuf", [128, 8 * L], BF), "mk": ("sbuf", [128, 4096 + 256], BF),
     "X": ("sbuf", [128, 4096], BF), "sm": ("sbuf", [128, 4096], BF),
     "yhf": ("sbuf", [128, 2 * L], F32), "w1": ("sbuf", [128, L], I32), "w2": ("sbuf", [128, L], I32), "w3": ("sbuf", [128, L], I32),
     "w4": ("sbuf", [128, L], I32),
     "hb": ("sbuf", [128, 2 * L], BF), "ht": ("sbuf", [128, 2 * L], BF), "hm": ("sbuf", [128, 2 * L], BF),
     "mb": ("sbuf", [128, 160], F16), "ph": ("sbuf", [128, 32], F16), "par": ("sbuf", [128, 2 * L], F32),
     "hl": ("sbuf", [128, 64], I32), "hlb": ("sbuf", [128, 64], F32),
-    "OH": ("sbuf", [128, 16 * 128], BF), "OL": ("sbuf", [128, 16 * 128], BF), "C": ("sbuf", [128, 256], BF),
+    "OH": ("sbuf", [128, 16 * 128], BF), "OL": ("sbuf", [128, 16 * 130], BF), "C": ("sbuf", [128, 256], BF), "Cs": ("sbuf", [128, 128], F32),
     "O0": ("sbuf", [128, W], BF), "O1": ("sbuf", [128, W], BF), "N16": ("sbuf", [128, W], F16), "D": ("sbuf", [128, W], BF),
     "LO0": ("sbuf", [128, 3 * W], BF), "LO1": ("sbuf", [128, 3 * W], BF),
     "HB": ("sbuf", [128, 2 * BW], BF),
@@ -51,20 +55,18 @@ AF = ActivationFunctionType
 
 def build():
     ops = []
-    hot = [0.0]
-    CYC, HOT = CFG["cyc"], CFG["hot"]
+    CYC = CFG["cyc"]
 
-    def add(q, cost, fn, rd, wr, kind="c", tag=""):
-        ops.append({"q": q, "cost": cost, "fn": fn, "rd": rd, "wr": wr, "kind": kind, "tag": tag, "hot": hot[0]})
+    def add(q, cost, fn, rd, wr, kind="c", **more):
+        ops.append(dict(q=q, cost=cost, fn=fn, rd=rd, wr=wr, kind=kind, **more))
 
     def vc(n, cyc=1.0):
         return max(64, n * cyc) * CYC + 0.01
 
-    def ga(n):
-        return n * CFG["g"] * CYC + 0.06
-
     def S(T, r, p=128):
         return T[r[0]][0:p, r[1]:r[2]] if len(r) == 3 else T[r[0]][0:p, r[1]:r[2]:r[3]]
+
+    R = lambda b, n, a=0: (b, a, a + n)
 
     def n_of(r):
         return len(range(*r[1:]))
@@ -92,32 +94,50 @@ def build():
         add("v", vc(n, 0.5), lambda g, T, X: g.vector.tensor_tensor_scan(S(T, out), T["scd"][:, 0:n], S(T, in_), 0.0, A.mult, A.max),
             [("scd", 0, n), in_], [out])
 
-    def vgath(out, win, off):
-        add("v", ga(n_of(out)), lambda g, T, X: g.vector.tensor_copy(S(T, out), S(T, win).indirect(S(T, off))), [win, off], [out])
+    def act(out, in_, bias=0.0, scale=1.0, f=AF.Copy, p=128):
+        add("s", max(64, n_of(out)) * CYC + 0.03,
+            lambda g, T, X: g.scalar.activation(S(T, out, p), S(T, in_, p), f, bias=S(T, bias) if isinstance(bias, tuple) else bias, scale=scale),
+            [r for r in (in_, bias) if isinstance(r, tuple)], [out])
 
-    def act(out, in_, bias=0.0, scale=1.0, f=AF.Copy, off=None, p=128):
-        def fn(g, T, X):
-            i = S(T, in_).indirect(S(T, off)) if off else S(T, in_, p)
-            return g.scalar.activation(S(T, out, p), i, f, bias=S(T, bias) if isinstance(bias, tuple) else bias, scale=scale)
-        add("s", ga(n_of(out)) if off else max(64, n_of(out)) * CYC + 0.03, fn, [r for r in (in_, bias, off) if isinstance(r, tuple)], [out])
+    def gather(q, out, win, off, call, more=(), other=None, parts=1, due=None):
+        w, key = n_of(off) // parts, len(ops)
+
+        def emit(g, T, a, b):
+            cut = lambda r, k: T[r[0]][:, r[1] + k * w * a:r[1] + k * w * b]
+            return call(g, T, cut(out, 16), S(T, win).indirect(cut(off, 1)), other and cut(other, 16))
+        for j in range(parts):
+            cut = lambda r, k: R(r[0], k * w, r[1] + k * w * j)
+            add(q, 16 * w * CFG["g"] * CYC + (0.06 if parts == 1 else 0.03), emit, [win, cut(off, 1)] + list(more) + ([cut(other, 16)] if other else []),
+                [cut(out, 16)], part=(key, j))
+            if due:
+                ops[-1]["due"] = due(j + 1.0 - parts)
+
+    def vgath(out, win, off, **k):
+        gather("v", out, win, off, lambda g, T, o, i, _: g.vector.tensor_copy(o, i), **k)
+
+    def sgath(out, win, off, bias=0.0, **k):
+        col = isinstance(bias, tuple)
+        gather("s", out, win, off, lambda g, T, o, i, _: g.scalar.activation(o, i, AF.Identity if col else AF.Copy, bias=S(T, bias) if col else bias),
+               [bias] if col else [], **k)
+
+    def matmuls(l, m=128):
+        piece, cost = [], 0
+        for k, x in enumerate(l):
+            piece.append(x)
+            cost += max(min(64, m), n_of(x[2])) * (4 if x[1][0] == "I32" else 1)
+            if cost >= CFG["pp"] or k == len(l) - 1:
+                add("t", cost * CYC * CFG["pe"], lambda g, T, X, piece=piece: [g.tensor.matmul(S(T, o, m), S(T, a), S(T, b), s, e) for o, a, b, s, e in piece][-1],
+                    [r for x in piece for r in x[1:3]], [x[0] for x in piece])
+                piece, cost = [], 0
 
     def mms(groups, m=128):
-        def fn(g, T, X):
-            r = None
-            for out, pairs in groups:
-                for i, (l, h) in enumerate(pairs):
-                    r = g.tensor.matmul(S(T, out, m), S(T, l), S(T, h), i == 0, i == len(pairs) - 1)
-            return r
-        add("t", sum(max(min(64, m), n_of(h)) for _, ps in groups for l, h in ps) * CYC + 0.03, fn,
-            [p for _, ps in groups for lh in ps for p in lh], [o for o, _ in groups])
+        matmuls([(o, a, b, i == 0, i == len(ps) - 1) for o, ps in groups for i, (a, b) in enumerate(ps)], m)
 
     def mm(out, pairs):
         mms([(out, pairs)])
 
-    def dma(out, in_, kb, rd, wr, q="y"):
-        def fn(g, T, X):
-            return (g.sync if q == "y" else g.scalar).dma_start(out(T), in_(T))
-        add(q, 2.0 + kb / 200.0, fn, rd, wr, kind="d")
+    def dma(out, in_, kb, rd, wr, **more):
+        add("y", 2.0 + kb / 200.0, lambda g, T, X: g.sync.dma_start(out(T), in_(T)), rd, wr, kind="d", **more)
 
     def iota(out, pattern, base, cm, small=False):
         def fn(g, T, X):
@@ -132,81 +152,114 @@ def build():
     def mset(out, v, cyc=0.5):
         add("v", vc(n_of(out), cyc), lambda g, T, X: g.vector.memset(S(T, out), v), [], [out])
 
-    R = lambda b, n, a=0: (b, a, a + n)
     con = [float(2048 * (e + 1)) for e in range(4)]
     P = [R("PW0", W), R("PW1", W)]
 
-    hot[0] = 9000.0
     mset(R("pv", H0), 0, 1.0)
-    loads = [("TTc", 0, 16, lambda T: T.lots[0::16, :], 8), ("ac", 0, 16, lambda T: T.packs[0::16, H0 - L:H0], 8), ("sc", 0, 2, lambda T: T.slack[:], 1),
+    ops[-1]["rank"] = -100.0
+    ops[-1]["wr"].append(R("gate", 1))
+    loads = [("TTc", 0, 16, lambda T: T.lots[0::16, :], 30), ("ac", 0, 16, lambda T: T.packs[0::16, H0 - L:H0], 30), ("sc", 0, 2, lambda T: T.slack[:], 30),
              ("PW0", 0, W, lambda T: T.price[:], 512), ("pv", 0, H0, lambda T: T.prev[:], 24), ("pk", H0 - L, L, lambda T: T.packs[:, H0 - L:H0], 128),
              ("TT", 0, L, lambda T: T.lots[:], 128), ("pk", 0, H0 - L, lambda T: T.packs[:, 0:H0 - L], 256),
-             ("wc", 0, 1, lambda T: T.wt[:], 1), ("ic", 0, 1, lambda T: T.inc[:], 1)]
+             ("wc", 0, 1, lambda T: T.wt[:], 30), ("ic", 0, 1, lambda T: T.inc[:], 30)]
     for k, (b, a, n, src, kb) in enumerate(loads):
-        dma(lambda T, b=b, a=a, n=n: T[b][0::16 if b == "pv" else 1, a:a + n], src, kb, [], [R(b, n, a)])
-        ops[-1]["at"] = 0.15 * k + (k > 3)
-    for k in (1, 2, 3) if CFG["rep"] else ():
-        dma(lambda T, k=k: T["PW0"][:, k * W:k * W + W], lambda T: T.price[:], 512, [R("pk", H0)], [R("PW0", W, k * W)])
-    hot[0] = HOT
+        dma(lambda T, b=b, a=a, n=n: T[b][0::16 if b == "pv" else 1, a:a + n], src, kb, [R("gate", 1)] * (k > 4), [R(b, n, a)], rank=k - 99.0)
     iota(R("ip", 1), [[1, 1]], 0, 1)
     iota(R("im", 128), [[1, 128]], 0, 0)
     iota(R("on", 128), [[0, 128]], 1, 0, True)
-    hot[0] = 0.0
-    iota(R("IL", 128), [[1, 128]], 0, 0, True)
-    iota(R("on", W - 128, 128), [[0, W - 128]], 1, 0, True)
-    select(R("ID", 128), R("on", 128), [[-1, 128]], A.is_equal, 1)
-    select(R("E", W), R("on", W), [[-1, 16], [-16, 8], [0, 16]], A.is_equal, 1)
-    select(R("scd", 1024), R("on", 1024), [[0, 64], [1, 16]], A.not_equal, 0)
-    iota(R("i16", 16), [[16, 16]], H0 - L, 1, True)
+    iota(R("mg", 128), [[1, 8], [0, 16]], 0, 0)
+    iota(R("IL", 130), [[1, 130]], 0, 0, True)
+    mset(R("E", W), 256.0)
+
+    def diagonal(b, v):
+        if v != 1:
+            iota(R(b, 128), [[0, 128]], v, 0, True)
+        select(R(b, 128), R("on" if v == 1 else b, 128), [[-1, 128]], A.is_equal, 1)
+    if CFG["ap"]:
+        iota(R("Z0", 144), [[0, 144]], 1, 0, True)
+        select(R("Z0", 144), R("Z0", 144), [[-16, 9], [1000, 16]], A.is_equal, 1, -15000)
+    if CFG["sg"]:
+        iota(R("NK", 128), [[0, 128]], -BIG // 128, 0, True)
+        diagonal("KI", BIG)
+    iota(R("I32", 128), [[0, 128]], 1, 0, True)
+    select(R("I32", 128), R("I32", 128), [[-1, 128]], A.is_equal, 1)
+    diagonal("ID", 1)
+    select(R("E", W), R("E", W), [[-1, 16], [-16, 8], [0, 16]], A.is_equal, 1)
+    iota(R("on", 384, 128), [[0, 384]], 1, 0, True)
+    select(R("scd", 512), R("on", 512), [[0, 32], [1, 16]], A.not_equal, 0)
+    if CFG["cs"]:
+        diagonal("M2", -2048)
+    diagonal("NI", -1)
     iota(R("LV", 80), [[1, 5], [0, 16]], 129, 0, True)
+    if CFG["tp"] or CFG["ap"]:
+        select(R("Z1", 144), R("on", 144), [[-16, 9], [1000, 16]], A.is_equal, 1, -15001)
     for h in range(2):
         for k in range(2):
             select(R("WP", 128, 128 * (2 * h + k)), R("on", 128), [[-32, 4], [1000, 2], [-1, 16]], A.is_equal, 1, -16 * h - 1000 * k)
-    hot[0] = 5 * HOT
+    for k, o in enumerate(ops):
+        if o["q"] == "g":
+            o["rank"] = k / 100.0 - 80.0
     mset(R("Z", 144), 0.0)
     mset(R("NG", 128), -BIG / 16.0)
-    for k, v in enumerate((-256.0, -1.0, 384.0, 129.0)):
+    for k, v in enumerate((-256.0, -1.0, 384.0, 129.0, -0.5)):
         mset(R("cst", 1, k), v)
     ts(R("pg", 1), R("ip", 1), 4, A.logical_shift_right)
     copy(R("ipf", 1), R("ip", 1))
     copy(R("pgf", 1), R("pg", 1))
-    ts(R("mg", 128), R("im", 128), 4, A.logical_shift_right)
     ts(("Z", 15, 128, 16), R("im", 8), R("pgf", 1), A.is_equal, float(BIG), A.mult)
     ts(R("Zh", 144), R("Z", 144), 1.0 / BIG, A.mult, cyc=0.5)
+    if CFG["off"] != ((), ()):
+        ts(R("Z2", 144), R("Z", 144), 0.5, A.mult, cyc=0.5)
     ts(R("pg16", 1), R("pg", 1), 16.0, A.mult)
-    ts(R("IB", 128), R("im", 128), R("pg16", 1), A.subtract)
-    ts(R("NI", 128), R("im", 128), R("ipf", 1), A.is_equal, -1.0, A.mult)
-    ts(R("IDh", 128), R("im", 128), R("ipf", 1), A.is_equal)
-    hot[0] = 0.0
-    ts(R("B", 16, 16), R("i16", 16), R("pg16", 1), A.subtract)
-    ts(R("B", 16, 96), R("i16", 16), R("pg16", 1), A.subtract, float(L), A.add)
+    ts(R("IB", 128), R("im", 128), R("pg16", 1), A.subtract, 0.5 * CFG["th"], A.add)
+    ts(R("pl", 1), R("ipf", 1), R("pg16", 1), A.subtract, float(H0 - L), A.add)
+    ts(R("B", 16, 16), R("im", 16), 16.0, A.mult, R("pl", 1), A.add)
+    ts(R("B", 16, 96), R("B", 16, 16), float(L), A.add)
+    ts(R("q1", 6), R("on", 6), R("pl", 1), A.mult, float(L - H0), A.add)
+    ts(R("ql", 6), R("q1", 6), 16.0, A.mult, 15.0, A.add)
     ts(R("icf", 1), R("ic", 1), 1.0 / 64, A.mult)
     ts(R("DG", 128), R("im", 128), R("ipf", 1), A.is_equal, R("icf", 1), A.mult)
     copy(R("wcf", 1), R("wc", 1))
     ts(R("BDw", 128), R("mg", 128), R("pgf", 1), A.is_equal, R("wcf", 1), A.mult)
     ts(R("scf", 1, 1), R("sc", 1, 1), -1.0, A.mult)
-    hot[0] = 4 * HOT
     copy(R("scf", 1), R("sc", 1))
     copy(R("A16c", 16), R("ac", 16))
     copy(R("T16c", 16), R("TTc", 16))
     ts(R("ACc", 16), R("ac", 16), con[0], A.add)
-    hot[0] = 3 * HOT
     for h in range(2):
         copy(R("A16", 128, 128 * h), R("pk", 128, H0 - L + 128 * h))
         copy(R("T16", 128, 128 * h), R("TT", 128, 128 * h))
-    hot[0] = 2 * HOT
     copy(R("bh", L), R("pv", L, H0 - L))
     copy(R("PK", L, H0 - L), R("pk", L, H0 - L))
     copy(R("PK", H0 - L), R("pk", H0 - L))
-    hot[0] = 0.0
     act(R("AC", L), R("PK", L, H0 - L), con[0])
 
-    bank = lambda c: "pb%d" % (2 + c - c % CFG["sw"])
+    SW = CFG["sw"]
+    bank = lambda c: "pb%d" % (2 + c // SW)
+    wide = lambda b: "pb%d" % ((0, 1, 4, 5)[b] if SW == 2 else b % 2)
 
     def claim_forms(i):
         t = i // 4
-        dma(lambda T: T["A16c"][:, 16 * i:16 * i + 16], lambda T: T["A16"][t::16, L * i:L * i + L], 8, [R("A16", L, L * i)], [R("A16c", 16, 16 * i)])
-        dma(lambda T: T["ACc"][:, 16 * i:16 * i + 16], lambda T: T["AC"][t::16, L * i:L * i + L], 8, [R("AC", L, L * i)], [R("ACc", 16, 16 * i)])
+        if i in CFG["ap"]:
+            h = R("ah", L, L * (i % 2))
+            if i == 4:
+                copy(h, R("A16", L, L * i), 0.5)
+            else:
+                ts(h, R("AC", L, L * i), -con[i % 4], A.add)
+            mm(R("pb7", 16, 64), [(R("Z%d" % t, 128, 15 - s), R("ah", 16, h[1] + 16 * s)) for s in range(16)])
+            copy(R("A16c", 16, 16 * i), R("pb7", 16, 64))
+            ts(R("ACc", 16, 16 * i), R("pb7", 16, 64), con[i % 4], A.add)
+            return
+        if CFG["one"]:
+            if i == 4:
+                dma(lambda T: T["A16c"][:, 64:80], lambda T: T["A16"][1::16, 4 * L:5 * L], 30, [R("A16", L, 4 * L)], [R("A16c", 16, 64)])
+                ts(R("ACc", 16, 64), R("A16c", 16, 64), con[0], A.add)
+            else:
+                dma(lambda T: T["ACc"][:, 16 * i:16 * i + 16], lambda T: T["AC"][t::16, L * i:L * i + L], 30, [R("AC", L, L * i)], [R("ACc", 16, 16 * i)])
+                ts(R("A16c", 16, 16 * i), R("ACc", 16, 16 * i), -con[i % 4], A.add)
+            return
+        dma(lambda T: T["A16c"][:, 16 * i:16 * i + 16], lambda T: T["A16"][t::16, L * i:L * i + L], 30, [R("A16", L, L * i)], [R("A16c", 16, 16 * i)])
+        dma(lambda T: T["ACc"][:, 16 * i:16 * i + 16], lambda T: T["AC"][t::16, L * i:L * i + L], 30, [R("AC", L, L * i)], [R("ACc", 16, 16 * i)])
 
     def package(i):
         t, e = i // 4, i % 4
@@ -219,7 +272,7 @@ def build():
             vgath(R("A16", L, L * i), R("pk", H0), ls)
             ts(R("AC", L, L * i), R("A16", L, L * i), con[e], A.add)
         else:
-            act(R("AC", L, L * i), R("PK", H0), con[e], off=ls)
+            sgath(R("AC", L, L * i), R("PK", H0), ls, con[e])
             ts(R("A16", L, L * i), R("AC", L, L * i), -con[e], A.add)
         claim_forms(i)
 
@@ -227,77 +280,91 @@ def build():
         t, e = i // 4, i % 4
         mm(R("pb7", 16), [(R("Zh", 128, 15 - s), (row[0], row[1] + s, row[2], 16)) for s in range(16)])
         copy(R("lst", 16, 16 * i), R("pb7", 16))
-        h0 = hot[0]
-        hot[0] = 0.0
         for k in ((e + 1,), (0, 4))[e == 3]:
             copy(R("B", 16, 80 * t + 16 * k), R("lst", 16, 16 * i))
-        hot[0] = h0
 
-    def ahead(t, e, c, k=1):
+    def trial(t, e, c):
         i = 4 * t + e
         if c is None:
-            act(R("Yc", L, L * i), P[t], R("scf", 1, t), f=AF.Identity, off=R("A16c", 16, 16 * i))
+            w, pb, win, due, ns, nv = 16, "pb6", P[t], None, 1, 1
+            a16, a, t16, tc, l = R("A16c", w, w * i), R("ACc", w, w * i), R("T16c", w, w * t), R("TTc", w, w * t), R("Lc", w)
+            y, m = R("Yc", L, L * i), R("mk", L, 4096)
         else:
-            act(R("Y", 16 * CW * k, 4096 * i + 16 * CW * c), P[t], R("scf", 1, t), f=AF.Identity, off=R("A16", CW * k, L * i + CW * c))
-
-    def compare(t, e, c):
-        i = 4 * t + e
+            w, pb, win, ns, nv = CW, bank(c), R("PW%d" % t, W * (e + 1) if i in CFG["rep"] else W), CFG["ns"], CFG["np"][i]
+            a16, a, t16, tc, l = [R(b, w, L * k + w * c) for b, k in (("A16", i), ("AC", i), ("T16", t), ("TT", t), ("Lr", t))]
+            y, m = R("Y", 16 * w, 4096 * (i % 6) + 16 * w * c), R("mk", 16 * w, 16 * w * c)
+            due = lambda j: CFG["t0"][t] + CFG["sl"][t] * (CFG["ord"][t].index(10 * e + c) + 1 + j / nv)
         if c is None:
-            w, mo, y, win, off, out = 16, 4096, R("Yc", L, L * i), P[t], R("T16c", 16, 16 * t), R("pb6", 16)
+            sgath(y, P[t], a16, R("scf", 1, t))
+        elif c == 0:
+            sgath(R("Y", 4096, y[1]), P[t], R("A16", L, L * i), R("scf", 1, t), parts=NCH * ns)
+        if c is not None and 10 * e + c in CFG["off"][t]:
+            x = R("X", 16 * w, 16 * w * c)
+            sgath(x, win, t16, parts=ns)
+            for h in (0, 512):
+                mm(R(pb, 512), [(R(("ID", "NI")[t], 128), R("X", 512, x[1] + h)), (R(("NI", "ID")[t], 128), R("Y", 512, y[1] + h))])
+                act(R("mk", 512, m[1] + h), R(pb, 512), R("cst", 1, 4), f=AF.Sign)
+            ops[-1]["due"] = due(0)
+            mm(R(pb, w), [(R("Z2", 128, 15 - k), ("mk", m[1] + k, m[2], 16)) for k in range(16)])
         else:
-            w, mo, win, off = CW, 16 * CW * c, R("PW%d" % t, W * (e + 1) if CFG["rep"] else W), R("T16", CW, L * t + CW * c)
-            y, out = R("Y", 16 * w, 4096 * i + mo), R(bank(c), w, w * (c % CFG["sw"]))
-        n = 16 * w
-        k = 1 if c is None else CFG["split"][i]
-        for j in range(k):
-            m, o, yy = R("mk", n // k, mo + n // k * j), R(off[0], w // k, off[1] + w // k * j), R(y[0], n // k, y[1] + n // k * j)
-            add("v", ga(n // k), lambda g, T, X, m=m, o=o, yy=yy: g.vector.tensor_tensor(S(T, m), S(T, win).indirect(S(T, o)), S(T, yy), (A.is_gt, A.is_lt)[t]),
-                [win, o, yy], [m])
-        mm(out, [(R("NG", 128), R("on", w))] + [(R("Z", 128, 15 - k), ("mk", mo + k, mo + n, 16)) for k in range(16)])
-
-    def revert(t, e, c, k=1):
-        i = 4 * t + e
-        if c is None:
-            pb, w, o = "pb6", 16, 0
-            a, tc, t16 = R("ACc", 16, 16 * i), R("TTc", 16, 16 * t), R("T16c", 16, 16 * t)
+            gather("v", m, win, t16, lambda g, T, o, x, yy: g.vector.tensor_tensor(o, x, yy, (A.is_gt, A.is_lt)[t]), other=y, parts=nv, due=due)
+            mm(R(pb, w, w * ((c or 0) % SW)), [(R("NG", 128), R("on", w))] + [(R("Z", 128, 15 - k), ("mk", m[1] + k, m[2], 16)) for k in range(16)])
+        if c is not None:
+            if (c + 1) % SW:
+                return
+            c, w = c + 1 - SW, CW * SW
+            a, t16, tc, l = [R(b, w, L * k + CW * c) for b, k in (("AC", i), ("T16", t), ("TT", t), ("Lr", t))]
+        if c is not None and i in CFG["sg"]:
+            act(R("sg", w, CW * c), R(pb, w), R("cst", 1, 4), f=AF.Sign)
+            mm(R(pb, w, 128), [(R("KI", 128), R("sg", w, CW * c)), (R("NK", 128), R("on", w)), (R("I32", 128), a)])
         else:
-            pb, w, o = bank(c), CW * k, 0
-            a, tc, t16 = R("AC", w, L * i + CW * c), R("TT", w, L * t + CW * c), R("T16", w, L * t + CW * c)
-        h0 = hot[0]
-        hot[0] += CFG["smh"]
-        tt(R(pb, w, 128 + o), R(pb, w, o), a, A.min)
-        tt(tc, R(pb, w, 128 + o), tc, A.max)
-        if e < 3 and c is None:
-            ts(R("Lc", 16), tc, 2047, A.bitwise_and)
-            copy(t16, R("Lc", 16))
-        elif e < 3 and CFG["rep"]:
+            tt(R(pb, w, 128), R(pb, w), a, A.min)
+        first = len(ops) - 1
+        old = tc
+        if c is not None and t in CFG["cs"] and e == 3:
+            tc = R("TF", w, tc[1])
+        tt(tc, R(pb, w, 128), old, A.max)
+        if e < 3 and i + 1 in CFG["rep"] and c is not None:
             copy(t16, tc)
         elif e < 3:
-            ts(R("Lr", w, tc[1]), tc, 2047, A.bitwise_and)
-            copy(t16, R("Lr", w, tc[1]))
-        hot[0] = h0
+            ts(l, tc, 2047, A.bitwise_and)
+            copy(t16, l)
+        if c is not None and e < 3 and CFG["td"]:
+            room = CFG["ord"][t].index(10 * e + 10 + c) - CFG["ord"][t].index(10 * e + c + SW - 1) - 1
+            for k, o in enumerate(ops[first:]):
+                o["due"] = due(0) + CFG["sl"][t] * CFG["td"][2] * (k + 1) / (len(ops) - first) * min(1.0, room / CFG["td"][2]) + 0.01
 
     def claims(t):
-        O, LO = "O%d" % t, "LO%d" % t
+        O, LO, I = "O%d" % t, "LO%d" % t, R(("ID", "NI")[t], 128)
         ts(R("hl", 16, 32 * t), R("TTc", 16, 16 * t), 7, A.logical_shift_right, 15, A.bitwise_and)
         ts(R("hl", 16, 32 * t + 16), R("TTc", 16, 16 * t), 127, A.bitwise_and)
-        copy(R("hlb", 32, 32 * t), R("hl", 32, 32 * t))
+        ts(R("hlb", 32, 32 * t), R("hl", 32, 32 * t), 0.5 * CFG["th"], A.add)
         for s in range(16):
             ts(R("OH", 128, 128 * s), R("IB", 128), R("hlb", 1, 32 * t + s), A.is_equal, cyc=0.5)
-            ts(R("OL", 128, 128 * s), R("IL", 128), R("hlb", 1, 32 * t + 16 + s), A.is_equal, cyc=0.5)
-        for h in range(4):
-            add("t", 512 * CYC, lambda g, T, X, h=h: [g.tensor.matmul(T["pb6"][:, 0:128], T["OH"][:, 128 * s:128 * s + 128], T["OL"][:, 128 * s:128 * s + 128],
-                                                                      s == 0, s == 15) for s in range(4 * h, 4 * h + 4)][-1],
-                [R("OH", 512, 512 * h), R("OL", 512, 512 * h), R("pb6", 128)][:2 + (h > 0)], [R("pb6", 128)])
-        ts(R("C", 128, 128 * t), R("pb6", 128), 1.0, A.min, 256.0, A.mult)
+            if CFG["th"]:
+                act(R("OL", 130, 130 * s), R("IL", 130), R("hlb", 1, 32 * t + 16 + s), -1.0, AF.Sign)
+            else:
+                ts(R("OL", 128, 128 * s), R("IL", 128), R("hlb", 1, 32 * t + 16 + s), A.is_equal, cyc=0.5)
+        if CFG["th"]:
+            mm(R("pb6", 130), [(R("OH", 128, 128 * s), R("OL", 130, 130 * s)) for s in range(16)])
+            act(R("Cs", 128), R("pb6", 128, 1))
+            tt(R("C", 128, 128 * t), R("pb6", 128), R("Cs", 128), A.is_gt)
+        else:
+            mm(R("pb6", 128), [(R("OH", 128, 128 * s), R("OL", 128, 128 * s)) for s in range(16)])
+            ts(R("C", 128, 128 * t), R("pb6", 128), 1.0, A.min)
         for b in range(NB):
-            pb, o = "pb%d" % (b % 2), BW * b
-            mms([(R(pb, 128, h), [(R(("ID", "NI")[t], 128), R(P[t][0], 128, o + h)), (R("E", 128, o + h), R("C", 128, 128 * t))]) for h in range(0, BW, 128)])
+            pb, o = wide(b), BW * b
+            fl = [(R(pb, 128, h), R("E", 128, o + h), R("C", 128, 128 * t)) for h in range(0, BW, 128)]
             if CFG["of"][t][b] == "S":
+                if CFG["pre"]:
+                    matmuls([(R(pb, BW), I, R(P[t][0], BW, o), True, False)] + [x + (False, x is fl[-1]) for x in fl])
+                else:
+                    mms([(x[0], [(I, R(P[t][0], 128, o + x[0][1])), x[1:]]) for x in fl])
                 act(R(O, BW, o), R(pb, BW), R("cst", 1, t), f=AF.Relu)
             else:
-                ts(R(O, BW, o), R(pb, BW), (-256.0, -1.0)[t], A.add, 0.0, A.max)
-            add("g", 0.6, lambda g, T, X, b=b: X["send"](g, T, t, b), [R(O, BW, o)], [("wire%d" % t, b, b + 1)], kind="r")
+                mms([(x[0], [x[1:]]) for x in fl])
+                tt(R(O, BW, o), R(pb, BW), R(P[t][0], BW, o), A.mult)
+            add("g", 0.6, lambda g, T, X, b=b: X["send"](g, T, t, b), [R(O, BW, o)], [("wire%d" % t, b, b + 1)], kind="r", due=CFG["sd"][t] + b)
             for far in ((0, 1) if CFG["route"] == "A" else (1,)):
                 add("x%d%d%d" % (far, t, b), CFG["xt"][t] * (0.6, 1.0)[far] + CFG["xs"] * b, "%s%d_%d" % (("arr", "far")[far], t, b), [("wire%d" % t, b, b + 1)],
                     [R(LO, BW, q * W + o) for q in (((0,), (1, 2))[far] if CFG["route"] == "A" else (0, 1, 2))], kind="x")
@@ -305,7 +372,7 @@ def build():
     def prices(t):
         LO, I = "LO%d" % t, R(("ID", "NI")[t], 128)
         for b in range(NB):
-            o, pb, how = BW * b, "pb%d" % (b % 2), CFG["pr"][t][b]
+            o, pb, how = BW * b, wide(b), CFG["pr"][t][b]
             new, old = R(("PW1", "P2")[t], BW, o), R(P[t][0], BW, o)
             s = [(R("DG", 128), R(LO, BW, q * W + o)) for q in range(3)]
             if how == "V":
@@ -326,36 +393,44 @@ def build():
                 else:
                     act(R("D", BW, o), R(pb, BW), R("cst", 1, 3), -1.0, AF.Relu)
                     act(new, R("D", BW, o), 255.0, -1.0)
+            ops[-1]["due"] = CFG["pd"][t] + b
             if t == 1:
                 dma(lambda T, o=o: T.yp[:, o:o + BW], lambda T, o=o: T["P2"][:, o:o + BW], 128, [R("P2", BW, o)], [])
-        if t == 0 and CFG["rep"]:
-            for k in (1, 2, 3):
-                dma(lambda T, k=k: T["PW1"][:, k * W:k * W + W], lambda T: T["PW1"][:, 0:W], 512, [P[1]], [R("PW1", W, k * W)])
 
-    def closing(t, c, k):
-        w = CW * k
-        r = lambda b: R(b, w, L * t + CW * c)
-        ts(r("Lr"), r("TT"), 2047, A.bitwise_and)
-        if t == 0:
-            copy(R("A16", w, 4 * L + CW * c), r("Lr"))
-        if (c + k) % 2 == 0:
-            o = L * t + CW * (c + k - 2)
+    def closing(t, c):
+        r = lambda b: R(b, CW * SW, L * t + CW * c)
+        if t in CFG["cs"]:
+            lot = R(bank(c), CW * SW, 384)
+            act(r("hb"), r("TF"), 129.0 - 2047.0 / 4096, 1.0 / 2048)
+            mm(lot, [(R("M2", 128), r("hb")), (R("I32", 128), r("TF"))])
+            if t == 0:
+                ts(R("A16", CW * SW, 4 * L + CW * c), lot, 129.0 * 2048, A.add)
+            act(r("yhf"), lot, 129.0 * 2048)
+        else:
+            ts(r("Lr"), r("TT"), 2047, A.bitwise_and)
+            if t == 0:
+                copy(R("A16", CW * SW, 4 * L + CW * c), r("Lr"))
+        if (c + SW) % 2 == 0:
+            o = L * t + CW * (c + SW - 2)
             hb, ht, yf = R("hb", 128, o), R("ht", 128, o), R("yhf", 128, o)
-            ts(hb, R("TT", 128, o), 1.0 / 2048, A.mult, 129.0 - 2047.0 / 4096, A.add)
+            if t not in CFG["cs"]:
+                ts(hb, R("TT", 128, o), 1.0 / 2048, A.mult, 129.0 - 2047.0 / 4096, A.add)
             add("v", vc(128, 0.5), lambda g, T, X: g.vector.transpose(S(T, ht), S(T, hb)), [hb], [ht])
             scan(R("hm", 128, o), ht)
-            copy(yf, R("Lr", 128, o))
+            if t not in CFG["cs"]:
+                copy(yf, R("Lr", 128, o))
             if t == 0:
                 act(R("AC", 128, 4 * L + o), yf, con[0])
-            dma(lambda T: T.yh[:, o:o + 128], lambda T: S(T, yf), 64, [yf], [])
+            if t == 1:
+                dma(lambda T: T.yh[:, o:o + 128], lambda T: S(T, yf), 64, [yf], [])
 
     def parents(t):
-        o = L * t
-        mms([(("pb7", 256 + 16 * l + h, 256 + 16 * l + 16, 2), [(R("WP", 128, 128 * (2 * h + k)), ("hm", o + 16 * k + 15, o + L, 32)) for k in range(2)])
-             for l in range(5) for h in range(2)])
+        o = 80 * t
+        vgath(R("hq", 80, o), R("hm", L, L * t), R("ql", 5))
+        mms([(("pb7", 256 + h, 336, 2), [(R("WP", 128, 128 * (2 * h + k)), ("hq", o + k, o + 80, 2)) for k in range(2)]) for h in range(2)])
         tt(R("pb7", 80, 384), R("pb7", 80, 256), R("LV", 80), A.is_equal)
-        tt(R("mb", 80, 80 * t), R("pb7", 80, 384), R("B", 80, 80 * t), A.mult)
-        mm(R("pb7", 16, 32), [(R("IDh", 128), R("mb", 16, 80 * t + 16 * l)) for l in range(5)])
+        tt(R("mb", 80, o), R("pb7", 80, 384), R("B", 80, o), A.mult)
+        mm(R("pb7", 16, 32), [(R("ID", 128), R("mb", 16, o + 16 * l)) for l in range(5)])
         if t == 0:
             copy(R("lst", 16, 80), R("pb7", 16, 32))
         copy(R("ph", 16, 16 * t), R("pb7", 16, 32))
@@ -364,70 +439,68 @@ def build():
 
     def parents_out(t):
         o = L * t
-        mms([(("pb7", 256 + s, 512, 16), [(("IDh", s, 128, 16), R("ph", 16, 16 * t))]) for s in range(16)], 8)
+        mms([(("pb7", 256 + s, 512, 16), [(("ID", s, 128, 16), R("ph", 16, 16 * t))]) for s in range(16)], 8)
         act(R("par", L, o), R("pb7", L, 256), p=8)
         dma(lambda T: T.yv[:, o:o + L], lambda T: T["par"][0:8, o:o + L], 8, [R("par", L, o)], [])
 
-    def next_lots(c, k):
-        w = CW * k
-        r = lambda b, a=0: R(b, w, a + CW * c)
-        u = R(bank(c), w, 256)
-        mm(u, [(R("BDw", 128), ("sm", 16 * CW * c + 15, 16 * (CW * c + w), 16))])
+    def next_lots(c):
+        r = lambda b, a=0: R(b, CW * SW, a + CW * c)
+        n, u = 8 * CW, R(bank(c), CW * SW, 256)
+        for h in range(2 * c, 2 * (c + SW)):
+            x = R("X", n, n * h)
+            (vgath if h in CFG["xv"] else sgath)(x, P[0], R("A16", CW // 2, 4 * L + CW // 2 * h))
+            scan(R("sm", n, x[1]), x)
+        mm(u, [(R("BDw", 128), ("sm", 2 * n * c + 15, 2 * n * (c + SW), 16))])
         copy(r("w1"), u)
         ts(r("w2"), r("w1"), 1023, A.bitwise_and)
         ts(u, r("w2"), 2.0, A.mult, 33.0, A.add)
-        tt(r("w3"), u, r("Lr"), A.mult)
+        tt(r("w3"), u, r("yhf" if 0 in CFG["cs"] else "Lr"), A.mult)
         ts(r("w4"), r("w3"), 2464.0, A.add)
         ts(r("TT", L), r("w4"), 5, A.logical_shift_right, 2047, A.bitwise_and)
         copy(r("T16", L), r("TT", L))
+        ops[-1]["due"] = CFG["t0"][0] + CFG["sl"][0] * (CFG["ord"][0].index(29 + c + SW) + 1) + CFG["nd"]
+        if CFG["tp"]:
+            copy(r("th"), r("TT", L))
 
     def early(t):
-        hot[0] = HOT
         for e in range(4):
             if e:
                 package(4 * t + e)
-            ahead(t, e, None)
-            compare(t, e, None)
-            revert(t, e, None)
+            trial(t, e, None)
+        for k in range(1, 1 + max([i % 4 for i in CFG["rep"] if i // 4 == t] or [0])):
+            dma(lambda T, k=k: T[P[t][0]][:, k * W:k * W + W], lambda T: T[P[t][0]][:, 0:W] if t else T.price[:], 512,
+                [P[t], R("A16c", 16, 16 * (4 * t + CFG["rg"][t]))], [R(P[t][0], W, k * W)])
         claims(t)
 
-    def trials(t):
-        sw = CFG["sw"]
+    def lanes(t):
         for e in range(4):
             for c in range(NCH):
-                hot[0] = CFG["yh"] - CFG["co"][t][c]
-                if c % CFG["yw"] == 0:
-                    ahead(t, e, c, CFG["yw"])
-                hot[0] = -CFG["co"][t][c]
-                compare(t, e, c)
-                if (c + 1) % sw == 0:
-                    revert(t, e, c + 1 - sw, sw)
-        for c in range(0, NCH, sw):
-            hot[0] = CFG["ch"][t]
-            closing(t, c, sw)
+                trial(t, e, c)
+        for c in range(0, NCH, SW):
+            closing(t, c)
             if t == 0:
-                for j in range(c, c + sw):
-                    n = 16 * CW
-                    act(R("X", n, n * j), P[0], off=R("A16", CW, 4 * L + CW * j))
-                    scan(R("sm", n, n * j), R("X", n, n * j))
-                next_lots(c, sw)
-        hot[0] = 0.0
+                next_lots(c)
 
-    hot[0] = HOT
     as_list(1, R("bh", L))
     early(0)
-    trials(0)
-    hot[0] = CFG["ph"]
+    lanes(0)
     prices(0)
-    hot[0] = HOT
-    dma(lambda T: T["T16c"][:, 16:32], lambda T: T["T16"][1::16, L:2 * L], 8, [R("T16", L, L)], [R("T16c", 16, 16)])
-    dma(lambda T: T["TTc"][:, 16:32], lambda T: T["TT"][1::16, L:2 * L], 8, [R("TT", L, L)], [R("TTc", 16, 16)])
+    if CFG["tp"]:
+        mm(R("pb6", 16), [(R("Z1", 128, 15 - s), R("th", 16, 16 * s)) for s in range(16)])
+        copy(R("T16c", 16, 16), R("pb6", 16))
+        copy(R("TTc", 16, 16), R("pb6", 16))
+    elif CFG["one"]:
+        dma(lambda T: T["TTc"][:, 16:32], lambda T: T["TT"][1::16, L:2 * L], 30, [R("TT", L, L)], [R("TTc", 16, 16)])
+        copy(R("T16c", 16, 16), R("TTc", 16, 16))
+    else:
+        dma(lambda T: T["T16c"][:, 16:32], lambda T: T["T16"][1::16, L:2 * L], 30, [R("T16", L, L)], [R("T16c", 16, 16)])
+        dma(lambda T: T["TTc"][:, 16:32], lambda T: T["TT"][1::16, L:2 * L], 30, [R("TT", L, L)], [R("TTc", 16, 16)])
     claim_forms(4)
     parents(0)
     early(1)
-    hot[0] = 0.0
+    dma(lambda T: T.yh[:, 0:L], lambda T: T["yhf"][:, 0:L], 128, [R("yhf", L), R("C", 128, 128)], [])
     parents_out(0)
-    trials(1)
+    lanes(1)
     prices(1)
     parents(1)
     parents_out(1)
@@ -441,7 +514,7 @@ def depend(ops):
         for wr, rs in ((False, o["rd"]), (True, o["wr"])):
             for r in rs:
                 for (j, a, b, w) in acc.get(r[0], []):
-                    bank = r[0][:2] == "pb" and ops[j]["q"] != o["q"]
+                    bank = r[0][:2] == "pb" and (ops[j]["q"] != o["q"] or o["q"] == "t")
                     if j != i and (bank or ((w or wr) and a < r[2] and r[1] < b)):
                         d.add(j)
         for wr, rs in ((False, o["rd"]), (True, o["wr"])):
@@ -452,51 +525,6 @@ def depend(ops):
                 lst.append((i, r[1], r[2], wr))
         deps.append(sorted(d))
     return deps
-
-
-def schedule(ops, deps):
-    n, LAT = len(ops), CFG["lat"]
-    succ = [[] for _ in range(n)]
-    for i, d in enumerate(deps):
-        for j in d:
-            succ[j].append(i)
-    lev = [0.0] * n
-    for i in range(n - 1, -1, -1):
-        lev[i] = ops[i]["cost"] + max([lev[k] + LAT for k in succ[i]] or [0.0])
-    wgt = [lev[i] + ops[i]["hot"] for i in range(n)]
-    left = [len(d) for d in deps]
-    ready = [o.get("at", 0.0) for o in ops]
-    cand, free, order = {}, {}, []
-    for i in range(n):
-        if not left[i]:
-            cand.setdefault(ops[i]["q"], []).append(i)
-    while True:
-        best = None
-        for q, l in cand.items():
-            if l:
-                t = max(free.get(q, 0.0), min(ready[i] for i in l))
-                if best is None or t < best[0]:
-                    best = (t, q)
-        if best is None:
-            break
-        t, q = best
-        i = max((i for i in cand[q] if ready[i] <= t + (CFG["dh"] if ops[i]["hot"] > 100 else CFG["dm"]) + 1e-9), key=lambda i: (wgt[i], -i))
-        t = max(t, ready[i])
-        cand[q].remove(i)
-        o = ops[i]
-        fin = t + o["cost"]
-        if o["kind"] == "d":
-            free["dma"] = max(free.get("dma", 0.0), t) + o["cost"] - 2.0
-            fin = free["dma"] + 2.0
-        free[q] = t + (0.06 if o["kind"] == "d" else o["cost"])
-        order.append(i)
-        for k in succ[i]:
-            left[k] -= 1
-            ready[k] = max(ready[k], fin + LAT)
-            if not left[k]:
-                cand.setdefault(ops[k]["q"], []).append(k)
-    assert len(order) == n
-    return order
 
 
 def place(seq, before, dur, lag, res, at):
@@ -513,24 +541,45 @@ def place(seq, before, dur, lag, res, at):
     return start
 
 
-def justify(ops, deps, seq):
+def schedule(ops, deps):
     n = len(ops)
     succ = [[] for _ in range(n)]
     for i, d in enumerate(deps):
         for j in d:
             succ[j].append(i)
     dur = [o["cost"] - 2.0 * (o["kind"] == "d") for o in ops]
-    lag = [CFG["lat"] + 2.0 * (o["kind"] == "d") for o in ops]
     res = [o["q"] for o in ops]
+    lag = lambda i, j: 0.0 if res[i] == res[j] == "t" else CFG["lat"] + 2.0 * (ops[j]["kind"] == "d")
+    late = [0.0] * n
+    for i in range(n - 1, -1, -1):
+        late[i] = min([ops[i].get("due", CFG["end"] - 2.0 * (ops[i]["kind"] == "d"))] + [late[k] - lag(k, i) for k in succ[i]]) - dur[i]
+    for i in range(n):
+        late[i] = ops[i].get("rank", late[i])
+    for i in range(n):
+        late[i] = max([late[i]] + [late[j] + 1e-6 for j in deps[i]])
+    tail = [2.0 * (o["kind"] == "d") for o in ops]
     best = None
     for _ in range(CFG["it"]):
-        st = place(seq, deps, dur, lambda i, j: lag[j], res, [o.get("at", 0.0) for o in ops])
-        end = max(st[i] + dur[i] + lag[i] for i in range(n))
-        if best is None or end < best[0]:
-            best = (end, sorted(range(n), key=lambda i: (st[i], i)))
-        rs = place(sorted(range(n), key=lambda i: (-st[i] - dur[i] - lag[i], -i)), succ, dur, lambda i, j: lag[i], res, lag)
-        seq = sorted(range(n), key=lambda i: (-rs[i] - dur[i], i))
-    return best[1]
+        st = place(sorted(range(n), key=lambda i: (late[i], i)), deps, dur, lag, res, [0.0] * n)
+        end = max(st[i] + dur[i] + tail[i] for i in range(n))
+        if best is None or end < best[0] - 0.05:
+            best = (end, st)
+        back = place(sorted(range(n), key=lambda i: (-st[i] - dur[i], -i)), succ, dur, lambda i, k: lag(k, i), res, tail)
+        late = [ops[i].get("rank", end - back[i] - dur[i]) for i in range(n)]
+        for i in range(n):
+            late[i] = max([late[i]] + [late[j] + 1e-6 for j in deps[i]])
+    st = best[1]
+    order = sorted(range(n), key=lambda i: (st[i], i))
+    calls, last = [], {}
+    for i in order:
+        p, c = ops[i].get("part"), last.get(res[i])
+        if p and c and ops[c[-1]].get("part") == (p[0], p[1] - 1) and all(st[j] + dur[j] + lag(i, j) <= st[c[0]] + 1e-9 for j in deps[i]):
+            c.append(i)
+        else:
+            last[res[i]] = [i]
+            calls.append(last[res[i]])
+    PLAN["end"] = max(st[i] + dur[i] for i in range(n))
+    return calls
 
 
 PLAN = {}
@@ -540,8 +589,8 @@ def plan():
     if "ops" not in PLAN:
         PLAN["ops"] = build()
         PLAN["deps"] = depend(PLAN["ops"])
-        PLAN["order"] = justify(PLAN["ops"], PLAN["deps"], schedule(PLAN["ops"], PLAN["deps"]))
-    return PLAN["ops"], PLAN["deps"], PLAN["order"]
+        PLAN["calls"] = schedule(PLAN["ops"], PLAN["deps"])
+    return PLAN["ops"], PLAN["deps"], PLAN["calls"]
 
 
 def helpers(c, cores, topo):
@@ -551,8 +600,13 @@ def helpers(c, cores, topo):
     return [h for pair in zip(far, near) for h in pair]
 
 
-def others(cores, dst, topo):
-    return sorted((c for c in cores if c != dst), key=lambda c: (not topo.same_plane(c, dst), c))
+def relays(d, topo):
+    hs = [h for h in range(WORLD) if topo.mates(h, d) and topo.may_write(h, d)]
+    return [h for pair in zip([h for h in hs if topo.die(h) == topo.die(d)], [h for h in hs if topo.die(h) != topo.die(d)]) for h in pair]
+
+
+def others(cores, c, topo):
+    return sorted((d for d in cores if d != c), key=lambda d: (not topo.same_plane(c, d), topo.host(c) != topo.host(d)))
 
 
 def bits(es):
@@ -573,14 +627,15 @@ def dst_id(d, src, topo):
 def hand_on(g, core, T, topo):
     cores = list(T.cores)
     for c in cores:
-        hs = helpers(c, cores, topo)
-        if core not in hs:
+        rest = others(cores, c, topo)
+        hs, rs = helpers(c, cores, topo), relays(rest[2], topo) if CFG["route"] == "C" else []
+        if core not in hs + rs:
             continue
-        b = hs.index(core)
-        to = others(cores, c, topo)[CFG["route"] == "A":]
+        b = (hs + rs).index(core) % NB
+        to = rest[2:] if core in rs else {"A": rest[1:], "B": rest, "C": rest[:2]}[CFG["route"]]
         es = topo.engines(core, to[0])
         for t in range(2):
-            g.wait_ge(T.sem["hin%d" % t], len(into(c, core, cores, topo)))
+            g.wait_ge(T.sem["hin%d" % t], len(topo.engines(c, core) if core in rs else into(c, core, cores, topo)))
             at = [others(cores, d, topo).index(c) * W + BW * b for d in to]
             g.remote_dma_fused([RemoteDMATransfer(dst_ids=[dst_id(d, core, topo) for d in to], dma_engine_mask=bits(es), remote_sem=T.sem["far%d_%d" % (t, b)],
                                                   srcs=[T["HB"][:, t * BW:t * BW + BW]], dsts=[T["LO%d" % t][:, o:o + BW] for o in at])],
@@ -594,7 +649,7 @@ def rank_program(g, core, T, topo):
         return
     cores = list(T.cores)
     hs, rest = helpers(core, cores, topo), others(cores, core, topo)
-    ops, deps, order = plan()
+    ops, deps, calls = plan()
     eng = {"v": g.vector, "s": g.scalar, "t": g.tensor, "y": g.sync, "g": g}
     sent = [0]
 
@@ -608,6 +663,12 @@ def rank_program(g, core, T, topo):
             tr.append(RemoteDMATransfer(dst_ids=[dst_id(rest[0], core, topo)], dma_engine_mask=bits(e0), remote_sem=T.sem["arr%d_%d" % (t, b)],
                                         srcs=[src], dsts=[T["LO%d" % t][:, BW * b:BW * b + BW]]))
             sent[0] += len(e0)
+        if CFG["route"] == "C":
+            r = relays(rest[2], topo)[b]
+            e0 = topo.engines(core, r)
+            tr.append(RemoteDMATransfer(dst_ids=[dst_id(r, core, topo)], dma_engine_mask=bits(e0), remote_sem=T.sem["hin%d" % t],
+                                        srcs=[src], dsts=[T["HB"][:, t * BW:t * BW + BW]]))
+            sent[0] += len(e0)
         g.remote_dma_fused(tr, local_sem=T.sem["snd"])
 
     arrive = {"a": len(topo.engines(rest[0], core)),
@@ -616,24 +677,24 @@ def rank_program(g, core, T, topo):
     cnt = {"v": 0, "s": 0, "t": 0, "g": 0}
     clock = {q: {} for q in eng}
     done = {}
-    pos = {i: k for k, i in enumerate(order)}
+    pos = {i: k for k, c in enumerate(calls) for i in c}
     nd = 0
-    for i in order:
-        o = ops[i]
+    for c in calls:
+        o = ops[c[0]]
         if o["kind"] == "x":
             n = arrive[o["fn"][0]]
-            done[i] = (o["fn"], n, {o["fn"]: n})
+            done[c[0]] = (o["fn"], n, {o["fn"]: n})
             continue
         q = o["q"]
         ck = clock[q]
-        for j in sorted(deps[i], key=lambda j: -pos[j]):
-            if j in done:
+        for j in sorted({j for i in c for j in deps[i]}, key=lambda j: -pos[j]):
+            if j in done and not q == ops[j]["q"] == "t":
                 s, n, c2 = done[j]
                 if ck.get(s, 0) < n:
                     eng[q].wait_ge(T.sem[s], n)
                     for k, v in c2.items():
                         ck[k] = max(ck.get(k, 0), v)
-        ins = o["fn"](g, T, X)
+        ins = o["fn"](g, T, o["part"][1], o["part"][1] + len(c)) if "part" in o else o["fn"](g, T, X)
         if o["kind"] == "c":
             cnt[q] += 1
             s, n = "q" + q, cnt[q]
@@ -646,7 +707,8 @@ def rank_program(g, core, T, topo):
             continue
         c2 = dict(ck)
         c2[s] = n
-        done[i] = (s, n, c2)
+        for i in c:
+            done[i] = (s, n, c2)
     for q, n in cnt.items():
         g.wait_ge(T.sem["q" + q], n)
     for k in range(nd):

from concourse.bass import DstId, RemoteDMATransfer
from concourse.mybir import AluOpType, ActivationFunctionType

BIG, WORLD = 16384, 256
W, L, H0 = 2048, 256, 768
NCH, CW = 4, 64
NB = 4
BW = W // NB
BF, F32, I32, U16, F16 = "bfloat16", "float32", "int32", "uint16", "float16"
CFG = {"cyc": 0.88e-3, "g": 1.5, "pe": 0.5, "lat": 0.24, "pd": (40.0, 90.0), "xt": (18.0, 14.0), "xs": 1.5, "rep": (2, 3, 6, 7), "rg": (3, 2), "pr": ("SSSV", "SSVV"), "of": ("SSSS", "SSSS"),
       "av": "1", "route": "C", "np": (8, 4, 1, 2, 8, 4, 1, 1), "ns": 4, "pp": 320, "it": 2, "t0": (6.0, 43.0), "sl": (1.8, 1.8), "sd": (16.0, 54.0), "end": 88.0, "xv": (5, 7), "pre": True, "nd": 10.0, "off": ((), ()), "th": False, "sg": (), "sw": 1, "tp": False, "cs": (), "ap": (), "td": (1, 2, 3), "one": True,
       "ord": ((0, 1, 2, 3, 10, 11, 20, 21, 12, 13, 30, 31, 22, 23, 32, 33), (0, 1, 10, 2, 11, 20, 3, 12, 21, 30, 13, 22, 31, 23, 32, 33))}

SCRATCH = {
    "PW0": ("sbuf", [128, 4 * W], BF), "PW1": ("sbuf", [128, 4 * W], BF), "P2": ("sbuf", [128, W], BF),
    "pk": ("sbuf", [128, H0], I32), "pv": ("sbuf", [128, H0], I32), "PK": ("sbuf", [128, H0], F32), "ac": ("sbuf", [128, 16], I32),
    "ic": ("sbuf", [128, 1], I32), "wc": ("sbuf", [128, 1], I32), "sc": ("sbuf", [128, 2], I32),
    "icf": ("sbuf", [128, 1], F32), "wcf": ("sbuf", [128, 1], F32), "scf": ("sbuf", [128, 2], F32), "cst": ("sbuf", [128, 8], F32), "Z2": ("sbuf", [128, 144], BF),
    "sg": ("sbuf", [128, L], BF), "KI": ("sbuf", [128, 128], BF), "NK": ("sbuf", [128, 128], BF), "I32": ("sbuf", [128, 128], F32),
    "ip": ("sbuf", [128, 1], I32), "im": ("sbuf", [128, 128], I32), "on": ("sbuf", [128, 1024], BF),
    "pg": ("sbuf", [128, 1], I32), "pgf": ("sbuf", [128, 1], F32), "pg16": ("sbuf", [128, 1], F32), "ipf": ("sbuf", [128, 1], F32),
    "mg": ("sbuf", [128, 128], I32), "pl": ("sbuf", [128, 1], F32), "Z1": ("sbuf", [128, 144], BF), "th": ("sbuf", [128, L], F16),
    "Z0": ("sbuf", [128, 144], BF), "ah": ("sbuf", [128, 2 * L], F16), "LV": ("sbuf", [128, 80], F32),
    "q1": ("sbuf", [128, 6], F32), "ql": ("sbuf", [128, 6], U16), "hq": ("sbuf", [128, 160], BF),
    "Z": ("sbuf", [128, 144], BF), "Zh": ("sbuf", [128, 144], F16), "NG": ("sbuf", [128, 128], BF),
    "BDw": ("sbuf", [128, 128], BF), "IB": ("sbuf", [128, 128], BF), "IL": ("sbuf", [128, 130], BF),
    "ID": ("sbuf", [128, 128], BF), "M2": ("sbuf", [128, 128], BF), "TF": ("sbuf", [128, 2 * L], F32), "NI": ("sbuf", [128, 128], BF), "DG": ("sbuf", [128, 128], BF),
    "E": ("sbuf", [128, W], BF), "WP": ("sbuf", [128, 512], BF), "scd": ("sbuf", [128, 1024], BF),
    "bh": ("sbuf", [128, 6 * L], F16), "lst": ("sbuf", [128, 8 * 16], U16), "B": ("sbuf", [128, 160], F32),
    "A16": ("sbuf", [128, 8 * L], U16), "AC": ("sbuf", [128, 8 * L], F32),
    "A16c": ("sbuf", [128, 8 * 16], U16), "ACc": ("sbuf", [128, 8 * 16], F32),
    "T16": ("sbuf", [128, 2 * L], U16), "TT": ("sbuf", [128, 2 * L], I32), "Lr": ("sbuf", [128, 2 * L], I32),
    "T16c": ("sbuf", [128, 32], U16), "TTc": ("sbuf", [128, 32], I32), "Lc": ("sbuf", [128, 16], I32),
    "Y": ("sbuf", [128, 6 * 4096], BF), "Yc": ("sbuf", [128, 8 * L], BF), "mk": ("sbuf", [128, 4096 + 256], BF),
    "X": ("sbuf", [128, 4096], BF), "sm": ("sbuf", [128, 4096], BF),
    "yhf": ("sbuf", [128, 2 * L], F32), "w1": ("sbuf", [128, L], I32), "w2": ("sbuf", [128, L], I32), "w3": ("sbuf", [128, L], I32),
    "w4": ("sbuf", [128, L], I32),
    "hb": ("sbuf", [128, 2 * L], BF), "ht": ("sbuf", [128, 2 * L], BF), "hm": ("sbuf", [128, 2 * L], BF),
    "mb": ("sbuf", [128, 160], F16), "ph": ("sbuf", [128, 32], F16), "par": ("sbuf", [128, 2 * L], F32),
    "hl": ("sbuf", [128, 64], I32), "hlb": ("sbuf", [128, 64], F32),
    "OH": ("sbuf", [128, 16 * 128], BF), "OL": ("sbuf", [128, 16 * 130], BF), "C": ("sbuf", [128, 256], BF), "Cs": ("sbuf", [128, 128], F32),
    "O0": ("sbuf", [128, W], BF), "O1": ("sbuf", [128, W], BF), "N16": ("sbuf", [128, W], F16), "D": ("sbuf", [128, W], BF),
    "LO0": ("sbuf", [128, 3 * W], BF), "LO1": ("sbuf", [128, 3 * W], BF),
    "HB": ("sbuf", [128, 2 * BW], BF),
}
for _i in range(8):
    SCRATCH["pb%d" % _i] = ("psum", [128, 512], F32)
ND = 56
SEMAPHORES = ["qv", "qs", "qt", "qg", "snd", "hs", "hin0", "hin1"] + ["d%d" % i for i in range(ND)] + \
    ["%s%d_%d" % (n, t, b) for n in ("arr", "far") for t in range(2) for b in range(NB)]

A = AluOpType
AF = ActivationFunctionType


def build():
    ops = []
    CYC = CFG["cyc"]

    def add(q, cost, fn, rd, wr, kind="c", **more):
        ops.append(dict(q=q, cost=cost, fn=fn, rd=rd, wr=wr, kind=kind, **more))

    def vc(n, cyc=1.0):
        return max(64, n * cyc) * CYC + 0.01

    def S(T, r, p=128):
        return T[r[0]][0:p, r[1]:r[2]] if len(r) == 3 else T[r[0]][0:p, r[1]:r[2]:r[3]]

    R = lambda b, n, a=0: (b, a, a + n)

    def n_of(r):
        return len(range(*r[1:]))

    def copy(out, in_, cyc=1.0):
        add("v", vc(n_of(out), cyc), lambda g, T, X: g.vector.tensor_copy(S(T, out), S(T, in_)), [in_], [out])

    def ts(out, in_, s1, op0, s2=None, op1=None, cyc=1.0):
        rd = [in_] + [s for s in (s1, s2) if isinstance(s, tuple)]

        def fn(g, T, X):
            a = S(T, s1) if isinstance(s1, tuple) else s1
            b = S(T, s2) if isinstance(s2, tuple) else s2
            if op1 is None:
                return g.vector.tensor_scalar(S(T, out), S(T, in_), a, None, op0)
            return g.vector.tensor_scalar(S(T, out), S(T, in_), a, b, op0, op1)
        add("v", vc(n_of(out), cyc), fn, rd, [out])

    def tt(out, a, b, op):
        two = 1.0 if (a[0][:2] == "pb" or b[0][:2] == "pb") else 2.0
        add("v", vc(n_of(out), two), lambda g, T, X: g.vector.tensor_tensor(S(T, out), S(T, a), S(T, b), op), [a, b], [out])

    def scan(out, in_):
        n = n_of(out)
        add("v", vc(n, 0.5), lambda g, T, X: g.vector.tensor_tensor_scan(S(T, out), T["scd"][:, 0:n], S(T, in_), 0.0, A.mult, A.max),
            [("scd", 0, n), in_], [out])

    def act(out, in_, bias=0.0, scale=1.0, f=AF.Copy, p=128):
        add("s", max(64, n_of(out)) * CYC + 0.03,
            lambda g, T, X: g.scalar.activation(S(T, out, p), S(T, in_, p), f, bias=S(T, bias) if isinstance(bias, tuple) else bias, scale=scale),
            [r for r in (in_, bias) if isinstance(r, tuple)], [out])

    def gather(q, out, win, off, call, more=(), other=None, parts=1, due=None):
        w, key = n_of(off) // parts, len(ops)

        def emit(g, T, a, b):
            cut = lambda r, k: T[r[0]][:, r[1] + k * w * a:r[1] + k * w * b]
            return call(g, T, cut(out, 16), S(T, win).indirect(cut(off, 1)), other and cut(other, 16))
        for j in range(parts):
            cut = lambda r, k: R(r[0], k * w, r[1] + k * w * j)
            add(q, 16 * w * CFG["g"] * CYC + (0.06 if parts == 1 else 0.03), emit, [win, cut(off, 1)] + list(more) + ([cut(other, 16)] if other else []),
                [cut(out, 16)], part=(key, j))
            if due:
                ops[-1]["due"] = due(j + 1.0 - parts)

    def vgath(out, win, off, **k):
        gather("v", out, win, off, lambda g, T, o, i, _: g.vector.tensor_copy(o, i), **k)

    def sgath(out, win, off, bias=0.0, **k):
        col = isinstance(bias, tuple)
        gather("s", out, win, off, lambda g, T, o, i, _: g.scalar.activation(o, i, AF.Identity if col else AF.Copy, bias=S(T, bias) if col else bias),
               [bias] if col else [], **k)

    def matmuls(l, m=128):
        piece, cost = [], 0
        for k, x in enumerate(l):
            piece.append(x)
            cost += max(min(64, m), n_of(x[2])) * (4 if x[1][0] == "I32" else 1)
            if cost >= CFG["pp"] or k == len(l) - 1:
                add("t", cost * CYC * CFG["pe"], lambda g, T, X, piece=piece: [g.tensor.matmul(S(T, o, m), S(T, a), S(T, b), s, e) for o, a, b, s, e in piece][-1],
                    [r for x in piece for r in x[1:3]], [x[0] for x in piece])
                piece, cost = [], 0

    def mms(groups, m=128):
        matmuls([(o, a, b, i == 0, i == len(ps) - 1) for o, ps in groups for i, (a, b) in enumerate(ps)], m)

    def mm(out, pairs):
        mms([(out, pairs)])

    def dma(out, in_, kb, rd, wr, **more):
        add("y", 2.0 + kb / 200.0, lambda g, T, X: g.sync.dma_start(out(T), in_(T)), rd, wr, kind="d", **more)

    def iota(out, pattern, base, cm, small=False):
        def fn(g, T, X):
            if small:
                return g.iota(S(T, out), pattern, base, cm, allow_small_or_imprecise_dtypes=True)
            return g.iota(S(T, out), pattern, base, cm)
        add("g", 0.15 + 2 * n_of(out) * CYC, fn, [], [out])

    def select(out, in_, pattern, cmp, cm, base=0):
        add("g", 0.17 + 2 * n_of(out) * CYC, lambda g, T, X: g.affine_select(S(T, out), S(T, in_), pattern, cmp, 0.0, base, cm), [in_], [out])

    def mset(out, v, cyc=0.5):
        add("v", vc(n_of(out), cyc), lambda g, T, X: g.vector.memset(S(T, out), v), [], [out])

    con = [float(2048 * (e + 1)) for e in range(4)]
    P = [R("PW0", W), R("PW1", W)]

    mset(R("pv", H0), 0, 1.0)
    ops[-1]["rank"] = -100.0
    ops[-1]["wr"].append(R("gate", 1))
    loads = [("TTc", 0, 16, lambda T: T.lots[0::16, :], 30), ("ac", 0, 16, lambda T: T.packs[0::16, H0 - L:H0], 30), ("sc", 0, 2, lambda T: T.slack[:], 30),
             ("PW0", 0, W, lambda T: T.price[:], 512), ("pv", 0, H0, lambda T: T.prev[:], 24), ("pk", H0 - L, L, lambda T: T.packs[:, H0 - L:H0], 128),
             ("TT", 0, L, lambda T: T.lots[:], 128), ("pk", 0, H0 - L, lambda T: T.packs[:, 0:H0 - L], 256),
             ("wc", 0, 1, lambda T: T.wt[:], 30), ("ic", 0, 1, lambda T: T.inc[:], 30)]
    for k, (b, a, n, src, kb) in enumerate(loads):
        dma(lambda T, b=b, a=a, n=n: T[b][0::16 if b == "pv" else 1, a:a + n], src, kb, [R("gate", 1)] * (k > 4), [R(b, n, a)], rank=k - 99.0)
    iota(R("ip", 1), [[1, 1]], 0, 1)
    iota(R("im", 128), [[1, 128]], 0, 0)
    iota(R("on", 128), [[0, 128]], 1, 0, True)
    iota(R("mg", 128), [[1, 8], [0, 16]], 0, 0)
    iota(R("IL", 130), [[1, 130]], 0, 0, True)
    mset(R("E", W), 256.0)

    def diagonal(b, v):
        if v != 1:
            iota(R(b, 128), [[0, 128]], v, 0, True)
        select(R(b, 128), R("on" if v == 1 else b, 128), [[-1, 128]], A.is_equal, 1)
    if CFG["ap"]:
        iota(R("Z0", 144), [[0, 144]], 1, 0, True)
        select(R("Z0", 144), R("Z0", 144), [[-16, 9], [1000, 16]], A.is_equal, 1, -15000)
    if CFG["sg"]:
        iota(R("NK", 128), [[0, 128]], -BIG // 128, 0, True)
        diagonal("KI", BIG)
    iota(R("I32", 128), [[0, 128]], 1, 0, True)
    select(R("I32", 128), R("I32", 128), [[-1, 128]], A.is_equal, 1)
    diagonal("ID", 1)
    select(R("E", W), R("E", W), [[-1, 16], [-16, 8], [0, 16]], A.is_equal, 1)
    iota(R("on", 384, 128), [[0, 384]], 1, 0, True)
    select(R("scd", 512), R("on", 512), [[0, 32], [1, 16]], A.not_equal, 0)
    if CFG["cs"]:
        diagonal("M2", -2048)
    diagonal("NI", -1)
    iota(R("LV", 80), [[1, 5], [0, 16]], 129, 0, True)
    if CFG["tp"] or CFG["ap"]:
        select(R("Z1", 144), R("on", 144), [[-16, 9], [1000, 16]], A.is_equal, 1, -15001)
    for h in range(2):
        for k in range(2):
            select(R("WP", 128, 128 * (2 * h + k)), R("on", 128), [[-32, 4], [1000, 2], [-1, 16]], A.is_equal, 1, -16 * h - 1000 * k)
    for k, o in enumerate(ops):
        if o["q"] == "g":
            o["rank"] = k / 100.0 - 80.0
    mset(R("Z", 144), 0.0)
    mset(R("NG", 128), -BIG / 16.0)
    for k, v in enumerate((-256.0, -1.0, 384.0, 129.0, -0.5)):
        mset(R("cst", 1, k), v)
    ts(R("pg", 1), R("ip", 1), 4, A.logical_shift_right)
    copy(R("ipf", 1), R("ip", 1))
    copy(R("pgf", 1), R("pg", 1))
    ts(("Z", 15, 128, 16), R("im", 8), R("pgf", 1), A.is_equal, float(BIG), A.mult)
    ts(R("Zh", 144), R("Z", 144), 1.0 / BIG, A.mult, cyc=0.5)
    if CFG["off"] != ((), ()):
        ts(R("Z2", 144), R("Z", 144), 0.5, A.mult, cyc=0.5)
    ts(R("pg16", 1), R("pg", 1), 16.0, A.mult)
    ts(R("IB", 128), R("im", 128), R("pg16", 1), A.subtract, 0.5 * CFG["th"], A.add)
    ts(R("pl", 1), R("ipf", 1), R("pg16", 1), A.subtract, float(H0 - L), A.add)
    ts(R("B", 16, 16), R("im", 16), 16.0, A.mult, R("pl", 1), A.add)
    ts(R("B", 16, 96), R("B", 16, 16), float(L), A.add)
    ts(R("q1", 6), R("on", 6), R("pl", 1), A.mult, float(L - H0), A.add)
    ts(R("ql", 6), R("q1", 6), 16.0, A.mult, 15.0, A.add)
    ts(R("icf", 1), R("ic", 1), 1.0 / 64, A.mult)
    ts(R("DG", 128), R("im", 128), R("ipf", 1), A.is_equal, R("icf", 1), A.mult)
    copy(R("wcf", 1), R("wc", 1))
    ts(R("BDw", 128), R("mg", 128), R("pgf", 1), A.is_equal, R("wcf", 1), A.mult)
    ts(R("scf", 1, 1), R("sc", 1, 1), -1.0, A.mult)
    copy(R("scf", 1), R("sc", 1))
    copy(R("A16c", 16), R("ac", 16))
    copy(R("T16c", 16), R("TTc", 16))
    ts(R("ACc", 16), R("ac", 16), con[0], A.add)
    for h in range(2):
        copy(R("A16", 128, 128 * h), R("pk", 128, H0 - L + 128 * h))
        copy(R("T16", 128, 128 * h), R("TT", 128, 128 * h))
    copy(R("bh", L), R("pv", L, H0 - L))
    copy(R("PK", L, H0 - L), R("pk", L, H0 - L))
    copy(R("PK", H0 - L), R("pk", H0 - L))
    act(R("AC", L), R("PK", L, H0 - L), con[0])

    SW = CFG["sw"]
    bank = lambda c: "pb%d" % (2 + c // SW)
    wide = lambda b: "pb%d" % ((0, 1, 4, 5)[b] if SW == 2 else b % 2)

    def claim_forms(i):
        t = i // 4
        if i in CFG["ap"]:
            h = R("ah", L, L * (i % 2))
            if i == 4:
                copy(h, R("A16", L, L * i), 0.5)
            else:
                ts(h, R("AC", L, L * i), -con[i % 4], A.add)
            mm(R("pb7", 16, 64), [(R("Z%d" % t, 128, 15 - s), R("ah", 16, h[1] + 16 * s)) for s in range(16)])
            copy(R("A16c", 16, 16 * i), R("pb7", 16, 64))
            ts(R("ACc", 16, 16 * i), R("pb7", 16, 64), con[i % 4], A.add)
            return
        if CFG["one"]:
            if i == 4:
                dma(lambda T: T["A16c"][:, 64:80], lambda T: T["A16"][1::16, 4 * L:5 * L], 30, [R("A16", L, 4 * L)], [R("A16c", 16, 64)])
                ts(R("ACc", 16, 64), R("A16c", 16, 64), con[0], A.add)
            else:
                dma(lambda T: T["ACc"][:, 16 * i:16 * i + 16], lambda T: T["AC"][t::16, L * i:L * i + L], 30, [R("AC", L, L * i)], [R("ACc", 16, 16 * i)])
                ts(R("A16c", 16, 16 * i), R("ACc", 16, 16 * i), -con[i % 4], A.add)
            return
        dma(lambda T: T["A16c"][:, 16 * i:16 * i + 16], lambda T: T["A16"][t::16, L * i:L * i + L], 30, [R("A16", L, L * i)], [R("A16c", 16, 16 * i)])
        dma(lambda T: T["ACc"][:, 16 * i:16 * i + 16], lambda T: T["AC"][t::16, L * i:L * i + L], 30, [R("AC", L, L * i)], [R("ACc", 16, 16 * i)])

    def package(i):
        t, e = i // 4, i % 4
        ls = R("lst", 16, 16 * i)
        if e < 3:
            row = R("bh", L, L * (3 * t + e))
            vgath(row, R("pv", H0), ls)
            as_list(i + 1, row)
        if str(i) in CFG["av"]:
            vgath(R("A16", L, L * i), R("pk", H0), ls)
            ts(R("AC", L, L * i), R("A16", L, L * i), con[e], A.add)
        else:
            sgath(R("AC", L, L * i), R("PK", H0), ls, con[e])
            ts(R("A16", L, L * i), R("AC", L, L * i), -con[e], A.add)
        claim_forms(i)

    def as_list(i, row):
        t, e = i // 4, i % 4
        mm(R("pb7", 16), [(R("Zh", 128, 15 - s), (row[0], row[1] + s, row[2], 16)) for s in range(16)])
        copy(R("lst", 16, 16 * i), R("pb7", 16))
        for k in ((e + 1,), (0, 4))[e == 3]:
            copy(R("B", 16, 80 * t + 16 * k), R("lst", 16, 16 * i))

    def trial(t, e, c):
        i = 4 * t + e
        if c is None:
            w, pb, win, due, ns, nv = 16, "pb6", P[t], None, 1, 1
            a16, a, t16, tc, l = R("A16c", w, w * i), R("ACc", w, w * i), R("T16c", w, w * t), R("TTc", w, w * t), R("Lc", w)
            y, m = R("Yc", L, L * i), R("mk", L, 4096)
        else:
            w, pb, win, ns, nv = CW, bank(c), R("PW%d" % t, W * (e + 1) if i in CFG["rep"] else W), CFG["ns"], CFG["np"][i]
            a16, a, t16, tc, l = [R(b, w, L * k + w * c) for b, k in (("A16", i), ("AC", i), ("T16", t), ("TT", t), ("Lr", t))]
            y, m = R("Y", 16 * w, 4096 * (i % 6) + 16 * w * c), R("mk", 16 * w, 16 * w * c)
            due = lambda j: CFG["t0"][t] + CFG["sl"][t] * (CFG["ord"][t].index(10 * e + c) + 1 + j / nv)
        if c is None:
            sgath(y, P[t], a16, R("scf", 1, t))
        elif c == 0:
            sgath(R("Y", 4096, y[1]), P[t], R("A16", L, L * i), R("scf", 1, t), parts=NCH * ns)
        if c is not None and 10 * e + c in CFG["off"][t]:
            x = R("X", 16 * w, 16 * w * c)
            sgath(x, win, t16, parts=ns)
            for h in (0, 512):
                mm(R(pb, 512), [(R(("ID", "NI")[t], 128), R("X", 512, x[1] + h)), (R(("NI", "ID")[t], 128), R("Y", 512, y[1] + h))])
                act(R("mk", 512, m[1] + h), R(pb, 512), R("cst", 1, 4), f=AF.Sign)
            ops[-1]["due"] = due(0)
            mm(R(pb, w), [(R("Z2", 128, 15 - k), ("mk", m[1] + k, m[2], 16)) for k in range(16)])
        else:
            gather("v", m, win, t16, lambda g, T, o, x, yy: g.vector.tensor_tensor(o, x, yy, (A.is_gt, A.is_lt)[t]), other=y, parts=nv, due=due)
            mm(R(pb, w, w * ((c or 0) % SW)), [(R("NG", 128), R("on", w))] + [(R("Z", 128, 15 - k), ("mk", m[1] + k, m[2], 16)) for k in range(16)])
        if c is not None:
            if (c + 1) % SW:
                return
            c, w = c + 1 - SW, CW * SW
            a, t16, tc, l = [R(b, w, L * k + CW * c) for b, k in (("AC", i), ("T16", t), ("TT", t), ("Lr", t))]
        if c is not None and i in CFG["sg"]:
            act(R("sg", w, CW * c), R(pb, w), R("cst", 1, 4), f=AF.Sign)
            mm(R(pb, w, 128), [(R("KI", 128), R("sg", w, CW * c)), (R("NK", 128), R("on", w)), (R("I32", 128), a)])
        else:
            tt(R(pb, w, 128), R(pb, w), a, A.min)
        first = len(ops) - 1
        old = tc
        if c is not None and t in CFG["cs"] and e == 3:
            tc = R("TF", w, tc[1])
        tt(tc, R(pb, w, 128), old, A.max)
        if e < 3 and i + 1 in CFG["rep"] and c is not None:
            copy(t16, tc)
        elif e < 3:
            ts(l, tc, 2047, A.bitwise_and)
            copy(t16, l)
        if c is not None and e < 3 and CFG["td"]:
            room = CFG["ord"][t].index(10 * e + 10 + c) - CFG["ord"][t].index(10 * e + c + SW - 1) - 1
            for k, o in enumerate(ops[first:]):
                o["due"] = due(0) + CFG["sl"][t] * CFG["td"][2] * (k + 1) / (len(ops) - first) * min(1.0, room / CFG["td"][2]) + 0.01

    def claims(t):
        O, LO, I = "O%d" % t, "LO%d" % t, R(("ID", "NI")[t], 128)
        ts(R("hl", 16, 32 * t), R("TTc", 16, 16 * t), 7, A.logical_shift_right, 15, A.bitwise_and)
        ts(R("hl", 16, 32 * t + 16), R("TTc", 16, 16 * t), 127, A.bitwise_and)
        ts(R("hlb", 32, 32 * t), R("hl", 32, 32 * t), 0.5 * CFG["th"], A.add)
        for s in range(16):
            ts(R("OH", 128, 128 * s), R("IB", 128), R("hlb", 1, 32 * t + s), A.is_equal, cyc=0.5)
            if CFG["th"]:
                act(R("OL", 130, 130 * s), R("IL", 130), R("hlb", 1, 32 * t + 16 + s), -1.0, AF.Sign)
            else:
                ts(R("OL", 128, 128 * s), R("IL", 128), R("hlb", 1, 32 * t + 16 + s), A.is_equal, cyc=0.5)
        if CFG["th"]:
            mm(R("pb6", 130), [(R("OH", 128, 128 * s), R("OL", 130, 130 * s)) for s in range(16)])
            act(R("Cs", 128), R("pb6", 128, 1))
            tt(R("C", 128, 128 * t), R("pb6", 128), R("Cs", 128), A.is_gt)
        else:
            mm(R("pb6", 128), [(R("OH", 128, 128 * s), R("OL", 128, 128 * s)) for s in range(16)])
            ts(R("C", 128, 128 * t), R("pb6", 128), 1.0, A.min)
        for b in range(NB):
            pb, o = wide(b), BW * b
            fl = [(R(pb, 128, h), R("E", 128, o + h), R("C", 128, 128 * t)) for h in range(0, BW, 128)]
            if CFG["of"][t][b] == "S":
                if CFG["pre"]:
                    matmuls([(R(pb, BW), I, R(P[t][0], BW, o), True, False)] + [x + (False, x is fl[-1]) for x in fl])
                else:
                    mms([(x[0], [(I, R(P[t][0], 128, o + x[0][1])), x[1:]]) for x in fl])
                act(R(O, BW, o), R(pb, BW), R("cst", 1, t), f=AF.Relu)
            else:
                mms([(x[0], [x[1:]]) for x in fl])
                tt(R(O, BW, o), R(pb, BW), R(P[t][0], BW, o), A.mult)
            add("g", 0.6, lambda g, T, X, b=b: X["send"](g, T, t, b), [R(O, BW, o)], [("wire%d" % t, b, b + 1)], kind="r", due=CFG["sd"][t] + b)
            for far in ((0, 1) if CFG["route"] == "A" else (1,)):
                add("x%d%d%d" % (far, t, b), CFG["xt"][t] * (0.6, 1.0)[far] + CFG["xs"] * b, "%s%d_%d" % (("arr", "far")[far], t, b), [("wire%d" % t, b, b + 1)],
                    [R(LO, BW, q * W + o) for q in (((0,), (1, 2))[far] if CFG["route"] == "A" else (0, 1, 2))], kind="x")

    def prices(t):
        LO, I = "LO%d" % t, R(("ID", "NI")[t], 128)
        for b in range(NB):
            o, pb, how = BW * b, wide(b), CFG["pr"][t][b]
            new, old = R(("PW1", "P2")[t], BW, o), R(P[t][0], BW, o)
            s = [(R("DG", 128), R(LO, BW, q * W + o)) for q in range(3)]
            if how == "V":
                mm(R(pb, BW), [(I, old)] + s)
                ts(R("N16", BW, o), R(pb, BW), 1025.0 + 255 * t - 63.0 / 128, A.add, 1280.0, A.min)
                if t == 0:
                    ts(new, R("N16", BW, o), -1.0, A.mult, 1280.0, A.add, cyc=0.5)
                else:
                    ts(new, R("N16", BW, o), -1025.0, A.add, cyc=0.5)
            else:
                mm(R(pb, BW), s)
                act(R("D", BW, o), R(pb, BW), 129.0 - 63.0 / 128)
                mm(R(pb, BW), [(I, old), (R("ID", 128), R("D", BW, o))])
                if t == 0:
                    act(new, R(pb, BW), R("cst", 1, 2), -1.0, AF.Relu)
                elif how == "M":
                    ts(new, R(pb, BW), 126.0, A.add, 255.0, A.min)
                else:
                    act(R("D", BW, o), R(pb, BW), R("cst", 1, 3), -1.0, AF.Relu)
                    act(new, R("D", BW, o), 255.0, -1.0)
            ops[-1]["due"] = CFG["pd"][t] + b
            if t == 1:
                dma(lambda T, o=o: T.yp[:, o:o + BW], lambda T, o=o: T["P2"][:, o:o + BW], 128, [R("P2", BW, o)], [])

    def closing(t, c):
        r = lambda b: R(b, CW * SW, L * t + CW * c)
        if t in CFG["cs"]:
            lot = R(bank(c), CW * SW, 384)
            act(r("hb"), r("TF"), 129.0 - 2047.0 / 4096, 1.0 / 2048)
            mm(lot, [(R("M2", 128), r("hb")), (R("I32", 128), r("TF"))])
            if t == 0:
                ts(R("A16", CW * SW, 4 * L + CW * c), lot, 129.0 * 2048, A.add)
            act(r("yhf"), lot, 129.0 * 2048)
        else:
            ts(r("Lr"), r("TT"), 2047, A.bitwise_and)
            if t == 0:
                copy(R("A16", CW * SW, 4 * L + CW * c), r("Lr"))
        if (c + SW) % 2 == 0:
            o = L * t + CW * (c + SW - 2)
            hb, ht, yf = R("hb", 128, o), R("ht", 128, o), R("yhf", 128, o)
            if t not in CFG["cs"]:
                ts(hb, R("TT", 128, o), 1.0 / 2048, A.mult, 129.0 - 2047.0 / 4096, A.add)
            add("v", vc(128, 0.5), lambda g, T, X: g.vector.transpose(S(T, ht), S(T, hb)), [hb], [ht])
            scan(R("hm", 128, o), ht)
            if t not in CFG["cs"]:
                copy(yf, R("Lr", 128, o))
            if t == 0:
                act(R("AC", 128, 4 * L + o), yf, con[0])
            if t == 1:
                dma(lambda T: T.yh[:, o:o + 128], lambda T: S(T, yf), 64, [yf], [])

    def parents(t):
        o = 80 * t
        vgath(R("hq", 80, o), R("hm", L, L * t), R("ql", 5))
        mms([(("pb7", 256 + h, 336, 2), [(R("WP", 128, 128 * (2 * h + k)), ("hq", o + k, o + 80, 2)) for k in range(2)]) for h in range(2)])
        tt(R("pb7", 80, 384), R("pb7", 80, 256), R("LV", 80), A.is_equal)
        tt(R("mb", 80, o), R("pb7", 80, 384), R("B", 80, o), A.mult)
        mm(R("pb7", 16, 32), [(R("ID", 128), R("mb", 16, o + 16 * l)) for l in range(5)])
        if t == 0:
            copy(R("lst", 16, 80), R("pb7", 16, 32))
        copy(R("ph", 16, 16 * t), R("pb7", 16, 32))
        if t == 0:
            copy(R("B", 16, 80 + 32), R("lst", 16, 80))

    def parents_out(t):
        o = L * t
        mms([(("pb7", 256 + s, 512, 16), [(("ID", s, 128, 16), R("ph", 16, 16 * t))]) for s in range(16)], 8)
        act(R("par", L, o), R("pb7", L, 256), p=8)
        dma(lambda T: T.yv[:, o:o + L], lambda T: T["par"][0:8, o:o + L], 8, [R("par", L, o)], [])

    def next_lots(c):
        r = lambda b, a=0: R(b, CW * SW, a + CW * c)
        n, u = 8 * CW, R(bank(c), CW * SW, 256)
        for h in range(2 * c, 2 * (c + SW)):
            x = R("X", n, n * h)
            (vgath if h in CFG["xv"] else sgath)(x, P[0], R("A16", CW // 2, 4 * L + CW // 2 * h))
            scan(R("sm", n, x[1]), x)
        mm(u, [(R("BDw", 128), ("sm", 2 * n * c + 15, 2 * n * (c + SW), 16))])
        copy(r("w1"), u)
        ts(r("w2"), r("w1"), 1023, A.bitwise_and)
        ts(u, r("w2"), 2.0, A.mult, 33.0, A.add)
        tt(r("w3"), u, r("yhf" if 0 in CFG["cs"] else "Lr"), A.mult)
        ts(r("w4"), r("w3"), 2464.0, A.add)
        ts(r("TT", L), r("w4"), 5, A.logical_shift_right, 2047, A.bitwise_and)
        copy(r("T16", L), r("TT", L))
        ops[-1]["due"] = CFG["t0"][0] + CFG["sl"][0] * (CFG["ord"][0].index(29 + c + SW) + 1) + CFG["nd"]
        if CFG["tp"]:
            copy(r("th"), r("TT", L))

    def early(t):
        for e in range(4):
            if e:
                package(4 * t + e)
            trial(t, e, None)
        for k in range(1, 1 + max([i % 4 for i in CFG["rep"] if i // 4 == t] or [0])):
            dma(lambda T, k=k: T[P[t][0]][:, k * W:k * W + W], lambda T: T[P[t][0]][:, 0:W] if t else T.price[:], 512,
                [P[t], R("A16c", 16, 16 * (4 * t + CFG["rg"][t]))], [R(P[t][0], W, k * W)])
        claims(t)

    def lanes(t):
        for e in range(4):
            for c in range(NCH):
                trial(t, e, c)
        for c in range(0, NCH, SW):
            closing(t, c)
            if t == 0:
                next_lots(c)

    as_list(1, R("bh", L))
    early(0)
    lanes(0)
    prices(0)
    if CFG["tp"]:
        mm(R("pb6", 16), [(R("Z1", 128, 15 - s), R("th", 16, 16 * s)) for s in range(16)])
        copy(R("T16c", 16, 16), R("pb6", 16))
        copy(R("TTc", 16, 16), R("pb6", 16))
    elif CFG["one"]:
        dma(lambda T: T["TTc"][:, 16:32], lambda T: T["TT"][1::16, L:2 * L], 30, [R("TT", L, L)], [R("TTc", 16, 16)])
        copy(R("T16c", 16, 16), R("TTc", 16, 16))
    else:
        dma(lambda T: T["T16c"][:, 16:32], lambda T: T["T16"][1::16, L:2 * L], 30, [R("T16", L, L)], [R("T16c", 16, 16)])
        dma(lambda T: T["TTc"][:, 16:32], lambda T: T["TT"][1::16, L:2 * L], 30, [R("TT", L, L)], [R("TTc", 16, 16)])
    claim_forms(4)
    parents(0)
    early(1)
    dma(lambda T: T.yh[:, 0:L], lambda T: T["yhf"][:, 0:L], 128, [R("yhf", L), R("C", 128, 128)], [])
    parents_out(0)
    lanes(1)
    prices(1)
    parents(1)
    parents_out(1)
    return ops


def depend(ops):
    acc, deps = {}, []
    for i, o in enumerate(ops):
        d = set()
        for wr, rs in ((False, o["rd"]), (True, o["wr"])):
            for r in rs:
                for (j, a, b, w) in acc.get(r[0], []):
                    bank = r[0][:2] == "pb" and (ops[j]["q"] != o["q"] or o["q"] == "t")
                    if j != i and (bank or ((w or wr) and a < r[2] and r[1] < b)):
                        d.add(j)
        for wr, rs in ((False, o["rd"]), (True, o["wr"])):
            for r in rs:
                lst = acc.setdefault(r[0], [])
                if wr and r[0][:2] != "pb" and len(r) == 3:
                    lst[:] = [e for e in lst if not (r[1] <= e[1] and e[2] <= r[2] and e[0] in d)]
                lst.append((i, r[1], r[2], wr))
        deps.append(sorted(d))
    return deps


def place(seq, before, dur, lag, res, at):
    start, busy = {}, {}
    for i in seq:
        t = max([at[i]] + [start[j] + dur[j] + lag(i, j) for j in before[i]])
        l = busy.setdefault(res[i], [])
        for k in range(len(l) + 1):
            if k == len(l) or t + dur[i] <= l[k][0] + 1e-9:
                break
            t = max(t, l[k][1])
        l.insert(k, (t, t + dur[i]))
        start[i] = t
    return start


def schedule(ops, deps):
    n = len(ops)
    succ = [[] for _ in range(n)]
    for i, d in enumerate(deps):
        for j in d:
            succ[j].append(i)
    dur = [o["cost"] - 2.0 * (o["kind"] == "d") for o in ops]
    res = [o["q"] for o in ops]
    lag = lambda i, j: 0.0 if res[i] == res[j] == "t" else CFG["lat"] + 2.0 * (ops[j]["kind"] == "d")
    late = [0.0] * n
    for i in range(n - 1, -1, -1):
        late[i] = min([ops[i].get("due", CFG["end"] - 2.0 * (ops[i]["kind"] == "d"))] + [late[k] - lag(k, i) for k in succ[i]]) - dur[i]
    for i in range(n):
        late[i] = ops[i].get("rank", late[i])
    for i in range(n):
        late[i] = max([late[i]] + [late[j] + 1e-6 for j in deps[i]])
    tail = [2.0 * (o["kind"] == "d") for o in ops]
    best = None
    for _ in range(CFG["it"]):
        st = place(sorted(range(n), key=lambda i: (late[i], i)), deps, dur, lag, res, [0.0] * n)
        end = max(st[i] + dur[i] + tail[i] for i in range(n))
        if best is None or end < best[0] - 0.05:
            best = (end, st)
        back = place(sorted(range(n), key=lambda i: (-st[i] - dur[i], -i)), succ, dur, lambda i, k: lag(k, i), res, tail)
        late = [ops[i].get("rank", end - back[i] - dur[i]) for i in range(n)]
        for i in range(n):
            late[i] = max([late[i]] + [late[j] + 1e-6 for j in deps[i]])
    st = best[1]
    order = sorted(range(n), key=lambda i: (st[i], i))
    calls, last = [], {}
    for i in order:
        p, c = ops[i].get("part"), last.get(res[i])
        if p and c and ops[c[-1]].get("part") == (p[0], p[1] - 1) and all(st[j] + dur[j] + lag(i, j) <= st[c[0]] + 1e-9 for j in deps[i]):
            c.append(i)
        else:
            last[res[i]] = [i]
            calls.append(last[res[i]])
    PLAN["end"] = max(st[i] + dur[i] for i in range(n))
    return calls


PLAN = {}


def plan():
    if "ops" not in PLAN:
        PLAN["ops"] = build()
        PLAN["deps"] = depend(PLAN["ops"])
        PLAN["calls"] = schedule(PLAN["ops"], PLAN["deps"])
    return PLAN["ops"], PLAN["deps"], PLAN["calls"]


def helpers(c, cores, topo):
    hs = [h for h in topo.cores_of(c) if h not in cores and all(topo.may_write(h, d) for d in cores if d != c)]
    far = [h for h in hs if topo.die(h) != topo.die(c)]
    near = [h for h in hs if topo.die(h) == topo.die(c)]
    return [h for pair in zip(far, near) for h in pair]


def relays(d, topo):
    hs = [h for h in range(WORLD) if topo.mates(h, d) and topo.may_write(h, d)]
    return [h for pair in zip([h for h in hs if topo.die(h) == topo.die(d)], [h for h in hs if topo.die(h) != topo.die(d)]) for h in pair]


def others(cores, c, topo):
    return sorted((d for d in cores if d != c), key=lambda d: (not topo.same_plane(c, d), topo.host(c) != topo.host(d)))


def bits(es):
    return sum(1 << e for e in es)


def into(c, h, cores, topo):
    if CFG["route"] == "B":
        return topo.engines(c, h)
    off = topo.engines(c, others(cores, c, topo)[0])
    return [e for e in topo.engines(c, h) if e not in off]


def dst_id(d, src, topo):
    return DstId(rid=topo.addr(d, src)[0], pnc=topo.addr(d, src)[1])


def hand_on(g, core, T, topo):
    cores = list(T.cores)
    for c in cores:
        rest = others(cores, c, topo)
        hs, rs = helpers(c, cores, topo), relays(rest[2], topo) if CFG["route"] == "C" else []
        if core not in hs + rs:
            continue
        b = (hs + rs).index(core) % NB
        to = rest[2:] if core in rs else {"A": rest[1:], "B": rest, "C": rest[:2]}[CFG["route"]]
        es = topo.engines(core, to[0])
        for t in range(2):
            g.wait_ge(T.sem["hin%d" % t], len(topo.engines(c, core) if core in rs else into(c, core, cores, topo)))
            at = [others(cores, d, topo).index(c) * W + BW * b for d in to]
            g.remote_dma_fused([RemoteDMATransfer(dst_ids=[dst_id(d, core, topo) for d in to], dma_engine_mask=bits(es), remote_sem=T.sem["far%d_%d" % (t, b)],
                                                  srcs=[T["HB"][:, t * BW:t * BW + BW]], dsts=[T["LO%d" % t][:, o:o + BW] for o in at])],
                               local_sem=T.sem["hs"])
        g.wait_ge(T.sem["hs"], 2 * len(es))


def rank_program(g, core, T, topo):
    if T.rank_of(core) is None:
        hand_on(g, core, T, topo)
        return
    cores = list(T.cores)
    hs, rest = helpers(core, cores, topo), others(cores, core, topo)
    ops, deps, calls = plan()
    eng = {"v": g.vector, "s": g.scalar, "t": g.tensor, "y": g.sync, "g": g}
    sent = [0]

    def send(g_, T_, t, b):
        src, es = T["O%d" % t][:, BW * b:BW * b + BW], into(core, hs[b], cores, topo)
        tr = [RemoteDMATransfer(dst_ids=[dst_id(hs[b], core, topo)], dma_engine_mask=bits(es), remote_sem=T.sem["hin%d" % t],
                                srcs=[src], dsts=[T["HB"][:, t * BW:t * BW + BW]])]
        sent[0] += len(es)
        if CFG["route"] == "A":
            e0 = topo.engines(core, rest[0])
            tr.append(RemoteDMATransfer(dst_ids=[dst_id(rest[0], core, topo)], dma_engine_mask=bits(e0), remote_sem=T.sem["arr%d_%d" % (t, b)],
                                        srcs=[src], dsts=[T["LO%d" % t][:, BW * b:BW * b + BW]]))
            sent[0] += len(e0)
        if CFG["route"] == "C":
            r = relays(rest[2], topo)[b]
            e0 = topo.engines(core, r)
            tr.append(RemoteDMATransfer(dst_ids=[dst_id(r, core, topo)], dma_engine_mask=bits(e0), remote_sem=T.sem["hin%d" % t],
                                        srcs=[src], dsts=[T["HB"][:, t * BW:t * BW + BW]]))
            sent[0] += len(e0)
        g.remote_dma_fused(tr, local_sem=T.sem["snd"])

    arrive = {"a": len(topo.engines(rest[0], core)),
              "f": sum(len(topo.engines(helpers(c, cores, topo)[0], core)) for c in rest[CFG["route"] == "A":])}
    X = {"send": send}
    cnt = {"v": 0, "s": 0, "t": 0, "g": 0}
    clock = {q: {} for q in eng}
    done = {}
    pos = {i: k for k, c in enumerate(calls) for i in c}
    nd = 0
    for c in calls:
        o = ops[c[0]]
        if o["kind"] == "x":
            n = arrive[o["fn"][0]]
            done[c[0]] = (o["fn"], n, {o["fn"]: n})
            continue
        q = o["q"]
        ck = clock[q]
        for j in sorted({j for i in c for j in deps[i]}, key=lambda j: -pos[j]):
            if j in done and not q == ops[j]["q"] == "t":
                s, n, c2 = done[j]
                if ck.get(s, 0) < n:
                    eng[q].wait_ge(T.sem[s], n)
                    for k, v in c2.items():
                        ck[k] = max(ck.get(k, 0), v)
        ins = o["fn"](g, T, o["part"][1], o["part"][1] + len(c)) if "part" in o else o["fn"](g, T, X)
        if o["kind"] == "c":
            cnt[q] += 1
            s, n = "q" + q, cnt[q]
            ins.then_inc(T.sem[s], 1)
        elif o["kind"] == "d":
            s, n = "d%d" % nd, 16
            nd += 1
            ins.then_inc(T.sem[s], 16)
        else:
            continue
        c2 = dict(ck)
        c2[s] = n
        for i in c:
            done[i] = (s, n, c2)
    for q, n in cnt.items():
        g.wait_ge(T.sem["q" + q], n)
    for k in range(nd):
        g.wait_ge(T.sem["d%d" % k], 16)
    g.wait_ge(T.sem["snd"], sent[0])
